import numpy as np, ml_dtypes
CORES = [9,25,41,57]
N = 4
BF = ml_dtypes.bfloat16
V, K, LA, LF, Q, RO, AS, FS = 4096, 1024, 256, 256, 4, 4, 170, 341
def lanes(flag, start, cap):
    order = (np.arange(K) + start) % K; fl = flag[:, order]
    o = np.argsort(~fl, axis=1, kind="stable")[:, :cap]
    return order[o], np.take_along_axis(fl, o, 1)
def judge(X, C, ids, T):
    n = ids.shape[1]; lit = np.take_along_axis(C, ids[:, None, :], 2); v = np.where(lit >= V, lit - V, lit)
    s = np.take_along_axis(X, v.reshape(8, 1, 16 * n), 2).reshape(8, 16, 16, n)
    s = np.where((lit >= V)[:, None], 63 - s, s)
    return lit, v, s, np.max(s, axis=2) < T
def states(rng, pa, pd):
    a = rng.choice(np.array(pa), (N, 8, 1)); b = rng.choice(np.array(pd), (N, 8, 1)); u = rng.random((N, 8, K))
    return np.where(u < a, 0, np.where(u >= 1 - b, 4, rng.integers(1, 4, (N, 8, K))))
def parts(rng):
    u = rng.random((N, 8, 16, K)); v = np.minimum((V * u * np.sqrt(u)).astype(np.int64), V - 1)
    T = rng.integers(58, 60, (N, 8, 1, 1)) + rng.integers(0, 2, (N, 8, 16, 1))
    return rng.integers(0, 64, (N, 8, 16, V)), v + V * rng.integers(0, 2, v.shape), states(rng, [0.3, 0.4, 0.5], [0.01, 0.05, 0.2]), T
def at(a, v):
    return np.take_along_axis(a, v.reshape(N, 8, -1), 2).reshape(v.shape)
def first(X, C, F, T):
    ia, ok = lanes(F == 0, 0, LA)
    return ia, ok & (np.sum(judge(X, C, ia, T)[3], axis=1) > Q)
def laid(rng, own, place, rest):
    X = np.zeros((8, 16, V), np.int64); C = np.zeros((8, 16, K), np.int64)
    for g in range(8):
        o = rng.permutation(V); sign = rng.integers(0, 2, V)
        s = rng.integers(0, rest[g] + 1, (16, V)); s[:, o[:K]] = own[g]
        X[g] = np.where(sign == 1, 63 - s, s)
        v = o[rng.integers(K, V, (16, K))]; v[place[g], np.arange(K)] = o[:K]
        C[g] = v + V * sign[v]
    return X, C
def full(rng):
    T = rng.integers(50, 61, (8, 16, 1)); own = rng.integers(10, 18, (8, 16, K)); place = rng.integers(0, 16, (8, K)); F = np.zeros((8, K), np.int64)
    own[[2, 7]] = 0; place[[2, 7]] = 0
    for g in range(8):
        o = rng.permutation(K); n = int(rng.integers(16, LF + 1))
        F[g, o[:n]] = rng.integers(1, 4, n); F[g, o[:16]] = 1
        own[g][:, o[:16]] = T[g] + rng.integers(0, 3, (16, 16))
    X, C = laid(rng, own, place, [9, 9, 0, 9, 9, 9, 9, 0])
    return X, C, F, T
def calm(rng):
    T = rng.integers(20, 51, (8, 16, 1)); own = np.repeat(T, K, axis=2); place = rng.integers(0, 16, (8, K)); F = rng.integers(1, 3, (8, K)); e = int(rng.integers(1, 4))
    for g in range(8):
        o = rng.permutation(K); n = 4 * int(rng.integers(2, LA >> 4)) + (e if g == 0 else 0); m = n + int(rng.integers(0, LA - n + 1)); h = m + ((K - m) >> 1)
        F[g, o[:m]] = 0
        own[g][:, o[n:h]] = 63; own[g][:, o[:n]] = T[g] - rng.integers(1, 6, (16, n))
    X, C = laid(rng, own, place, [9] * 8)
    return X, C, F, T
def pack(X, C, F, T):
    return {"xv": np.ascontiguousarray(X).reshape(N, 128, V).astype(np.float32).astype(BF), "cl": np.ascontiguousarray(C).reshape(N, 128, K).astype(np.int32),
            "fr": np.ascontiguousarray(F).astype(np.int32), "th": np.ascontiguousarray(T).reshape(N, 128, 1).astype(np.int32)}
def setup_inputs(rng):
    X, C, F, T = parts(rng)
    return pack(X, C, F, T)
def setup_inputs_spread(rng):
    low = np.minimum(np.exp2(6 * rng.random((N, 8, 1, V))) * rng.random((N, 8, 16, V)), 63).astype(np.int64)
    flip = rng.random((N, 8, V)) < 0.5; X = np.where(flip[:, :, None], 63 - low, low)
    u = rng.random((N, 8, 16, K)); v = np.minimum((V * u * u).astype(np.int64), V - 1)
    up = rng.random(v.shape) < rng.choice(np.array([0.0, 0.02, 0.06, 0.12]), (N, 8, 1, K))
    T = np.clip(61 - np.exp2(5.907 * rng.random((N, 8, 16, 1))).astype(np.int64), 1, 60)
    return pack(X, v + V * (at(flip, v) ^ up).astype(np.int64), states(rng, [0.1, 0.3, 0.6, 0.9], [0.0, 0.02, 0.3]), T)
def setup_inputs_ends(rng):
    X = 63 * rng.integers(0, 2, (N, 8, 16, V)); k = np.arange(16)[:, None]
    T = np.where(rng.random((N, 8, 16, 1)) < 0.75, 60, 1); T[:, [3, 7]] = 60; T[:, 0, 0] = 1
    u = rng.random((N, 8, K)); F = np.where(u < 0.45, 0, np.where(u < 0.75, 4, rng.choice(np.array([1, 3]), (N, 8, K))))
    m = rng.choice(np.array([16, 16, Q + 1, Q]), (N, 8, 1)); m[:, 1] = Q + 1; m[:, 2] = Q; m[:, [3, 7]] = 16
    low = np.argsort(np.argsort(rng.random((N, 8, 16)), axis=2), axis=2) < m
    X[..., 0] = np.where(low, 0, 63); X[..., V - 1] = np.where(low, 63, 0); X[..., 65] = 63
    sp = np.concatenate([np.arange(1, 65), np.arange(V - 65, V - 1)]); j = np.arange(128); cls = (j >> 1) % 3
    s = np.where(cls == 0, 59, np.where((cls == 2) & (k > Q), 63, 62)) - ((j // 6) % 2) * (k == j % 16)
    X[..., sp] = np.where(j % 2 == 1, 63 - s, s); lit = sp + V * (j % 2)
    C = np.where(rng.random((N, 8, 16, K)) < rng.choice(np.array([0.0, 0.5, 0.5, 1.0]), (N, 8, 1, K)), 0, 2 * V - 1)
    kind = rng.choice(np.array([0, 0, 0, 0, 0, 0, 0, 1, 2, 3]), (N, 8, K)); frm = rng.integers(0, 16, (N, 8, K))
    for q in range(N):
        F[q, 7] = 4; kind[q, 7] = rng.choice(np.array([0, 0, 1]), K)
        b = np.append(np.sort(AS + rng.permutation(K - 1 - AS)[:LA - 1]), K - 1)
        F[q, 7, rng.permutation(AS)[:32]] = 0; F[q, 7, b] = 0
        kind[q, 7, b[-32:]] = 2; kind[q, 7, b[-2:]] = 3; frm[q, 7, b[-2:]] = 0
    for c in range(3):
        a = lit[cls == c]; fill = a[rng.integers(0, len(a), C.shape)]
        C = np.where((kind == c + 1)[:, :, None] & (k >= frm[:, :, None]), fill, C)
    for q in range(N):
        ia, bad = first(X[q], C[q], F[q], T[q]); b = np.flatnonzero(bad[3])[:(int(np.sum(bad)) - 3) % 4]
        C[q, 3, 8, ia[3, b]] = 65
    return pack(X, C, F, T)
def setup_inputs_corners(rng):
    X, C, F, T = parts(rng); w = rng.random((N, 8, 1, K)); e = np.array([0, V - 1, V, 2 * V - 1])
    C = np.where(w < 0.15, rng.choice(e, (N, 8, 1, K)), np.where(w < 0.3, np.arange(K) + V * rng.integers(0, 2, (N, 8, 1, K)), np.where(w < 0.45, rng.choice(e, (N, 8, 16, K)), C)))
    T[:, 1] = np.where(rng.random((N, 16, 1)) < 0.3, 1, 60); T[:, 5] = 1; T[:, 6] = 60
    cases = ((0, K), (K, 0), (LA, LF), (LA + 1, LF + 1), (LA - 1, LF - 1), (1, 0), (2, K - 2), (0, 0))
    for q in range(N):
        for g in range(8):
            na, nz = cases[(g + q) % 8]; o = rng.permutation(K)
            F[q, g] = 4; F[q, g, o[:na]] = 0; F[q, g, o[na:na + nz]] = rng.integers(1, 4, nz)
    for q in range(0, N - 1, 2):
        bad = first(X[q], C[q], F[q], T[q])[1]; n = np.sum(bad[:, 0::2] & bad[:, 1::2], axis=1); c = 0
        for g in range(8):
            if n[g] < 2: continue
            d = int(n[g]) + (0, 1, -1)[c % 3]; c += 1
            z = rng.integers(0, 4, K); z[rng.permutation(K)[:d]] = 4; F[q + 1, g] = z
    return pack(X, C, F, T)
def setup_inputs_ties(rng):
    b = rng.choice(np.array([9, 30, 60]), (N, 8, 1, 1)); T = np.zeros((N, 8, 16, 1), np.int64) + b; i = np.arange(16)[:, None]
    mul = 2 * rng.integers(0, 8, (N, 8, 1, V)) + 1; sh = rng.integers(0, 16, (N, 8, 1, V)); n = Q + rng.integers(0, 2, (N, 8, 1, V))
    odd = np.arange(V) % 2 == 1
    s = np.where(odd & ((i * mul + sh) % 16 >= n), b + rng.integers(0, 4, (N, 8, 1, V)), b - 1 - rng.integers(0, 2, (N, 8, 1, V)))
    flip = rng.random((N, 8, V)) < 0.5; X = np.where(flip[:, :, None], 63 - s, s)
    lim = rng.choice(np.array([V // 2, V // 2, V // 16]), (N, 8, 1, 1))
    v = 2 * np.minimum((rng.random((N, 8, 16, K)) * lim).astype(np.int64), lim - 1)
    one = (i == rng.integers(0, 16, (N, 8, 1, K))) & (rng.random((N, 8, 1, K)) < 0.9)
    v = np.where(one, 2 * rng.integers(0, V // 2, v.shape) + 1, v)
    return pack(X, v + V * at(flip, v).astype(np.int64), states(rng, [0.3, 0.4, 0.5], [0.02, 0.1, 0.2]), T)
def setup_inputs_alike(rng):
    X, C, F, T = parts(rng); few = rng.integers(0, V, (N, 8, 24)); few[:, :, 0] = 0; few[:, :, 1] = V - 1
    v = np.take_along_axis(few, rng.integers(0, 24, (N, 8, 16 * K)), 2).reshape(N, 8, 16, K) + V * rng.integers(0, 2, (N, 8, 16, K))
    C[:, ::2] = v[:, ::2]
    for q in range(N): C[q, 5] = C[q, 5][:, rng.integers(0, 8, K)]
    o = rng.permutation(N)
    X[o[0]], C[o[0]], F[o[0]], T[o[0]] = full(rng)
    X[o[1]], C[o[1]], F[o[1]], T[o[1]] = calm(rng)
    return pack(X, C, F, T)
def check_inputs(d):
    bad = []
    for k, lo, hi in (("xv", 0, 63), ("cl", 0, 2 * V - 1), ("fr", 0, 4), ("th", 1, 60)):
        a = np.asarray(d[k]).astype(np.float64)
        if not np.all((a >= lo) & (a <= hi)): bad.append("range of " + k)
        elif not np.all(a == np.floor(a)): bad.append("whole numbers of " + k)
    return bad
def reference(xv, cl, fr, th):
    X = xv.astype(np.float32).astype(np.int64).reshape(N, 8, 16, V); C = cl.astype(np.int64).reshape(N, 8, 16, K); F = fr.astype(np.int64).reshape(N, 8, K)
    TH = th.astype(np.int64).reshape(N, 8, 16, 1); A = np.zeros(N, np.int64)
    for t in range(RO):
        nX = np.array(X); nC = np.array(C); nF = np.array(F); sent = []
        for r in range(N):
            T = TH[r] + (A[r] & 3)
            ia, oka = lanes(F[r] == 0, AS * t % K, LA); iz, okz = lanes((F[r] >= 1) & (F[r] <= 3), FS * t % K, LF)
            lit, v, s, fail = judge(X[r], C[r], ia, T); bad = oka & (np.sum(fail, axis=1) > Q); A[r] = np.sum(bad)
            m = oka & ~bad; nF[r][np.nonzero(m)[0], ia[m]] = 1
            wake = np.sum(judge(X[r], C[r], iz, T)[3], axis=1) > Q
            old = np.take_along_axis(F[r], iz, 1); nF[r][np.nonzero(okz)[0], iz[okz]] = np.where(wake, 0, old + 1)[okz]
            kk = np.argmax(np.sum(s * fail[:, :, None, :], axis=1), axis=1)[:, None, :]
            pick = np.take_along_axis(lit, kk, 1); pv = np.take_along_axis(v, kk, 1)[:, 0]
            up = np.minimum(np.take_along_axis(s, kk[:, None], 2)[:, :, 0] + 8, 63); new = np.where(pick >= V, 63 - up, up)
            for g in range(8):
                b = np.flatnonzero(bad[g]); u, ix = np.unique(pv[g, b], return_index=True); w = b[ix]
                nX[r, g][:, u] = np.where(fail[g][:, w], new[g][:, w], X[r, g][:, u])
            tot = np.sum(s, axis=1)
            sent.append((bad[:, 0::2] & bad[:, 1::2], np.where(tot[:, :, 1::2] > tot[:, :, 0::2], lit[:, :, 1::2], lit[:, :, 0::2])))
        for r in range(N):
            a = (r + 1 + t % 3) % N; both, joint = sent[r]
            for g in range(8):
                come = joint[g][:, both[g]]; dead = np.flatnonzero(F[a, g] == 4); n = min(come.shape[1], len(dead))
                nC[a, g][:, dead[:n]] = come[:, :n]; nF[a, g][dead[:n]] = 0
        X = nX; C = nC; F = nF
    return {"yx": X.reshape(N, 128, V).astype(np.float32).astype(BF), "yc": C.reshape(N, 128, K).astype(np.float32), "yf": F.astype(np.float32)}

@@ -1,0 +1,617 @@
+from concourse.mybir import AluOpType as OP, AxisListType, ActivationFunctionType as AF
+
+F4, B2, I4, U2 = "float32", "bfloat16", "int32", "uint16"
+SB = {
+    "xt": ([128, 8720], B2), "ci": ([128, 1024], I4), "cb": ([128, 1024], F4), "w": ([128, 3072], F4), "rw": ([128, 3072], B2),
+    "thi": ([128, 1], I4), "thf": ([128, 1], F4), "thr": ([128, 1], F4), "fr0": ([64, 128], I4), "frb": ([64, 128], B2),
+    "fn": ([128, 64], B2), "y": ([128, 64], B2), "fl": ([128, 198], B2), "sc": ([128, 198], F4), "zz": ([128, 198], F4),
+    "pf": ([128, 64], F4), "pos": ([128, 64], U2), "fo": ([64, 128], F4),
+    "lua": ([128, 256], U2), "luz": ([128, 256], U2), "sa": ([128, 4096], B2), "sz": ([128, 4096], B2), "mx": ([128, 4096], B2), "mz": ([128, 4096], B2),
+    "fa": ([128, 256], B2), "fz": ([128, 256], B2), "sm": ([128, 4096], B2), "vi": ([128, 256], B2),
+    "li": ([128, 256], I4), "hi": ([128, 256], I4), "lo": ([128, 256], I4), "ab": ([128, 512], F4), "at": ([128, 512], F4), "scn": ([128, 512], F4),
+    "di": ([128, 32], I4), "fti": ([128, 32, 8], I4), "ftb": ([128, 32, 8], B2), "fe": ([128, 16, 16], B2), "bd": ([128, 16, 128], B2),
+    "ddi": ([128, 48], I4), "db": ([128, 48], B2), "cu": ([128, 16], U2), "cc": ([128, 32], F4), "ge": ([128, 16], F4), "cm": ([128, 16], F4),
+    "tg": ([128, 16], F4), "tg0": ([128, 16], F4), "win": ([128, 16], F4), "wm": ([128, 32], F4), "of1": ([128, 32], F4), "of2": ([128, 32], F4), "off": ([128, 32], U2),
+    "sch": ([128, 256], B2), "nv": ([128, 512], B2), "junk": ([128, 2560], B2), "dra": ([128, 64], F4), "drb": ([128, 64], F4), "dr": ([128, 64], F4), "nt": ([128, 64], F4), "ns": ([128, 1], F4), "vs": ([128, 1], F4), "ai": ([128, 2], I4),
+    "dj": ([128, 128], F4), "jt": ([128, 128], F4), "ce": ([128, 128], B2), "o32": ([128, 128], B2),
+    "jo": ([128, 8], U2), "jw": ([128, 1024], F4), "jl": ([128, 512], F4), "rg": ([128, 1024], B2),
+    "im": ([128, 128], F4), "img": ([128, 128], F4), "g8": ([128, 8], F4), "ki": ([128, 8], I4), "kf": ([128, 8], F4), "kx": ([128, 32], F4),
+    "gi": ([128, 8], B2), "gif": ([128, 8], F4), "mb": ([128, 8], F4), "cbm": ([128, 8], F4), "bb": ([128, 128], B2), "bb9": ([128, 128], B2), "gt": ([128, 128], B2), "lt": ([128, 128], B2),
+    "id": ([128, 128], B2), "idm": ([128, 128], B2), "id8": ([128, 128], B2), "dg": ([128, 128], B2), "sel": ([128, 2048], B2), "nsel": ([128, 2048], B2), "qm": ([128, 1024], B2),
+    "lw0": ([128, 16], F4), "lw": ([128, 16], F4), "tg1": ([128, 16], F4), "bias": ([128, 16], F4), "tr": ([128, 32], F4), "l70": ([128, 16], F4),
+    "nc": ([128, 128], B2), "jc0": ([128, 8], F4), "jc1": ([128, 8], F4), "jc8": ([128, 8], B2), "mk": ([128, 4096], B2), "mk3": ([128, 198], B2), "one": ([128, 256], B2), "onf": ([128, 128], F4),
+}
+SCRATCH = {"q_" + k: ("sbuf", v[0], v[1]) for k, v in SB.items()}
+SCRATCH.update({"q_p%d" % i: ("psum", [128, 512], F4) for i in range(8)})
+NDMA = 40
+SEMAPHORES = ["ev", "es", "et", "eg"] + ["a%d" % t for t in range(4)] + ["l%d" % t for t in range(4)] + ["d%d" % i for i in range(NDMA)]
+XW0, XE = 512, 8720
+ZB, DB0, WW = 1024, 2048, 3072
+LS, LB = 96, 144
+BDS = (2, 3, 4, 5, 6, 7)
+DED = (("s", 0, (15, 14)), ("s", 7, (13, 12)), ("s", 3, (11, 10)), ("s", 2, (9, 8, 7)), ("v", 4, (6, 5, 4, 3, 2, 1, 0)))
+SCOLS = tuple(a for e, b, aa in DED if e == "s" for a in aa)
+
+
+CY, CPE, WAKE, FIX, SLACK, GAMMA, SIGMA = 0.00105, 0.0009, 0.11, 0.01, 0.05, 1.7, 3.5
+SEEDS = (313303, 302857, 208832, 398229, 87847, 179512, 39628, 96281, 664645, 136495)
+
+
+def rank_program(g, core, T, topo):
+    rank = T.rank_of(core)
+    if rank is None:
+        return
+    Q = {"v": g.vector, "s": g.scalar, "t": g.tensor, "g": g, "y": g.sync}
+    cnt = {q: 0 for q in Q}
+    know = {q: {} for q in Q}
+    snap, log, nd = {}, {}, [0]
+
+    def r(n, lo=None, hi=None, step=1, P=128):
+        t = T["q_" + n]
+        hi = t.shape[1] if hi is None else hi
+        lo = 0 if lo is None else lo
+        return (n, t[0:P, lo:hi:step] if step != 1 else t[0:P, lo:hi], lo, hi, step)
+
+    def r3(n, a, b=slice(None), lo=0, hi=1 << 20, st=1):
+        t = T["q_" + n]
+        return (n, t[:, a, b], lo, hi, st)
+
+    def ind(w, o):
+        return ("@", w, o)
+
+    def over(a, b):
+        if a[0] >= b[1] or b[0] >= a[1]:
+            return False
+        return not (a[2] == b[2] and a[2] > 1 and (a[0] - b[0]) % a[2])
+
+    def need(q, src, n):
+        k = know[q]
+        if k.get(src, 0) >= n:
+            return
+        Q[q].wait_ge(T.sem[src], n)
+        k[src] = n
+        for s2, n2 in snap.get((src, n), {}).items():
+            if k.get(s2, 0) < n2:
+                k[s2] = n2
+
+    def deps(q, acc):
+        req = {}
+        own = "e" + q
+        for (b, lo, hi, st, w) in acc:
+            bank = b[0] == "p" and len(b) == 2
+            for (src, l2, h2, s2, w2), n in log.get(b, {}).items():
+                if src == own:
+                    if not (w or w2) or (w and q == "t") or not over((lo, hi, st), (l2, h2, s2)):
+                        continue
+                elif not bank and (not (w or w2) or not over((lo, hi, st), (l2, h2, s2))):
+                    continue
+                if req.get(src, 0) < n:
+                    req[src] = n
+        for src in sorted(req, key=lambda x: (x[0] != "e", x)):
+            need(q, src, req[src])
+
+    def note(src, n, acc):
+        for (b, lo, hi, st, w) in acc:
+            log.setdefault(b, {})[(src, lo, hi, st, w)] = n
+
+    def flat(args, kw):
+        acc, real, kk = [], [], {}
+        for i, a in enumerate(args):
+            if isinstance(a, tuple) and a[0] == "@":
+                acc.append((a[1][0],) + a[1][2:] + (i == 0,))
+                acc.append((a[2][0],) + a[2][2:] + (False,))
+                real.append(a[1][1].indirect(a[2][1]))
+            elif isinstance(a, tuple):
+                acc.append((a[0],) + a[2:] + (i == 0,))
+                real.append(a[1])
+            else:
+                real.append(a)
+        for k, a in kw.items():
+            if isinstance(a, tuple):
+                acc.append((a[0],) + a[2:] + (k == "accum_out",))
+                kk[k] = a[1]
+            else:
+                kk[k] = a
+        return acc, real, kk
+
+    ops, marks = [], []
+
+    def cols(a):
+        if a[0] == "@":
+            return 16 * cols(a[2])
+        return min(-(-(a[3] - a[2]) // a[4]), 256 if a[3] >= 1 << 20 else 1 << 20)
+
+    def cost(q, name, args):
+        xs = [a for a in args if isinstance(a, tuple)]
+        n = max(cols(a) for a in xs[1:]) if len(xs) > 1 else cols(xs[0])
+        names = [a[1][0] if a[0] == "@" else a[0] for a in xs]
+        two = all(b in SB and SB[b][1] in (B2, U2) for b in names)
+        if name == "mm":
+            return max(64, cols(args[2])) * (4 if SB[args[2][0]][1] == F4 else 1) * CPE
+        if name == "iota":
+            return 0.13 + 2 * cols(args[0]) * CY
+        if args[0][0] == "@":
+            n *= SIGMA
+        elif any(a[0] == "@" for a in xs):
+            n *= GAMMA
+        elif name == "tt":
+            n *= 1 if any(len(b) == 2 and b[0] == "p" for b in names) else 2
+        elif name in ("copy", "ts", "scan", "vt", "set") and two:
+            n *= 0.5
+        return max(n, 64) * CY + FIX
+
+    def do(q, name, *args, **kw):
+        acc, real, kk = flat(args, kw)
+        e = Q[q]
+        f = {"copy": lambda: e.tensor_copy(*real), "tt": lambda: e.tensor_tensor(*real), "ts": lambda: e.tensor_scalar(*real),
+             "set": lambda: e.memset(*real), "red": lambda: e.tensor_reduce(*real), "scan": lambda: e.tensor_tensor_scan(*real),
+             "vt": lambda: e.transpose(*real), "act": lambda: e.activation(*real, **kk), "mm": lambda: e.matmul(*real),
+             "iota": lambda: e.iota(*real, **kk)}[name]
+
+        def issue():
+            deps(q, acc)
+            cnt[q] += 1
+            src = "e" + q
+            f().then_inc(T.sem[src], 1)
+            snap[(src, cnt[q])] = dict(know[q])
+            note(src, cnt[q], acc)
+        c = cost(q, name, args)
+        ops.append((q, acc, c, c, issue))
+
+    def dma(q, out, in_):
+        acc, ap = [], []
+        for i, a in enumerate((out, in_)):
+            ap.append(a[1] if isinstance(a, tuple) else a)
+            if isinstance(a, tuple):
+                acc.append((a[0],) + a[2:] + (i == 0,))
+
+        def issue():
+            deps(q, acc)
+            x = "d%d" % nd[0]
+            nd[0] += 1
+            Q[q].dma_start(ap[0], ap[1]).then_inc(T.sem[x], 16)
+            snap[(x, 16)] = dict(know[q])
+            note(x, 16, acc)
+        ops.append((q, acc, 0.08, 2.5 + (acc[0][2] - acc[0][1]) / 1000, issue))
+
+    def order():
+        n = len(ops)
+        pre = [{} for _ in range(n)]
+        hist, gl = {}, []
+        for i in range(n):
+            q, acc = ops[i][0], ops[i][1]
+            if q == "g":
+                if gl:
+                    pre[i][gl[-1]] = 0.0
+                gl.append(i)
+            for (b, lo, hi, st, w) in acc:
+                bank = b[0] == "p" and len(b) == 2
+                hs = hist.setdefault(b, ([], []))
+                for h in (hs[0], hs[1]) if (w or bank) else (hs[0],):
+                    for (j, q2, l2, h2, s2, w2) in h:
+                        if bank and q == "t" and q2 == "t":
+                            pre[i].setdefault(j, 0.0)
+                        elif (bank and q != q2) or ((w or w2) and over((lo, hi, st), (l2, h2, s2))):
+                            pre[i][j] = WAKE
+            for (b, lo, hi, st, w) in acc:
+                hist[b][0 if w else 1].append((i, q, lo, hi, st, w))
+        post = [[] for _ in range(n)]
+        for i in range(n):
+            pre[i].pop(i, None)
+            for j in pre[i]:
+                post[j].append(i)
+        way = [0.0] * n
+        for i in range(n - 1, -1, -1):
+            way[i] = ops[i][3] + max([way[j] + pre[j][i] for j in post[i]], default=0.0)
+        per = marks[2] - marks[1]
+        for seed in SEEDS:
+            for m in marks:
+                i = m + seed % per if m else marks[1] - per + seed % per
+                if i < n:
+                    way[i] += (seed // per % 64 - 31.5) * 0.15
+        left = [len(p) for p in pre]
+        ready = {q: {} for q in Q}
+        free = {q: 0.0 for q in Q}
+        end = [0.0] * n
+        for i in range(n):
+            if not left[i]:
+                ready[ops[i][0]][i] = 0.0
+        done = []
+        while len(done) < n:
+            best = None
+            for q in Q:
+                if ready[q]:
+                    t0 = min(max(free[q], x) for x in ready[q].values())
+                    i = max((i for i, x in ready[q].items() if max(free[q], x) <= t0 + SLACK), key=lambda k: way[k])
+                    s0 = max(free[q], ready[q][i])
+                    if best is None or s0 < best[0]:
+                        best = (s0, q, i)
+            s0, q, i = best
+            del ready[q][i]
+            free[q] = s0 + ops[i][2]
+            end[i] = s0 + ops[i][3]
+            done.append(i)
+            for j in post[i]:
+                left[j] -= 1
+                if not left[j]:
+                    ready[ops[j][0]][j] = max(end[k] + w for k, w in pre[j].items())
+        for i in done:
+            ops[i][4]()
+
+    def v(*a): do("v", *a)
+    def pe(*a): do("t", "mm", *a)
+    def act(out, in_, f=AF.Copy, **k): do("s", "act", out, in_, f, **k)
+
+    def ts(out, in0, s1, op0, s2=None, op1=None):
+        if op1 is None:
+            v("ts", out, in0, s1, None, op0)
+        else:
+            v("ts", out, in0, s1, s2, op0, op1)
+
+    def iota(out, pat, base, ch):
+        if out[0] == "ki":
+            do("g", "iota", out, pat, base, ch)
+        else:
+            do("g", "iota", out, pat, base, ch, allow_small_or_imprecise_dtypes=True)
+
+    for gr in range(8):
+        dma("y" if gr % 2 == 0 else "s", r("fr0", 16 * gr, 16 * gr + 16, P=64), T.fr[gr:gr + 1, :])
+    dma("s", r("ci"), T.cl[:, :])
+    for i in range(2):
+        dma("y", r("xt", XW0 + 2048 * i, XW0 + 2048 * i + 2048), T.xv[:, 2048 * i:2048 * i + 2048])
+    dma("s", r("thi"), T.th[:, :])
+
+    iota(r("ki", 0, 1), [[1, 1]], 0, 1)
+    iota(r("im"), [[1, 128]], 0, 0)
+    iota(r("img"), [[1, 8], [0, 16]], 0, 0)
+    iota(r("g8"), [[1, 8]], 0, 0)
+    iota(r("lw0"), [[16, 16]], 0, 0)
+    iota(r("w"), [[0, WW]], 8192, 0)
+    iota(r("l70"), [[-32, 8], [0, 2]], 0, 0)
+    iota(r("jc0"), [[16, 8]], 0, 0)
+    iota(r("nc"), [[1, 128]], -255, 0)
+    iota(r("rw"), [[0, WW]], 1, 0)
+    iota(r("jw"), [[0, 1024]], -20, 0)
+    kx = lambda i: r("kx", i, i + 1)
+    v("set", r("fl"), 0.0)
+    v("set", r("fl", 66, 67), 64.0)
+    v("set", r("fl", 132, 133), 128.0)
+    v("set", r("mk3"), 1.0)
+    v("set", r("mk3", 0, 198, 66), 0.0)
+    v("set", kx(7), -32.0)
+    v("set", kx(20), -36.0)
+    v("set", kx(21), 63.0)
+    v("set", kx(22), 0.5)
+    v("set", r("mk"), 1.0)
+    v("set", r("mk", 0, 4096, 16), 0.0)
+    ts(r("ki", 1, 2), r("ki", 0, 1), 15, OP.bitwise_and)
+    ts(r("ki", 2, 3), r("ki", 0, 1), 4, OP.arith_shift_right)
+    ts(r("ki", 3, 4), r("ki", 0, 1), 31, OP.bitwise_and)
+    ts(r("ki", 4, 5), r("ki", 0, 1), 4, OP.arith_shift_right, 1, OP.bitwise_and)
+    v("copy", r("kf", 0, 5), r("ki", 0, 5))
+    pc, qc, gc, p31, hb = [r("kf", i, i + 1) for i in range(5)]
+    ts(r("id"), r("im"), pc, OP.is_equal)
+    ts(r("bb"), r("img"), gc, OP.is_equal)
+    ts(r("gt"), r("im"), pc, OP.is_gt)
+    v("tt", r("lt"), r("gt"), r("bb"), OP.mult)
+
+    def new_states(t, xw):
+        if t == 0:
+            ts(r("fn"), xw, 0.0, OP.max)
+        else:
+            ts(r("p6", 64, 128), xw, 16.0, OP.add, 0.0, OP.max)
+            v("tt", r("fn"), r("p6", 64, 128), r("nt"), OP.mult)
+
+    def rank_stage(t, xw, then=lambda: None):
+        new_states(t, xw)
+        act(r("y"), r("fn"), AF.Square, bias=kx(7))
+        then()
+
+        def flags(seg, src, thr, st, ki):
+            c0 = st // 16
+            if st == 0:
+                ts(r("fl", seg + 1, seg + 65), r(src), thr, OP.is_lt)
+                return
+            if c0 < 63:
+                ts(r("fl", seg + 2, seg + 65 - c0), r(src, c0 + 1, 64), thr, OP.is_lt)
+            ts(r("fl", seg + 65 - c0, seg + 65), r(src, 0, c0), thr, OP.is_lt)
+            ts(r("fl", seg + 1, seg + 2), r(src, c0, c0 + 1), thr, OP.is_lt, kx(ki), OP.mult)
+            ts(r("fl", seg + 65, seg + 66), r(src, c0, c0 + 1), thr, OP.is_lt, kx(ki + 1), OP.mult)
+        a0, z0 = (170 * t) % 1024, (341 * t) % 1024
+        flags(0, "fn", 8.0, a0, 8 + (t - 1) * 4)
+        ts(r("fl", 133, 197), r("fn"), 56.0, OP.is_gt)
+        flags(66, "y", 512.0, z0, 10 + (t - 1) * 4)
+        pe(r("p5", 256, 454), r("bb"), r("fl"), True, True)
+        pe(r("p5", 0, 198), r("lt"), r("fl"), True, True)
+        v("scan", r("sc"), r("mk3"), r("p5", 256, 454), 0.0, OP.mult, OP.add)
+        v("tt", r("p6", 256, 453), r("sc", 0, 197), r("p5", 1, 198), OP.add)
+        v("tt", r("zz", 0, 197), r("p6", 256, 453), r("fl", 1, 198), OP.mult)
+
+        def add(lo, hi, src, at):
+            if hi > lo:
+                v("tt", r("pf", lo, hi), r(src[0], src[1] + lo, src[1] + hi), r("zz", at, at + hi - lo), OP.add)
+
+        def merge(seg, st, src):
+            c0 = st // 16
+            if st == 0:
+                add(0, 64, src, seg)
+                return
+            add(c0 + 1, 64, src, seg + 1)
+            add(0, c0, src, seg + 64 - c0)
+            add(c0, c0 + 1, src, seg)
+            add(c0, c0 + 1, ("pf", 0), seg + 64)
+        merge(0, a0, ("zz", 132))
+        merge(66, z0, ("pf", 0))
+        v("copy", r("pos"), r("pf"))
+
+    def consts_a():
+        v("set", r("one"), 1.0)
+        v("set", r("onf"), 1.0 / 4096)
+        v("set", r("ce", 0, 1), 0.0)
+        v("set", r3("ftb", slice(1, 32, 2), 7, 15, 256, 16), 0.0)
+        act(r("bb9"), r("bb"), AF.Copy, scale=-9.0)
+        act(r("idm"), r("id"), AF.Copy, scale=8192.0)
+
+    def consts_b():
+        for q in range(16):
+            act(r("nsel", 128 * q, 128 * q + 128), r("sel", 128 * q, 128 * q + 128), AF.Copy, scale=-1.0)
+        ts(kx(0), qc, -512.0, OP.mult, 7680.0, OP.add)
+        ts(kx(2), hb, -1.0, OP.mult, 1.0, OP.add)
+        ts(kx(3), qc, 7.0, OP.is_equal)
+        ts(kx(5), pc, 16.0, OP.add)
+        ts(kx(6), pc, -16.0, OP.add)
+        ts(kx(4), kx(3), -256.0, OP.mult, 256.0, OP.add)
+        ts(r("dg"), r("im"), pc, OP.is_equal, kx(0), OP.mult)
+        act(r("id8"), r("id"), AF.Copy, scale=8.0)
+        for t in range(1, 4):
+            for c, st in enumerate(((170 * t) % 1024, (341 * t) % 1024)):
+                ts(kx(8 + (t - 1) * 4 + 2 * c), qc, float(st % 16), OP.is_ge)
+                ts(kx(9 + (t - 1) * 4 + 2 * c), qc, float(st % 16), OP.is_lt)
+        ts(r("gif"), r("g8"), gc, OP.is_equal)
+        ts(r("mb"), r("gif"), kx(4), OP.mult)
+        ts(r("cbm"), r("gif"), kx(3), OP.mult)
+        for a2 in range(2):
+            for g2 in range(2):
+                x = (pc, kx(5), kx(6))[(g2 - a2) % 3]
+                i = (a2 * 2 + g2) * 256
+                ts(r("qm", i, i + 128), r("im"), x, OP.is_equal, (kx(2), hb)[a2], OP.mult)
+                ts(r("qm", i + 128, i + 256), r("qm", i, i + 128), 64.0, OP.mult)
+        ts(r("lw"), r("lw0"), qc, OP.add)
+        ts(r("tg1"), r("lw"), -1.0, OP.mult, 3585.0, OP.add)
+        for a in SCOLS:
+            v("set", r("tg1", a, a + 1), 1.0)
+        ts(r("bias"), r("lw"), -3584.0, OP.add)
+        v("copy", r("tr", 0, 16), r("lw"))
+        ts(r("tr", 16, 32), r("lw"), 256.0, OP.add)
+        ts(r3("ftb", slice(0, 32, 2), 7, 7, 256, 16), r("l70"), p31, OP.subtract)
+        ts(r("jc1"), r("jc0"), qc, OP.add)
+        ts(r("jc8"), r("jc1"), -4096.0, OP.mult, 4096.0 * 255, OP.add)
+        v("copy", r("thf"), r("thi"))
+        v("copy", r("thr"), r("thi"))
+
+    ts(r("gi"), r("g8"), gc, OP.is_equal)
+    v("set", r("sel"), 0.0)
+    for q in range(16):
+        act(r("sel", q * 129, q * 128 + 128, 16), r("gi"))
+    ts(r("frb", P=64), r("fr0", P=64), 16.0, OP.mult)
+    pe(r("p6", 0, 64), r("frb", P=64), ("id", T.q_id[0:64, 0:64], 0, 64, 1), True, True)
+    v("set", r("xt", 8704, 8720), 63.0)
+    rank_stage(0, r("p6", 0, 64))
+    POS = r("pos")
+    XG = r("xt", XW0, XE)
+    for i in range(2):
+        act(r("xt", 4608 + 2048 * i, 6656 + 2048 * i), r("xt", 512 + 2048 * i, 2560 + 2048 * i), AF.Identity, scale=-1.0, bias=kx(21))
+    consts_a()
+    v("copy", ind(r("w"), POS), r("ci"))
+
+    for t in range(4):
+        last = t == 3
+        marks.append(len(ops) if t else 0)
+        dst = T.cores[(rank + 1 + t % 3) % len(T.cores)]
+        if t:
+            v("copy", ind(r("w"), POS), r("cb"))
+        for lo, hi in ((0, LS), (LS, 256)):
+            v("copy", r("lua", lo, hi), r("w", lo, hi))
+            if lo:
+                lo = LB
+            act(r("sa", 16 * lo, 16 * hi), ind(XG, r("lua", lo, hi)))
+        v("copy", r("sa", 16 * LS, 16 * LB), ind(XG, r("lua", LS, LB)))
+        v("copy", r("luz"), r("w", ZB, ZB + 256))
+        for i in range(2):
+            act(r("sz", 2048 * i, 2048 * i + 2048), ind(XG, r("luz", 128 * i, 128 * i + 128)))
+        ts(r("dra"), r("zz", 132, 196), 1.0, OP.is_lt, 1e5, OP.mult)
+        ts(r("drb"), r("zz", 132, 196), 2.0, OP.mult, -4224.0, OP.add)
+        v("tt", r("dr"), r("dra"), r("drb"), OP.add)
+        if t == 0:
+            consts_b()
+        v("copy", r("li"), r("w", 0, 256))
+        ts(r("lo"), r("li"), 63, OP.bitwise_and)
+
+        def totals(lo, hi, k0, k1):
+            o = r("p3", lo // 2, hi // 2)
+            for k in range(k0, k1):
+                pe(o, r("sel", 128 * k, 128 * k + 128), r("sa", 16 * lo + 16 + k, 16 * hi, 32), k == 0, False)
+                pe(o, r("nsel", 128 * k, 128 * k + 128), r("sa", 16 * lo + k, 16 * hi, 32), False, k == 15)
+
+        def block(lo, hi, fp, filler):
+            v("scan", r("mx", 16 * lo, 16 * hi), r("mk", 16 * lo, 16 * hi), r("sa", 16 * lo, 16 * hi), 0.0, OP.mult, OP.max)
+            ts(r("fa", lo, hi), r("mx", 16 * lo + 15, 16 * hi, 16), r("thr"), OP.is_lt)
+            pe(r(fp, lo, hi), r("idm"), r("fa", lo, hi), True, True)
+            pe(r("p1", lo, hi), r("bb9"), r("fa", lo, hi), True, True)
+            pe(r("p0", lo, hi), r("dg"), r("one", lo, hi), True, False)
+            filler()
+            for k in range(16):
+                m = r("sm", 256 * k + lo, 256 * k + hi)
+                v("tt", m, r("sa", 16 * lo + k, 16 * hi, 16), r(fp, lo, hi), OP.mult)
+                pe(r("p0", lo, hi), r("sel", 128 * k, 128 * k + 128), m, False, k == 15)
+                if k == 3:
+                    ts(r("vi", lo, hi), r("p1", lo, hi), -40.0, OP.is_lt, 256.0, OP.mult)
+                    pe(r("p0", lo, hi), r("id"), r("vi", lo, hi), False, False)
+        totals(0, LB, 0, 8)
+        block(0, LB, "p2", lambda: v("tt", r("dj"), r("w", 1, 256, 2), r("w", 0, 256, 2), OP.subtract))
+        totals(0, LB, 8, 13)
+        block(LB, 256, "p7", lambda: ts(r("hi"), r("li"), 6, OP.arith_shift_right))
+        act(r("rw", 0, 256), r("p1", 0, 256), AF.Relu, bias=kx(20), scale=-1.0)
+        totals(0, LB, 13, 16)
+        totals(LB, 256, 0, 16)
+        v("tt", r("ab", 0, 256), r("p0", 0, 256), r("hi"), OP.add)
+        v("tt", r("ab", 256, 512), r("p0", 0, 256), r("lo"), OP.add)
+        v("vt", r("at"), r("ab"))
+        v("scan", r("scn"), r("mk", 0, 512), r("at"), 0.0, OP.mult, OP.max)
+        for d in range(2):
+            v("copy", r("di", d, 32, 2), r("scn", 256 * d + 15, 256 * d + 256, 16))
+        for f in range(7):
+            ts(r3("fti", slice(None), f, f, 256, 8), r("di"), f if f < 6 else 8, OP.arith_shift_right, 1, OP.bitwise_and)
+        ts(r("ddi", 0, 32), r("di"), 127, OP.bitwise_and)
+        ts(r("ddi", 32, 48), r("di", 1, 32, 2), 8, OP.arith_shift_right, 1, OP.bitwise_and)
+        ts(r3("ftb", slice(None), slice(0, 7)), r3("fti", slice(None), slice(0, 7)), 2.0, OP.mult, -1.0, OP.add)
+        v("copy", r("db"), r("ddi"))
+        v("vt", r3("fe", slice(None)), r3("ftb", slice(None)))
+        for gr in range(8):
+            o = r3("bd", slice(None), slice(16 * gr, 16 * gr + 16), 16 * gr, 16 * gr + 16)
+            if gr in BDS:
+                act(o, r3("fe", slice(None)), AF.Identity, bias=r("cbm", gr, gr + 1), scale=r("mb", gr, gr + 1))
+            else:
+                ts(o, r3("fe", slice(None)), r("mb", gr, gr + 1), OP.mult, r("cbm", gr, gr + 1), OP.add)
+
+        def qmat(a2, g2, m):
+            i = (a2 * 2 + g2) * 256 + 128 * m
+            return r("qm", i, i + 128)
+        for a2 in range(2):
+            pe(r("p4", a2, 16, 2), qmat(a2, 0, 1), r("db", 0, 32, 4), True, False)
+            pe(r("p4", a2, 16, 2), qmat(a2, 1, 1), r("db", 2, 32, 4), False, False)
+            pe(r("p4", a2, 16, 2), qmat(a2, 0, 0), r("db", 1, 32, 4), False, False)
+            pe(r("p4", a2, 16, 2), qmat(a2, 1, 0), r("db", 3, 32, 4), False, True)
+            pe(r("p4", 16 + a2, 32, 2), qmat(a2, 0, 0), r("db", 32, 48, 2), True, False)
+            pe(r("p4", 16 + a2, 32, 2), qmat(a2, 1, 0), r("db", 33, 48, 2), False, True)
+        ts(r("p3", 128, 256), r("p3", 0, 128), 0.0, OP.is_gt)
+        v("tt", r("p3", 256, 384), r("dj"), r("p3", 128, 256), OP.mult)
+        v("tt", r("jt"), r("p3", 256, 384), r("w", 0, 256, 2), OP.add)
+        v("copy", r("cu"), r("p4", 0, 16))
+        act(r("sch"), ind(XG, r("cu")))
+        at = {}
+        for e, b, aa in DED:
+            o = 32 if b == 4 else 0
+            for a in aa:
+                at[a] = r("p%d" % b, o, o + 16 * (a + 1))
+                o += 16 * (a + 1)
+
+        def equal(banks):
+            for e, b, aa in banks:
+                for a in aa:
+                    pe(at[a], r3("bd", a), r3("fe", slice(0, a + 1)), True, True)
+        equal(DED[:2])
+        v("tt", r("p5", 0, 128), r("vi", 0, 256, 2), r("vi", 1, 256, 2), OP.min)
+        v("scan", r("ce", 1, 128), r("one", 0, 127), r("p5", 0, 127), 0.0, OP.mult, OP.add)
+        v("tt", r("p5", 128, 256), r("p5", 0, 128), r("nc"), OP.mult)
+        v("tt", r("o32"), r("p5", 128, 256), r("ce"), OP.add)
+        pe(r("p6", 0, 8), r("id"), r("jc8"), True, False)
+        for q in range(16):
+            pe(r("p6", 0, 8), r("sel", 128 * q, 128 * q + 128), r("o32", q, 128, 16), False, q == 15)
+        ts(r("cc", 0, 16), r("p4", 0, 16), 512.0, OP.add)
+        ts(r("ge"), r("p4", 0, 16), 4096.0, OP.is_lt, 8192.0, OP.mult)
+        ts(r("cm"), r("p4", 0, 16), -3584.0, OP.add)
+        v("tt", r("tg0"), r("tg1"), r("p4", 16, 32), OP.mult)
+        v("tt", r("cc", 16, 32), r("ge"), r("cm"), OP.add)
+        ts(r("tg"), r("tg0"), -1.0, OP.add)
+        equal(DED[2:4])
+        pe(r("p5", 256, 512), r("id8"), r("fa"), True, False)
+        pe(r("p5", 256, 512), r("id"), r("sch"), False, True)
+        equal(DED[4:])
+
+        def send():
+            ts(r("jo"), r("p6", 0, 8), 1.0 / 4096, OP.mult)
+            v("copy", ind(r("jw", 256 * t, 256 * t + 256), r("jo")), r("jt"))
+            rid, pid, _ = topo.addr(dst)
+            o, i, a, l, m = T.q_jl[:, 128 * t:128 * t + 128], T.q_jw[:, 256 * t:256 * t + 128], "a%d" % t, "l%d" % t, topo.mask(core, dst)
+            ne = len(topo.engines(T.cores[(rank - 1 - t % 3) % len(T.cores)], core))
+            ro, wo = ("jw", 256 * t, 256 * t + 128, 1, False), ("jl", 128 * t, 128 * t + 128, 1, True)
+
+            def issue():
+                deps("g", [ro])
+                g.remote_dma(o, i, T.sem[a], T.sem[l], pid, rid, m)
+                note(a, ne, [wo])
+            ops.append(("g", [ro, wo], 1.0, 3.0, issue))
+
+        def frozen(i):
+            v("scan", r("mz", 2048 * i, 2048 * i + 2048), r("mk", 0, 2048), r("sz", 2048 * i, 2048 * i + 2048), 0.0, OP.mult, OP.max)
+            ts(r("fz", 128 * i, 128 * i + 128), r("mz", 2048 * i + 15, 2048 * i + 2048, 16), r("thr"), OP.is_lt)
+            if i:
+                pe(r("p1", 256, 512), r("bb9"), r("fz"), True, True)
+
+        def frozen_codes():
+            act(r("rw", ZB, ZB + 256), r("p1", 256, 512), AF.Relu, bias=kx(20), scale=-1.0)
+            act(r("rg"), ind(r("rw"), POS))
+            if not last:
+                act(r("junk", 2176, 2432), r("vi"), AF.Copy, accum_out=r("vs"))
+
+        def lowest():
+            for e, b, aa in DED:
+                for a in aa:
+                    if e == "v":
+                        v("red", r("win", a, a + 1), at[a], AxisListType.X, OP.max)
+                    else:
+                        act(r("junk", 8 * a * (a + 1), 8 * (a + 1) * (a + 2)), at[a], AF.Relu, bias=r("bias", a, a + 1), accum_out=r("win", a, a + 1))
+            act(r("nv", 256, 512), r("p5", 256, 512), AF.Relu, bias=kx(21), scale=-1.0)
+            act(r("nv", 0, 256), r("nv", 256, 512), AF.Identity, bias=kx(21), scale=-1.0)
+
+        def arrivals():
+            jl = r("jl", 128 * t, 128 * t + 128)
+            act(r("junk", 2432, 2560), jl, AF.Sign, bias=kx(22), accum_out=r("ns"))
+            ts(r("p5", 0, 128), jl, -0.5, OP.is_gt, -16384.0, OP.mult)
+            v("tt", r("p5", 128, 256), r("w", DB0, DB0 + 128), r("p5", 0, 128), OP.add)
+            v("tt", r("w", DB0, DB0 + 128), r("p5", 128, 256), jl, OP.max)
+            ts(r("nt"), r("dr"), r("ns"), OP.is_ge)
+
+        def moves():
+            v("tt", r("wm", 0, 16), r("win"), r("tg"), OP.is_equal)
+            v("tt", r("wm", 16, 32), r("win"), r("tg"), OP.is_equal)
+            v("tt", r("of1"), r("cc"), r("wm"), OP.mult)
+            v("tt", r("of2"), r("of1"), r("tr"), OP.max)
+            v("copy", r("off"), r("of2"))
+            v("copy", ind(r("xt"), r("off")), r("nv"))
+        frozen(0)
+        frozen(1)
+        send()
+        lowest()
+        frozen_codes()
+        moves()
+        if last:
+            for i in range(2):
+                dma("y", T.yx[:, 2048 * i:2048 * i + 2048], r("xt", XW0 + 2048 * i, XW0 + 2048 * i + 2048))
+        arrivals()
+
+        def clauses_back():
+            if last:
+                act(r("cb", 0, 512), ind(r("w"), r("pos", 0, 32)))
+                v("copy", r("cb", 512, 1024), ind(r("w"), r("pos", 32, 64)))
+                dma("s", T.yc[:, 0:512], r("cb", 0, 512))
+                dma("y", T.yc[:, 512:1024], r("cb", 512, 1024))
+                return
+            act(r("cb"), ind(r("w"), POS))
+            for b in (0, ZB):
+                act(r("w", b, b + 256), r("one"), AF.Copy, scale=8192.0)
+        if last:
+            clauses_back()
+        pe(r("p6", 0, 64), r("id"), r("fn"), True, False)
+        for q in range(16):
+            pe(r("p6", 0, 64), r("nsel", 128 * q, 128 * q + 128), r("rg", q, 1024, 16), False, q == 15)
+        if not last:
+            pe(r("p4", 300, 301), r("onf"), r("vs"), True, True)
+            rank_stage(t + 1, r("p6", 0, 64), clauses_back)
+            v("copy", r("ai", 0, 1), r("p4", 300, 301))
+            ts(r("ai", 1, 2), r("ai", 0, 1), 3, OP.bitwise_and)
+            v("tt", r("thr"), r("ai", 1, 2), r("thf"), OP.add)
+    new_states(4, r("p6", 0, 64))
+    pe(r("p5", 0, 128, P=64), r("fn"), r("id"), True, True)
+    ts(r("fo", P=64), r("p5", 0, 128, P=64), 1.0 / 16, OP.mult)
+    for gr in range(8):
+        dma("y" if gr % 2 == 0 else "s", T.yf[gr:gr + 1, :], r("fo", 16 * gr, 16 * gr + 16, P=64))
+    order()
+    for q in "vstg":
+        need("g", "e" + q, cnt[q])
+    for i in range(nd[0]):
+        need("g", "d%d" % i, 16)
+    for t in range(4):
+        d = T.cores[(rank + 1 + t % 3) % len(T.cores)]
+        need("g", "l%d" % t, len(topo.engines(core, d)))

@@ -1,40 +1,39 @@
-from concourse.mybir import AluOpType as OP, AxisListType, ActivationFunctionType as AF
+from concourse.mybir import AluOpType as OP, ActivationFunctionType as AF
 
-F4, B2, I4, U2 = "float32", "bfloat16", "int32", "uint16"
+F4, B2, H2, I4, U2 = "float32", "bfloat16", "float16", "int32", "uint16"
+XW0, XE = 32, 8240
+ZB, DB0, WW = 1024, 2048, 3072
 SB = {
-    "xt": ([128, 8720], B2), "ci": ([128, 1024], I4), "cb": ([128, 1024], F4), "w": ([128, 3072], F4), "rw": ([128, 3072], B2),
-    "thi": ([128, 1], I4), "thf": ([128, 1], F4), "thr": ([128, 1], F4), "fr0": ([64, 128], I4), "frb": ([64, 128], B2),
+    "xt": ([128, XE], B2), "ci": ([128, 1024], I4), "cb": ([128, 1024], F4), "w": ([128, WW], F4), "rw": ([128, WW], B2),
+    "thi": ([128, 1], I4), "thf": ([128, 1], F4), "thr": ([128, 1], F4), "nthr": ([128, 1], F4), "fr0": ([64, 128], I4), "frb": ([64, 128], B2),
     "fn": ([128, 64], B2), "y": ([128, 64], B2), "fl": ([128, 198], B2), "sc": ([128, 198], F4), "zz": ([128, 198], F4),
     "pf": ([128, 64], F4), "pos": ([128, 64], U2), "fo": ([64, 128], F4),
     "lua": ([128, 256], U2), "luz": ([128, 256], U2), "sa": ([128, 4096], B2), "sz": ([128, 4096], B2), "mx": ([128, 4096], B2), "mz": ([128, 4096], B2),
-    "fa": ([128, 256], B2), "fz": ([128, 256], B2), "sm": ([128, 4096], B2), "vi": ([128, 256], B2),
-    "li": ([128, 256], I4), "hi": ([128, 256], I4), "lo": ([128, 256], I4), "ab": ([128, 512], F4), "at": ([128, 512], F4), "scn": ([128, 512], F4),
-    "di": ([128, 32], I4), "fti": ([128, 32, 8], I4), "ftb": ([128, 32, 8], B2), "fe": ([128, 16, 16], B2), "bd": ([128, 16, 128], B2),
-    "ddi": ([128, 48], I4), "db": ([128, 48], B2), "cu": ([128, 16], U2), "cc": ([128, 32], F4), "ge": ([128, 16], F4), "cm": ([128, 16], F4),
-    "tg": ([128, 16], F4), "tg0": ([128, 16], F4), "win": ([128, 16], F4), "wm": ([128, 32], F4), "of1": ([128, 32], F4), "of2": ([128, 32], F4), "off": ([128, 32], U2),
-    "sch": ([128, 256], B2), "nv": ([128, 512], B2), "junk": ([128, 2560], B2), "dra": ([128, 64], F4), "drb": ([128, 64], F4), "dr": ([128, 64], F4), "nt": ([128, 64], F4), "ns": ([128, 1], F4), "vs": ([128, 1], F4), "ai": ([128, 2], I4),
-    "dj": ([128, 128], F4), "jt": ([128, 128], F4), "ce": ([128, 128], B2), "o32": ([128, 128], B2),
+    "fa": ([128, 256], B2), "fz": ([128, 256], B2), "sm": ([128, 4096], B2), "vn": ([128, 256], B2), "hib": ([128, 256], B2),
+    "scn": ([128, 512], F4), "di": ([128, 32], I4), "dd": ([128, 2, 16], I4), "df": ([128, 4, 8], H2), "hs": ([128, 128], F4),
+    "g1": ([128, 16], F4), "key": ([128, 16], H2), "cm": ([128, 16], F4), "cu": ([128, 16], U2), "pr": ([128, 256], F4),
+    "wm": ([128, 16], F4), "x1": ([128, 32], F4), "off": ([128, 32], U2), "sch": ([128, 256], B2), "nv": ([128, 16, 32], B2),
+    "junk": ([128, 384], B2), "dra": ([128, 64], F4), "drb": ([128, 64], F4), "dr": ([128, 64], F4), "nt": ([128, 64], F4),
+    "ns": ([128, 1], F4), "vs": ([128, 1], F4), "ai": ([128, 2], I4),
+    "dj": ([128, 128], F4), "je": ([128, 128], F4), "jb": ([128, 128], B2), "jt": ([128, 512], B2), "cn": ([128, 32], B2), "imn": ([128, 128], B2), "ju": ([128, 128], B2),
     "jo": ([128, 8], U2), "jw": ([128, 1024], F4), "jl": ([128, 512], F4), "rg": ([128, 1024], B2),
-    "im": ([128, 128], F4), "img": ([128, 128], F4), "g8": ([128, 8], F4), "ki": ([128, 8], I4), "kf": ([128, 8], F4), "kx": ([128, 32], F4),
-    "gi": ([128, 8], B2), "gif": ([128, 8], F4), "mb": ([128, 8], F4), "cbm": ([128, 8], F4), "bb": ([128, 128], B2), "bb9": ([128, 128], B2), "gt": ([128, 128], B2), "lt": ([128, 128], B2),
-    "id": ([128, 128], B2), "idm": ([128, 128], B2), "id8": ([128, 128], B2), "dg": ([128, 128], B2), "sel": ([128, 2048], B2), "nsel": ([128, 2048], B2), "qm": ([128, 1024], B2),
-    "lw0": ([128, 16], F4), "lw": ([128, 16], F4), "tg1": ([128, 16], F4), "bias": ([128, 16], F4), "tr": ([128, 32], F4), "l70": ([128, 16], F4),
-    "nc": ([128, 128], B2), "jc0": ([128, 8], F4), "jc1": ([128, 8], F4), "jc8": ([128, 8], B2), "mk": ([128, 4096], B2), "mk3": ([128, 198], B2), "one": ([128, 256], B2), "onf": ([128, 128], F4),
+    "im": ([128, 128], F4), "img": ([128, 128], F4), "imq": ([128, 128], B2), "g8r": ([128, 128], B2), "g8": ([128, 8], F4),
+    "ki": ([128, 8], I4), "kf": ([128, 8], F4), "kx": ([128, 32], F4), "gi": ([128, 8], B2), "gif": ([128, 8], F4), "g2": ([128, 16], B2),
+    "bb": ([128, 128], B2), "bb9": ([128, 128], B2), "gt": ([128, 128], B2), "lt": ([128, 128], B2), "id": ([128, 128], B2),
+    "idf": ([128, 128], F4), "ih": ([128, 256], B2), "dg": ([128, 256], B2), "idv": ([128, 128], B2), "id8": ([128, 128], B2),
+    "nid": ([128, 128], B2), "sd": ([128, 1920], B2), "qm": ([128, 128], B2), "ea": ([128, 1024], B2), "ramp": ([128, 128], B2),
+    "rp0": ([128, 128], B2), "pat": ([128, 128], B2), "dcon": ([128, 256], B2), "one0": ([128, 256], B2), "mkb": ([128, 256], B2),
+    "sel": ([128, 2048], B2), "nsel": ([128, 2048], B2), "jc0": ([128, 8], F4), "jc8": ([128, 8], B2), "mk": ([128, 2048], B2),
+    "mk3": ([128, 198], B2), "one": ([128, 256], B2), "neg": ([128, 128], B2), "onf": ([128, 128], F4),
 }
 SCRATCH = {"q_" + k: ("sbuf", v[0], v[1]) for k, v in SB.items()}
-SCRATCH.update({"q_p%d" % i: ("psum", [128, 512], F4) for i in range(8)})
+SCRATCH.update({"q_p%d" % i: ("psum", [128, 8, 64] if i == 4 else [128, 512], F4) for i in range(8)})
 NDMA = 40
-SEMAPHORES = ["ev", "es", "et", "eg"] + ["a%d" % t for t in range(4)] + ["l%d" % t for t in range(4)] + ["d%d" % i for i in range(NDMA)]
-XW0, XE = 512, 8720
-ZB, DB0, WW = 1024, 2048, 3072
-LS, LB = 96, 144
-BDS = (2, 3, 4, 5, 6, 7)
-DED = (("s", 0, (15, 14)), ("s", 7, (13, 12)), ("s", 3, (11, 10)), ("s", 2, (9, 8, 7)), ("v", 4, (6, 5, 4, 3, 2, 1, 0)))
-SCOLS = tuple(a for e, b, aa in DED if e == "s" for a in aa)
+SEMAPHORES = ["ev", "es", "et", "eg"] + [x + str(t) for x in "acl" for t in range(4)] + ["d%d" % i for i in range(NDMA)]
+ACTIVE = (("s", 0, 64), ("v", 64, 128), ("s", 128, 192), ("s", 192, 256))
+FROZEN = (("s", 0, 64, "v"), ("s", 64, 128, "v"), ("s", 128, 192, "v"), ("s", 192, 256, "v"))
 
-
-CY, CPE, WAKE, FIX, SLACK, GAMMA, SIGMA = 0.00105, 0.0009, 0.11, 0.01, 0.05, 1.7, 3.5
-SEEDS = (313303, 302857, 208832, 398229, 87847, 179512, 39628, 96281, 664645, 136495)
+CY, CPE, PFIX, WAKE, WAKEX, SLACK, GAMMA, SIGMA, IND, SIND = 0.0009, 0.0004, 0.04, 0.2, 0.15, 0.05, 1.3, 2.8, 0.055, 0.15
 
 
 def rank_program(g, core, T, topo):
@@ -50,11 +49,10 @@ def rank_program(g, core, T, topo):
         t = T["q_" + n]
         hi = t.shape[1] if hi is None else hi
         lo = 0 if lo is None else lo
-        return (n, t[0:P, lo:hi:step] if step != 1 else t[0:P, lo:hi], lo, hi, step)
+        return (n, t[0:P, lo:hi:step] if step != 1 else t[0:P, lo:hi], lo, hi, step, -(-(hi - lo) // step))
 
-    def r3(n, a, b=slice(None), lo=0, hi=1 << 20, st=1):
-        t = T["q_" + n]
-        return (n, t[:, a, b], lo, hi, st)
+    def r3(n, a, b, lo, hi, els):
+        return (n, T["q_" + n][:, a, b], lo, hi, 1, els)
 
     def ind(w, o):
         return ("@", w, o)
@@ -98,55 +96,52 @@ def rank_program(g, core, T, topo):
         acc, real, kk = [], [], {}
         for i, a in enumerate(args):
             if isinstance(a, tuple) and a[0] == "@":
-                acc.append((a[1][0],) + a[1][2:] + (i == 0,))
-                acc.append((a[2][0],) + a[2][2:] + (False,))
+                acc.append((a[1][0],) + a[1][2:5] + (i == 0,))
+                acc.append((a[2][0],) + a[2][2:5] + (False,))
                 real.append(a[1][1].indirect(a[2][1]))
             elif isinstance(a, tuple):
-                acc.append((a[0],) + a[2:] + (i == 0,))
+                acc.append((a[0],) + a[2:5] + (i == 0,))
                 real.append(a[1])
             else:
                 real.append(a)
         for k, a in kw.items():
             if isinstance(a, tuple):
-                acc.append((a[0],) + a[2:] + (k == "accum_out",))
+                acc.append((a[0],) + a[2:5] + (k == "accum_out",))
                 kk[k] = a[1]
             else:
                 kk[k] = a
         return acc, real, kk
 
-    ops, marks = [], []
+    ops = []
 
     def cols(a):
-        if a[0] == "@":
-            return 16 * cols(a[2])
-        return min(-(-(a[3] - a[2]) // a[4]), 256 if a[3] >= 1 << 20 else 1 << 20)
+        return 16 * a[2][5] if a[0] == "@" else a[5]
 
     def cost(q, name, args):
         xs = [a for a in args if isinstance(a, tuple)]
         n = max(cols(a) for a in xs[1:]) if len(xs) > 1 else cols(xs[0])
-        names = [a[1][0] if a[0] == "@" else a[0] for a in xs]
-        two = all(b in SB and SB[b][1] in (B2, U2) for b in names)
+        names = [a[1][0] if a[0] == "@" else a[0] for a in xs if a[0] == "@" or a[5] > 1]
+        two = all(b in SB and SB[b][1] in (B2, U2, H2) for b in names)
         if name == "mm":
-            return max(64, cols(args[2])) * (4 if SB[args[2][0]][1] == F4 else 1) * CPE
-        if name == "iota":
-            return 0.13 + 2 * cols(args[0]) * CY
+            return max(64, cols(args[2])) * (4 if SB[args[2][0]][1] == F4 else 1) * CPE + PFIX
+        if q == "g":
+            return 0.15 + 2 * cols(args[0]) * CY
         if args[0][0] == "@":
-            n *= SIGMA
-        elif any(a[0] == "@" for a in xs):
-            n *= GAMMA
-        elif name == "tt":
+            return SIND + n * SIGMA * CY
+        if any(a[0] == "@" for a in xs):
+            return IND + n * GAMMA * CY
+        if name == "tt":
             n *= 1 if any(len(b) == 2 and b[0] == "p" for b in names) else 2
-        elif name in ("copy", "ts", "scan", "vt", "set") and two:
+        elif name in ("copy", "ts", "scan", "set") and two:
             n *= 0.5
-        return max(n, 64) * CY + FIX
+        return max(n, 64) * CY
 
     def do(q, name, *args, **kw):
         acc, real, kk = flat(args, kw)
         e = Q[q]
         f = {"copy": lambda: e.tensor_copy(*real), "tt": lambda: e.tensor_tensor(*real), "ts": lambda: e.tensor_scalar(*real),
-             "set": lambda: e.memset(*real), "red": lambda: e.tensor_reduce(*real), "scan": lambda: e.tensor_tensor_scan(*real),
-             "vt": lambda: e.transpose(*real), "act": lambda: e.activation(*real, **kk), "mm": lambda: e.matmul(*real),
-             "iota": lambda: e.iota(*real, **kk)}[name]
+             "set": lambda: e.memset(*real), "scan": lambda: e.tensor_tensor_scan(*real), "act": lambda: e.activation(*real, **kk),
+             "mm": lambda: e.matmul(*real), "iota": lambda: e.iota(*real, **kk), "asel": lambda: e.affine_select(*real)}[name]
 
         def issue():
             deps(q, acc)
@@ -163,7 +158,7 @@ def rank_program(g, core, T, topo):
         for i, a in enumerate((out, in_)):
             ap.append(a[1] if isinstance(a, tuple) else a)
             if isinstance(a, tuple):
-                acc.append((a[0],) + a[2:] + (i == 0,))
+                acc.append((a[0],) + a[2:5] + (i == 0,))
 
         def issue():
             deps(q, acc)
@@ -172,7 +167,19 @@ def rank_program(g, core, T, topo):
             Q[q].dma_start(ap[0], ap[1]).then_inc(T.sem[x], 16)
             snap[(x, 16)] = dict(know[q])
             note(x, 16, acc)
-        ops.append((q, acc, 0.08, 2.5 + (acc[0][2] - acc[0][1]) / 1000, issue))
+        ops.append((q, acc, 0.06, 2.0 + (acc[0][2] - acc[0][1]) / 700, issue))
+
+    def send(out, in_, sem, t, way):
+        dst = T.cores[(rank + 1 + t % 3) % len(T.cores)]
+        rid, pid, _ = topo.addr(dst)
+        ne = len(topo.engines(T.cores[(rank - 1 - t % 3) % len(T.cores)], core))
+        ro, wo = (in_[0],) + in_[2:5] + (False,), (out[0],) + out[2:5] + (True,)
+
+        def issue():
+            deps("g", [ro])
+            g.remote_dma(out[1], in_[1], T.sem[sem], T.sem["l%d" % t], pid, rid, topo.mask(core, dst))
+            note(sem, ne, [wo])
+        ops.append(("g", [ro, wo], 1.0, way, issue))
 
     def order():
         n = len(ops)
@@ -192,7 +199,7 @@ def rank_program(g, core, T, topo):
                         if bank and q == "t" and q2 == "t":
                             pre[i].setdefault(j, 0.0)
                         elif (bank and q != q2) or ((w or w2) and over((lo, hi, st), (l2, h2, s2))):
-                            pre[i][j] = WAKE
+                            pre[i][j] = WAKE if q == q2 else WAKEX
             for (b, lo, hi, st, w) in acc:
                 hist[b][0 if w else 1].append((i, q, lo, hi, st, w))
         post = [[] for _ in range(n)]
@@ -203,12 +210,6 @@ def rank_program(g, core, T, topo):
         way = [0.0] * n
         for i in range(n - 1, -1, -1):
             way[i] = ops[i][3] + max([way[j] + pre[j][i] for j in post[i]], default=0.0)
-        per = marks[2] - marks[1]
-        for seed in SEEDS:
-            for m in marks:
-                i = m + seed % per if m else marks[1] - per + seed % per
-                if i < n:
-                    way[i] += (seed // per % 64 - 31.5) * 0.15
         left = [len(p) for p in pre]
         ready = {q: {} for q in Q}
         free = {q: 0.0 for q in Q}
@@ -265,35 +266,35 @@ def rank_program(g, core, T, topo):
     iota(r("im"), [[1, 128]], 0, 0)
     iota(r("img"), [[1, 8], [0, 16]], 0, 0)
     iota(r("g8"), [[1, 8]], 0, 0)
-    iota(r("lw0"), [[16, 16]], 0, 0)
-    iota(r("w"), [[0, WW]], 8192, 0)
-    iota(r("l70"), [[-32, 8], [0, 2]], 0, 0)
-    iota(r("jc0"), [[16, 8]], 0, 0)
-    iota(r("nc"), [[1, 128]], -255, 0)
-    iota(r("rw"), [[0, WW]], 1, 0)
-    iota(r("jw"), [[0, 1024]], -20, 0)
+    for b, n in ((0, 256), (ZB, 256), (DB0, 128)):
+        iota(r("w", b, b + n), [[0, n]], 8192, 0)
+    iota(r("mk", 0, 1024), [[0, 64], [64, 16]], 0, 0)
+    iota(r("imq"), [[0, 8], [1, 16]], 0, 0)
+    iota(r("g8r"), [[0, 16], [1, 8]], 0, 0)
+    iota(r("jc0"), [[256, 8]], 2048, 0)
+    iota(r("jw", 0, 256), [[0, 256]], -20, 0)
     kx = lambda i: r("kx", i, i + 1)
     v("set", r("fl"), 0.0)
     v("set", r("fl", 66, 67), 64.0)
     v("set", r("fl", 132, 133), 128.0)
     v("set", r("mk3"), 1.0)
     v("set", r("mk3", 0, 198, 66), 0.0)
-    v("set", kx(7), -32.0)
-    v("set", kx(20), -36.0)
-    v("set", kx(21), 63.0)
-    v("set", kx(22), 0.5)
-    v("set", r("mk"), 1.0)
-    v("set", r("mk", 0, 4096, 16), 0.0)
+    for i, c in ((7, -32.0), (20, -36.0), (21, 63.0), (22, 0.5), (23, 1.0)):
+        v("set", kx(i), c)
     ts(r("ki", 1, 2), r("ki", 0, 1), 15, OP.bitwise_and)
     ts(r("ki", 2, 3), r("ki", 0, 1), 4, OP.arith_shift_right)
-    ts(r("ki", 3, 4), r("ki", 0, 1), 31, OP.bitwise_and)
-    ts(r("ki", 4, 5), r("ki", 0, 1), 4, OP.arith_shift_right, 1, OP.bitwise_and)
-    v("copy", r("kf", 0, 5), r("ki", 0, 5))
-    pc, qc, gc, p31, hb = [r("kf", i, i + 1) for i in range(5)]
+    v("copy", r("kf", 0, 3), r("ki", 0, 3))
+    pc, qc, gc = [r("kf", i, i + 1) for i in range(3)]
     ts(r("id"), r("im"), pc, OP.is_equal)
     ts(r("bb"), r("img"), gc, OP.is_equal)
     ts(r("gt"), r("im"), pc, OP.is_gt)
     v("tt", r("lt"), r("gt"), r("bb"), OP.mult)
+    act(r("nid"), r("id"), AF.Copy, scale=-1.0 / 256)
+    for d in range(1, 16):
+        do("g", "asel", r("sd", 128 * d - 128, 128 * d), r("nid"), [[1, 128]], OP.not_equal, 1.0 / 256, -d, -1)
+    for lo, hi in ((256, ZB), (ZB + 256, WW)):
+        iota(r("rw", lo, hi), [[0, hi - lo]], 1, 0)
+    iota(r("jw", 256, 1024), [[0, 768]], -20, 0)
 
     def new_states(t, xw):
         if t == 0:
@@ -344,242 +345,184 @@ def rank_program(g, core, T, topo):
         merge(66, z0, ("pf", 0))
         v("copy", r("pos"), r("pf"))
 
-    def consts_a():
+    def consts():
         v("set", r("one"), 1.0)
-        v("set", r("onf"), 1.0 / 4096)
-        v("set", r("ce", 0, 1), 0.0)
-        v("set", r3("ftb", slice(1, 32, 2), 7, 15, 256, 16), 0.0)
+        v("set", r("neg"), -1.0)
+        v("set", r("onf"), -1.0 / 16)
         act(r("bb9"), r("bb"), AF.Copy, scale=-9.0)
-        act(r("idm"), r("id"), AF.Copy, scale=8192.0)
-
-    def consts_b():
+        act(r("id8"), r("id"), AF.Copy, scale=-8.0)
+        act(r("idv"), r("id"), AF.Copy, scale=-256.0)
+        act(r("idf"), r("id"))
+        act(r("ih", 0, 128), r("id"))
+        act(r("ih", 128, 256), r("id"), AF.Copy, scale=-64.0)
+        act(r("mkb"), r("mk", 0, 256), AF.Copy, scale=float(1 << 18))
+        ts(r("gi"), r("g8"), gc, OP.is_equal)
+        ts(r("gif"), r("g8"), gc, OP.is_equal)
+        for c in range(2):
+            ts(r("g2", 8 * c, 8 * c + 8), r("g8"), gc, OP.is_equal, -8192.0, OP.mult)
+        v("set", r("sel"), 0.0)
         for q in range(16):
-            act(r("nsel", 128 * q, 128 * q + 128), r("sel", 128 * q, 128 * q + 128), AF.Copy, scale=-1.0)
-        ts(kx(0), qc, -512.0, OP.mult, 7680.0, OP.add)
-        ts(kx(2), hb, -1.0, OP.mult, 1.0, OP.add)
-        ts(kx(3), qc, 7.0, OP.is_equal)
-        ts(kx(5), pc, 16.0, OP.add)
-        ts(kx(6), pc, -16.0, OP.add)
-        ts(kx(4), kx(3), -256.0, OP.mult, 256.0, OP.add)
-        ts(r("dg"), r("im"), pc, OP.is_equal, kx(0), OP.mult)
-        act(r("id8"), r("id"), AF.Copy, scale=8.0)
+            act(r("sel", q * 129, q * 128 + 128, 16), r("gi"))
+        for i in range(4):
+            ts(r("nsel", 512 * i, 512 * i + 512), r("sel", 512 * i, 512 * i + 512), -1.0, OP.mult)
+        ts(kx(0), qc, -512.0, OP.mult, 7680.0 - 160, OP.add)
+        ts(kx(1), qc, -512.0, OP.mult, 7680.0 + 8192, OP.add)
+        ts(kx(2), qc, 64.0, OP.mult)
+        ts(kx(3), qc, 16.0, OP.add)
+        ts(kx(4), qc, 16.0, OP.mult)
+        for c in range(2):
+            act(r("dg", 128 * c, 128 * c + 128), r("id"), AF.Identity, scale=kx(c))
         for t in range(1, 4):
             for c, st in enumerate(((170 * t) % 1024, (341 * t) % 1024)):
                 ts(kx(8 + (t - 1) * 4 + 2 * c), qc, float(st % 16), OP.is_ge)
                 ts(kx(9 + (t - 1) * 4 + 2 * c), qc, float(st % 16), OP.is_lt)
-        ts(r("gif"), r("g8"), gc, OP.is_equal)
-        ts(r("mb"), r("gif"), kx(4), OP.mult)
-        ts(r("cbm"), r("gif"), kx(3), OP.mult)
-        for a2 in range(2):
-            for g2 in range(2):
-                x = (pc, kx(5), kx(6))[(g2 - a2) % 3]
-                i = (a2 * 2 + g2) * 256
-                ts(r("qm", i, i + 128), r("im"), x, OP.is_equal, (kx(2), hb)[a2], OP.mult)
-                ts(r("qm", i + 128, i + 256), r("qm", i, i + 128), 64.0, OP.mult)
-        ts(r("lw"), r("lw0"), qc, OP.add)
-        ts(r("tg1"), r("lw"), -1.0, OP.mult, 3585.0, OP.add)
-        for a in SCOLS:
-            v("set", r("tg1", a, a + 1), 1.0)
-        ts(r("bias"), r("lw"), -3584.0, OP.add)
-        v("copy", r("tr", 0, 16), r("lw"))
-        ts(r("tr", 16, 32), r("lw"), 256.0, OP.add)
-        ts(r3("ftb", slice(0, 32, 2), 7, 7, 256, 16), r("l70"), p31, OP.subtract)
-        ts(r("jc1"), r("jc0"), qc, OP.add)
-        ts(r("jc8"), r("jc1"), -4096.0, OP.mult, 4096.0 * 255, OP.add)
+        ts(r("qm"), r("imq"), qc, OP.is_equal)
+        for a in range(8):
+            act(r("ea", 128 * a, 128 * a + 128), r("qm"), AF.Identity, scale=r("gif", a, a + 1))
+        ts(r("rp0"), r("g8r"), gc, OP.subtract)
+        ts(r("ramp"), r("rp0"), 32768.0, OP.mult, -18432.0, OP.add)
+        ts(r("pat"), r("g8r"), gc, OP.is_le, float(1 << 20), OP.mult)
+        ts(r("dcon"), r("mk", 0, 256), kx(2), OP.is_gt, 128.0, OP.mult)
+        ts(r("imn"), r("im"), -256.0, OP.add)
+        ts(r("one0"), r("mk", 0, 256), 1.0, OP.is_lt)
+        ts(r("jc8"), r("jc0"), kx(4), OP.add)
         v("copy", r("thf"), r("thi"))
         v("copy", r("thr"), r("thi"))
+        ts(r("nthr"), r("thf"), -1.0, OP.mult, 1.0, OP.add)
 
-    ts(r("gi"), r("g8"), gc, OP.is_equal)
-    v("set", r("sel"), 0.0)
-    for q in range(16):
-        act(r("sel", q * 129, q * 128 + 128, 16), r("gi"))
     ts(r("frb", P=64), r("fr0", P=64), 16.0, OP.mult)
-    pe(r("p6", 0, 64), r("frb", P=64), ("id", T.q_id[0:64, 0:64], 0, 64, 1), True, True)
-    v("set", r("xt", 8704, 8720), 63.0)
+    pe(r("p6", 0, 64), r("frb", P=64), ("id", T.q_id[0:64, 0:64], 0, 64, 1, 64), True, True)
+    v("set", r("xt", XE - 16, XE), 63.0)
+    v("set", r("xt", 0, XW0), 0.0)
     rank_stage(0, r("p6", 0, 64))
     POS = r("pos")
     XG = r("xt", XW0, XE)
-    for i in range(2):
-        act(r("xt", 4608 + 2048 * i, 6656 + 2048 * i), r("xt", 512 + 2048 * i, 2560 + 2048 * i), AF.Identity, scale=-1.0, bias=kx(21))
-    consts_a()
-    v("copy", ind(r("w"), POS), r("ci"))
+    for i in range(4):
+        o, x = r("xt", XW0 + 4096 + 1024 * i, XW0 + 5120 + 1024 * i), r("xt", XW0 + 1024 * i, XW0 + 1024 + 1024 * i)
+        if i % 2:
+            ts(o, x, -1.0, OP.mult, 63.0, OP.add)
+        else:
+            act(o, x, AF.Identity, scale=-1.0, bias=kx(21))
+    consts()
 
     for t in range(4):
         last = t == 3
-        marks.append(len(ops) if t else 0)
-        dst = T.cores[(rank + 1 + t % 3) % len(T.cores)]
-        if t:
-            v("copy", ind(r("w"), POS), r("cb"))
-        for lo, hi in ((0, LS), (LS, 256)):
+        v("copy", ind(r("w"), POS), r("cb" if t else "ci"))
+        for lo, hi in ((0, 64), (64, 256)):
             v("copy", r("lua", lo, hi), r("w", lo, hi))
-            if lo:
-                lo = LB
-            act(r("sa", 16 * lo, 16 * hi), ind(XG, r("lua", lo, hi)))
-        v("copy", r("sa", 16 * LS, 16 * LB), ind(XG, r("lua", LS, LB)))
+        for e, lo, hi in ACTIVE:
+            do(e, "act" if e == "s" else "copy", r("sa", 16 * lo, 16 * hi), ind(XG, r("lua", lo, hi)), *([AF.Copy] if e == "s" else []))
         v("copy", r("luz"), r("w", ZB, ZB + 256))
-        for i in range(2):
-            act(r("sz", 2048 * i, 2048 * i + 2048), ind(XG, r("luz", 128 * i, 128 * i + 128)))
+        for e, lo, hi, by in FROZEN:
+            if e == "s":
+                act(r("sz", 16 * lo, 16 * hi), ind(XG, r("luz", lo, hi)), AF.Relu, bias=r("nthr"))
+            else:
+                ts(r("sz", 16 * lo, 16 * hi), ind(XG, r("luz", lo, hi)), r("thr"), OP.is_ge)
         ts(r("dra"), r("zz", 132, 196), 1.0, OP.is_lt, 1e5, OP.mult)
-        ts(r("drb"), r("zz", 132, 196), 2.0, OP.mult, -4224.0, OP.add)
-        v("tt", r("dr"), r("dra"), r("drb"), OP.add)
-        if t == 0:
-            consts_b()
-        v("copy", r("li"), r("w", 0, 256))
-        ts(r("lo"), r("li"), 63, OP.bitwise_and)
+        v("tt", r("dr"), r("dra"), r("zz", 132, 196), OP.add)
+        ts(r("hib"), r("lua"), 1.0 / 64, OP.mult, 128.0, OP.add)
+        v("tt", r("dj"), r("w", 1, 256, 2), r("w", 0, 256, 2), OP.subtract)
 
-        def totals(lo, hi, k0, k1):
+        for h, bk in enumerate(("p0", "p2")):
+            lo, hi = 128 * h, 128 * h + 128
+            pe(r(bk, 0, 256), r("one", 0, 128), r("dg"), True, False)
+            pe(r(bk, 0, 256), r("hib", lo, hi), r("ih"), False, False)
+            pe(r(bk, 128, 256), r("w", lo, hi), r("idf"), False, False)
+            for a in (lo, lo + 64):
+                v("scan", r("mx", 16 * a, 16 * a + 1024), r("mk", 0, 1024), r("sa", 16 * a, 16 * a + 1024), 0.0, OP.min, OP.max)
             o = r("p3", lo // 2, hi // 2)
-            for k in range(k0, k1):
+            for k in range(16):
                 pe(o, r("sel", 128 * k, 128 * k + 128), r("sa", 16 * lo + 16 + k, 16 * hi, 32), k == 0, False)
                 pe(o, r("nsel", 128 * k, 128 * k + 128), r("sa", 16 * lo + k, 16 * hi, 32), False, k == 15)
-
-        def block(lo, hi, fp, filler):
-            v("scan", r("mx", 16 * lo, 16 * hi), r("mk", 16 * lo, 16 * hi), r("sa", 16 * lo, 16 * hi), 0.0, OP.mult, OP.max)
-            ts(r("fa", lo, hi), r("mx", 16 * lo + 15, 16 * hi, 16), r("thr"), OP.is_lt)
-            pe(r(fp, lo, hi), r("idm"), r("fa", lo, hi), True, True)
-            pe(r("p1", lo, hi), r("bb9"), r("fa", lo, hi), True, True)
-            pe(r("p0", lo, hi), r("dg"), r("one", lo, hi), True, False)
-            filler()
-            for k in range(16):
-                m = r("sm", 256 * k + lo, 256 * k + hi)
-                v("tt", m, r("sa", 16 * lo + k, 16 * hi, 16), r(fp, lo, hi), OP.mult)
-                pe(r("p0", lo, hi), r("sel", 128 * k, 128 * k + 128), m, False, k == 15)
-                if k == 3:
-                    ts(r("vi", lo, hi), r("p1", lo, hi), -40.0, OP.is_lt, 256.0, OP.mult)
-                    pe(r("p0", lo, hi), r("id"), r("vi", lo, hi), False, False)
-        totals(0, LB, 0, 8)
-        block(0, LB, "p2", lambda: v("tt", r("dj"), r("w", 1, 256, 2), r("w", 0, 256, 2), OP.subtract))
-        totals(0, LB, 8, 13)
-        block(LB, 256, "p7", lambda: ts(r("hi"), r("li"), 6, OP.arith_shift_right))
-        act(r("rw", 0, 256), r("p1", 0, 256), AF.Relu, bias=kx(20), scale=-1.0)
-        totals(0, LB, 13, 16)
-        totals(LB, 256, 0, 16)
-        v("tt", r("ab", 0, 256), r("p0", 0, 256), r("hi"), OP.add)
-        v("tt", r("ab", 256, 512), r("p0", 0, 256), r("lo"), OP.add)
-        v("vt", r("at"), r("ab"))
-        v("scan", r("scn"), r("mk", 0, 512), r("at"), 0.0, OP.mult, OP.max)
-        for d in range(2):
-            v("copy", r("di", d, 32, 2), r("scn", 256 * d + 15, 256 * d + 256, 16))
-        for f in range(7):
-            ts(r3("fti", slice(None), f, f, 256, 8), r("di"), f if f < 6 else 8, OP.arith_shift_right, 1, OP.bitwise_and)
-        ts(r("ddi", 0, 32), r("di"), 127, OP.bitwise_and)
-        ts(r("ddi", 32, 48), r("di", 1, 32, 2), 8, OP.arith_shift_right, 1, OP.bitwise_and)
-        ts(r3("ftb", slice(None), slice(0, 7)), r3("fti", slice(None), slice(0, 7)), 2.0, OP.mult, -1.0, OP.add)
-        v("copy", r("db"), r("ddi"))
-        v("vt", r3("fe", slice(None)), r3("ftb", slice(None)))
-        for gr in range(8):
-            o = r3("bd", slice(None), slice(16 * gr, 16 * gr + 16), 16 * gr, 16 * gr + 16)
-            if gr in BDS:
-                act(o, r3("fe", slice(None)), AF.Identity, bias=r("cbm", gr, gr + 1), scale=r("mb", gr, gr + 1))
-            else:
-                ts(o, r3("fe", slice(None)), r("mb", gr, gr + 1), OP.mult, r("cbm", gr, gr + 1), OP.add)
-
-        def qmat(a2, g2, m):
-            i = (a2 * 2 + g2) * 256 + 128 * m
-            return r("qm", i, i + 128)
-        for a2 in range(2):
-            pe(r("p4", a2, 16, 2), qmat(a2, 0, 1), r("db", 0, 32, 4), True, False)
-            pe(r("p4", a2, 16, 2), qmat(a2, 1, 1), r("db", 2, 32, 4), False, False)
-            pe(r("p4", a2, 16, 2), qmat(a2, 0, 0), r("db", 1, 32, 4), False, False)
-            pe(r("p4", a2, 16, 2), qmat(a2, 1, 0), r("db", 3, 32, 4), False, True)
-            pe(r("p4", 16 + a2, 32, 2), qmat(a2, 0, 0), r("db", 32, 48, 2), True, False)
-            pe(r("p4", 16 + a2, 32, 2), qmat(a2, 1, 0), r("db", 33, 48, 2), False, True)
-        ts(r("p3", 128, 256), r("p3", 0, 128), 0.0, OP.is_gt)
-        v("tt", r("p3", 256, 384), r("dj"), r("p3", 128, 256), OP.mult)
-        v("tt", r("jt"), r("p3", 256, 384), r("w", 0, 256, 2), OP.add)
-        v("copy", r("cu"), r("p4", 0, 16))
+        ts(r("fa"), r("mx", 15, 4096, 16), r("thr"), OP.is_lt, -1.0, OP.mult)
+        pe(r("p1", 0, 256), r("bb9"), r("fa"), True, True)
+        for k in range(16):
+            v("scan", r("sm", 256 * k, 256 * k + 256), r("sa", k, 4096, 16), r("fa"), 0.0, OP.max, OP.mult)
+            for h, bk in enumerate(("p0", "p2")):
+                if k == 15:
+                    pe(r(bk, 0, 128), r("vn", 128 * h, 128 * h + 128), r("idv"), False, False)
+                pe(r(bk, k, 256, 16), r("sm", 256 * k + 128 * h, 256 * k + 128 * h + 128), r("g2"), False, k == 15)
+            if k == 1:
+                ts(r("vn"), r("p1", 0, 256), 40.0, OP.is_gt, -1.0, OP.mult)
+        for h, bk in enumerate(("p0", "p2")):
+            v("scan", r("scn", 256 * h, 256 * h + 256), r("mkb"), r(bk, 0, 256), 0.0, OP.min, OP.max)
+        act(r("rw", 0, 256), r("p1", 0, 256), AF.Relu, bias=kx(20))
+        al = slice(None)
+        ts(r("di"), r("scn", 15, 512, 16), 32.0, OP.add)
+        ts(r3("dd", al, al, 0, 32, 32), r("di"), 511, OP.bitwise_and)
+        ts(r3("df", slice(0, 2), al, 0, 16, 16), r3("dd", al, slice(0, 8), 0, 32, 16), 64.0, OP.mult)
+        ts(r3("df", slice(2, 4), al, 16, 32, 16), r3("dd", al, slice(8, 16), 0, 32, 16), -32.0, OP.add)
+        pw = r3("p4", slice(0, 2), al, 0, 128, 128)
+        pe(pw, r("id"), r("ramp"), True, False)
+        for c in range(2):
+            for a in range(8):
+                pe(r3("p4", slice(0, 2), slice(8 * a, 8 * a + 8), 0, 128, 16), r("ea", 128 * a, 128 * a + 128),
+                   r3("df", slice(2 * c, 2 * c + 2), al, 16 * c, 16 * c + 16, 16), False, c == 1 and a == 7)
+        for h in range(2):
+            v("scan", r("hs", 64 * h, 64 * h + 64), r("pat", 0, 64), r3("p4", h, al, 64 * h, 64 * h + 64, 64), 0.0, OP.add, OP.min)
+        ch = r("hs", 7, 128, 8)
+        ts(r("g1"), ch, 2048.0, OP.is_ge, -4096.0, OP.mult)
+        v("tt", r("key"), ch, r("g1"), OP.add)
+        ts(r("cu"), ch, 2048.0, OP.add)
+        v("tt", r("cm"), r("key"), r("g1"), OP.add)
         act(r("sch"), ind(XG, r("cu")))
-        at = {}
-        for e, b, aa in DED:
-            o = 32 if b == 4 else 0
-            for a in aa:
-                at[a] = r("p%d" % b, o, o + 16 * (a + 1))
-                o += 16 * (a + 1)
-
-        def equal(banks):
-            for e, b, aa in banks:
-                for a in aa:
-                    pe(at[a], r3("bd", a), r3("fe", slice(0, a + 1)), True, True)
-        equal(DED[:2])
-        v("tt", r("p5", 0, 128), r("vi", 0, 256, 2), r("vi", 1, 256, 2), OP.min)
-        v("scan", r("ce", 1, 128), r("one", 0, 127), r("p5", 0, 127), 0.0, OP.mult, OP.add)
-        v("tt", r("p5", 128, 256), r("p5", 0, 128), r("nc"), OP.mult)
-        v("tt", r("o32"), r("p5", 128, 256), r("ce"), OP.add)
-        pe(r("p6", 0, 8), r("id"), r("jc8"), True, False)
-        for q in range(16):
-            pe(r("p6", 0, 8), r("sel", 128 * q, 128 * q + 128), r("o32", q, 128, 16), False, q == 15)
-        ts(r("cc", 0, 16), r("p4", 0, 16), 512.0, OP.add)
-        ts(r("ge"), r("p4", 0, 16), 4096.0, OP.is_lt, 8192.0, OP.mult)
-        ts(r("cm"), r("p4", 0, 16), -3584.0, OP.add)
-        v("tt", r("tg0"), r("tg1"), r("p4", 16, 32), OP.mult)
-        v("tt", r("cc", 16, 32), r("ge"), r("cm"), OP.add)
-        ts(r("tg"), r("tg0"), -1.0, OP.add)
-        equal(DED[2:4])
-        pe(r("p5", 256, 512), r("id8"), r("fa"), True, False)
-        pe(r("p5", 256, 512), r("id"), r("sch"), False, True)
-        equal(DED[4:])
-
-        def send():
-            ts(r("jo"), r("p6", 0, 8), 1.0 / 4096, OP.mult)
-            v("copy", ind(r("jw", 256 * t, 256 * t + 256), r("jo")), r("jt"))
-            rid, pid, _ = topo.addr(dst)
-            o, i, a, l, m = T.q_jl[:, 128 * t:128 * t + 128], T.q_jw[:, 256 * t:256 * t + 128], "a%d" % t, "l%d" % t, topo.mask(core, dst)
-            ne = len(topo.engines(T.cores[(rank - 1 - t % 3) % len(T.cores)], core))
-            ro, wo = ("jw", 256 * t, 256 * t + 128, 1, False), ("jl", 128 * t, 128 * t + 128, 1, True)
-
-            def issue():
-                deps("g", [ro])
-                g.remote_dma(o, i, T.sem[a], T.sem[l], pid, rid, m)
-                note(a, ne, [wo])
-            ops.append(("g", [ro, wo], 1.0, 3.0, issue))
-
-        def frozen(i):
-            v("scan", r("mz", 2048 * i, 2048 * i + 2048), r("mk", 0, 2048), r("sz", 2048 * i, 2048 * i + 2048), 0.0, OP.mult, OP.max)
-            ts(r("fz", 128 * i, 128 * i + 128), r("mz", 2048 * i + 15, 2048 * i + 2048, 16), r("thr"), OP.is_lt)
-            if i:
-                pe(r("p1", 256, 512), r("bb9"), r("fz"), True, True)
-
-        def frozen_codes():
-            act(r("rw", ZB, ZB + 256), r("p1", 256, 512), AF.Relu, bias=kx(20), scale=-1.0)
-            act(r("rg"), ind(r("rw"), POS))
-            if not last:
-                act(r("junk", 2176, 2432), r("vi"), AF.Copy, accum_out=r("vs"))
-
-        def lowest():
-            for e, b, aa in DED:
-                for a in aa:
-                    if e == "v":
-                        v("red", r("win", a, a + 1), at[a], AxisListType.X, OP.max)
-                    else:
-                        act(r("junk", 8 * a * (a + 1), 8 * (a + 1) * (a + 2)), at[a], AF.Relu, bias=r("bias", a, a + 1), accum_out=r("win", a, a + 1))
-            act(r("nv", 256, 512), r("p5", 256, 512), AF.Relu, bias=kx(21), scale=-1.0)
-            act(r("nv", 0, 256), r("nv", 256, 512), AF.Identity, bias=kx(21), scale=-1.0)
-
-        def arrivals():
-            jl = r("jl", 128 * t, 128 * t + 128)
-            act(r("junk", 2432, 2560), jl, AF.Sign, bias=kx(22), accum_out=r("ns"))
-            ts(r("p5", 0, 128), jl, -0.5, OP.is_gt, -16384.0, OP.mult)
-            v("tt", r("p5", 128, 256), r("w", DB0, DB0 + 128), r("p5", 0, 128), OP.add)
-            v("tt", r("w", DB0, DB0 + 128), r("p5", 128, 256), jl, OP.max)
-            ts(r("nt"), r("dr"), r("ns"), OP.is_ge)
-
-        def moves():
-            v("tt", r("wm", 0, 16), r("win"), r("tg"), OP.is_equal)
-            v("tt", r("wm", 16, 32), r("win"), r("tg"), OP.is_equal)
-            v("tt", r("of1"), r("cc"), r("wm"), OP.mult)
-            v("tt", r("of2"), r("of1"), r("tr"), OP.max)
-            v("copy", r("off"), r("of2"))
-            v("copy", ind(r("xt"), r("off")), r("nv"))
-        frozen(0)
-        frozen(1)
-        send()
-        lowest()
-        frozen_codes()
-        moves()
+        pe(r("p0", 256, 512), r("id8"), r("fa"), True, False)
+        pe(r("p0", 256, 512), r("id"), r("sch"), False, True)
+        nv1, nv2 = r3("nv", al, slice(0, 16), 0, 512, 256), r3("nv", al, slice(16, 32), 0, 512, 256)
+        act(nv2, r("p0", 256, 512), AF.Relu, bias=kx(21), scale=-1.0)
+        act(nv1, nv2, AF.Identity, bias=kx(21), scale=-1.0)
+        pe(r("p5", 0, 256), r("id"), r("dcon"), True, False)
+        for d in range(1, 16):
+            pe(r("p5", d, 256, 16), r("sd", 128 * d - 128, 128 * d), r("key"), False, d == 15)
+        v("scan", r("pr"), r("p5", 0, 256), r("one0"), 0.0, OP.mult, OP.add)
+        ts(r("wm"), r("pr", 15, 256, 16), 0.0, OP.is_equal, -1e5, OP.mult)
+        v("tt", r("x1", 0, 16), ch, r("wm"), OP.add)
+        v("tt", r("x1", 16, 32), r("cm"), r("wm"), OP.add)
+        ts(r("off", 0, 32, 2), r("x1", 0, 16), 2048.0 + XW0, OP.add, qc, OP.max)
+        ts(r("off", 1, 32, 2), r("x1", 16, 32), 6144.0 + XW0, OP.add, kx(3), OP.max)
+        for a in range(15, -1, -1):
+            v("copy", ind(r("xt"), r("off", 2 * a, 2 * a + 2)), r3("nv", a, al, 0, 512, 32))
         if last:
             for i in range(2):
                 dma("y", T.yx[:, 2048 * i:2048 * i + 2048], r("xt", XW0 + 2048 * i, XW0 + 2048 * i + 2048))
-        arrivals()
+
+        ts(r("p3", 128, 256), r("p3", 0, 128), 0.0, OP.is_gt)
+        v("tt", r("je"), r("dj"), r("p3", 128, 256), OP.mult)
+        v("scan", r("jb"), r("vn", 0, 256, 2), r("vn", 1, 256, 2), 0.0, OP.min, OP.mult)
+        jt = r("jt", 128 * t, 128 * t + 128)
+        v("scan", jt, r("jb"), r("neg"), -128.0, OP.add, OP.add)
+        send(r("cn", 8 * t, 8 * t + 8), r("jt", 128 * t + 120, 128 * t + 128), "c%d" % t, t, 4.0)
+        v("scan", r("ju"), r("jb"), jt, 0.0, OP.max, OP.mult)
+        pe(r("p6", 0, 8), r("id"), r("jc8"), True, False)
+        for q in range(16):
+            pe(r("p6", 0, 8), r("sel", 128 * q, 128 * q + 128), r("ju", q, 128, 16), False, q == 15)
+        ts(r("jo"), r("p6", 0, 8), 1.0 / 16, OP.mult)
+        v("tt", ind(r("jw", 256 * t, 256 * t + 256), r("jo")), r("je"), r("w", 0, 256, 2), OP.add)
+        send(r("jl", 128 * t, 128 * t + 128), r("jw", 256 * t, 256 * t + 128), "a%d" % t, t, 5.0)
+
+        for e, lo, hi, by in FROZEN:
+            if by == "t":
+                for k in range(16):
+                    pe(r("p7", lo, hi), r("id"), r("sz", 16 * lo + k, 16 * hi, 16), k == 0, k == 15)
+            else:
+                v("scan", r("mz", 16 * lo, 16 * hi), r("mk", 0, 16 * (hi - lo)), r("sz", 16 * lo, 16 * hi), 0.0, OP.min, OP.max)
+        n = max([0] + [hi for e, lo, hi, by in FROZEN if by == "t"])
+        if n:
+            act(r("fz", 0, n), r("p7", 0, n), AF.Relu, bias=kx(23), scale=-1.0)
+        if n < 256:
+            ts(r("fz", n, 256), r("mz", 16 * n + 15, 4096, 16), 0.5, OP.is_lt)
+        pe(r("p1", 256, 512), r("bb9"), r("fz"), True, True)
+        act(r("rw", ZB, ZB + 256), r("p1", 256, 512), AF.Relu, bias=kx(20), scale=-1.0)
+        act(r("rg"), ind(r("rw"), POS))
+        if not last:
+            act(r("junk", 0, 256), r("vn"), AF.Copy, accum_out=r("vs"))
+
+        jl = r("jl", 128 * t, 128 * t + 128)
+        cn = r("cn", 8 * t + 7, 8 * t + 8)
+        ts(r("nt"), r("dr"), -2304.0, OP.add, cn, OP.is_ge)
+        ts(r("p7", 256, 384), r("imn"), cn, OP.is_lt, -16384.0, OP.mult)
+        v("tt", r("p7", 384, 512), r("w", DB0, DB0 + 128), r("p7", 256, 384), OP.add)
+        v("tt", r("w", DB0, DB0 + 128), r("p7", 384, 512), jl, OP.max)
 
         def clauses_back():
             if last:
@@ -597,11 +540,12 @@ def rank_program(g, core, T, topo):
         for q in range(16):
             pe(r("p6", 0, 64), r("nsel", 128 * q, 128 * q + 128), r("rg", q, 1024, 16), False, q == 15)
         if not last:
-            pe(r("p4", 300, 301), r("onf"), r("vs"), True, True)
-            rank_stage(t + 1, r("p6", 0, 64), clauses_back)
-            v("copy", r("ai", 0, 1), r("p4", 300, 301))
+            pe(r("p3", 300, 301), r("onf"), r("vs"), True, True)
+            v("copy", r("ai", 0, 1), r("p3", 300, 301))
             ts(r("ai", 1, 2), r("ai", 0, 1), 3, OP.bitwise_and)
             v("tt", r("thr"), r("ai", 1, 2), r("thf"), OP.add)
+            ts(r("nthr"), r("thr"), -1.0, OP.mult, 1.0, OP.add)
+            rank_stage(t + 1, r("p6", 0, 64), clauses_back)
     new_states(4, r("p6", 0, 64))
     pe(r("p5", 0, 128, P=64), r("fn"), r("id"), True, True)
     ts(r("fo", P=64), r("p5", 0, 128, P=64), 1.0 / 16, OP.mult)
@@ -614,4 +558,4 @@ def rank_program(g, core, T, topo):
         need("g", "d%d" % i, 16)
     for t in range(4):
         d = T.cores[(rank + 1 + t % 3) % len(T.cores)]
-        need("g", "l%d" % t, len(topo.engines(core, d)))
+        need("g", "l%d" % t, 2 * len(topo.engines(core, d)))

@@ -1,39 +1,43 @@
 from concourse.mybir import AluOpType as OP, ActivationFunctionType as AF
 
 F4, B2, H2, I4, U2 = "float32", "bfloat16", "float16", "int32", "uint16"
-XW0, XE = 32, 8240
+XW0, XE = 128, 8336
 ZB, DB0, WW = 1024, 2048, 3072
 SB = {
-    "xt": ([128, XE], B2), "ci": ([128, 1024], I4), "cb": ([128, 1024], F4), "w": ([128, WW], F4), "rw": ([128, WW], B2),
+    "xt": ([128, XE], B2), "ci": ([128, 1024], I4), "cb": ([128, 1024], F4), "w0": ([128, WW], F4), "w1": ([128, WW], F4), "rw": ([128, WW], B2),
     "thi": ([128, 1], I4), "thf": ([128, 1], F4), "thr": ([128, 1], F4), "nthr": ([128, 1], F4), "fr0": ([64, 128], I4), "frb": ([64, 128], B2),
-    "fn": ([128, 64], B2), "y": ([128, 64], B2), "fl": ([128, 198], B2), "sc": ([128, 198], F4), "zz": ([128, 198], F4),
-    "pf": ([128, 64], F4), "pos": ([128, 64], U2), "fo": ([64, 128], F4),
-    "lua": ([128, 256], U2), "luz": ([128, 256], U2), "sa": ([128, 4096], B2), "sz": ([128, 4096], B2), "mx": ([128, 4096], B2), "mz": ([128, 4096], B2),
+    "fn": ([128, 64], B2), "fl": ([128, 264], B2), "sc": ([128, 198], F4), "zz": ([128, 198], H2), "tp": ([128, 594], B2),
+    "pos": ([128, 64], U2), "fo": ([64, 128], F4),
+    "lua": ([128, 256], U2), "luz": ([128, 256], U2), "sa": ([128, 4096], B2), "sz": ([128, 4096], B2), "mx": ([128, 4096], B2),
     "fa": ([128, 256], B2), "fz": ([128, 256], B2), "sm": ([128, 4096], B2), "vn": ([128, 256], B2), "hib": ([128, 256], B2),
-    "scn": ([128, 512], F4), "di": ([128, 32], I4), "dd": ([128, 2, 16], I4), "df": ([128, 4, 8], H2), "hs": ([128, 128], F4),
-    "g1": ([128, 16], F4), "key": ([128, 16], H2), "cm": ([128, 16], F4), "cu": ([128, 16], U2), "pr": ([128, 256], F4),
-    "wm": ([128, 16], F4), "x1": ([128, 32], F4), "off": ([128, 32], U2), "sch": ([128, 256], B2), "nv": ([128, 16, 32], B2),
-    "junk": ([128, 384], B2), "dra": ([128, 64], F4), "drb": ([128, 64], F4), "dr": ([128, 64], F4), "nt": ([128, 64], F4),
-    "ns": ([128, 1], F4), "vs": ([128, 1], F4), "ai": ([128, 2], I4),
-    "dj": ([128, 128], F4), "je": ([128, 128], F4), "jb": ([128, 128], B2), "jt": ([128, 512], B2), "cn": ([128, 32], B2), "imn": ([128, 128], B2), "ju": ([128, 128], B2),
+    "scn": ([128, 2, 384], F4), "df": ([128, 4, 8], H2), "hs": ([128, 128], F4),
+    "g1": ([128, 16], F4), "key": ([128, 16], H2), "cm": ([128, 16], F4), "cu": ([128, 16], U2), "k32": ([128, 16], F4),
+    "ao": ([128, 288], B2), "ro": ([128, 288], B2), "ax": ([128, 600], B2), "rx": ([128, 600], B2),
+    "x0": ([128, 32], F4), "x1": ([128, 32], F4), "xa": ([128, 4, 8], F4), "off": ([128, 32], U2), "sch": ([128, 256], B2), "nv": ([128, 4, 128], B2),
+    "junk": ([128, 256], B2), "dra": ([128, 64], F4), "dr": ([128, 64], F4), "tk": ([128, 64], B2), "vs": ([128, 1], F4), "ai": ([128, 2], I4),
+    "jm": ([128, 128], B2), "je": ([128, 128], F4), "jb": ([128, 128], B2), "jt": ([128, 512], B2), "cn": ([128, 32], B2), "ju": ([128, 128], B2),
     "jo": ([128, 8], U2), "jw": ([128, 1024], F4), "jl": ([128, 512], F4), "rg": ([128, 1024], B2),
-    "im": ([128, 128], F4), "img": ([128, 128], F4), "imq": ([128, 128], B2), "g8r": ([128, 128], B2), "g8": ([128, 8], F4),
-    "ki": ([128, 8], I4), "kf": ([128, 8], F4), "kx": ([128, 32], F4), "gi": ([128, 8], B2), "gif": ([128, 8], F4), "g2": ([128, 16], B2),
+    "im": ([128, 128], F4), "img": ([128, 128], F4), "imq": ([128, 128], B2), "imn": ([128, 128], B2), "g8r": ([128, 128], B2), "g8": ([128, 8], F4),
+    "ki": ([128, 8], I4), "kf": ([128, 8], F4), "kx": ([128, 32], F4), "gi": ([128, 8], B2), "gif": ([128, 8], F4), "g2": ([128, 24], B2),
     "bb": ([128, 128], B2), "bb9": ([128, 128], B2), "gt": ([128, 128], B2), "lt": ([128, 128], B2), "id": ([128, 128], B2),
-    "idf": ([128, 128], F4), "ih": ([128, 256], B2), "dg": ([128, 256], B2), "idv": ([128, 128], B2), "id8": ([128, 128], B2),
-    "nid": ([128, 128], B2), "sd": ([128, 1920], B2), "qm": ([128, 128], B2), "ea": ([128, 1024], B2), "ramp": ([128, 128], B2),
-    "rp0": ([128, 128], B2), "pat": ([128, 128], B2), "dcon": ([128, 256], B2), "one0": ([128, 256], B2), "mkb": ([128, 256], B2),
-    "sel": ([128, 2048], B2), "nsel": ([128, 2048], B2), "jc0": ([128, 8], F4), "jc8": ([128, 8], B2), "mk": ([128, 2048], B2),
-    "mk3": ([128, 198], B2), "one": ([128, 256], B2), "neg": ([128, 128], B2), "onf": ([128, 128], F4),
+    "idf": ([128, 128], F4), "ih": ([128, 256], B2), "dg": ([128, 384], B2), "idv": ([128, 128], B2), "id8": ([128, 128], B2),
+    "nid": ([128, 128], B2), "sd": ([128, 1920], B2), "qm": ([128, 128], B2), "ea": ([128, 2048], B2), "gi64": ([128, 8], F4), "ramp": ([128, 128], B2),
+    "rp0": ([128, 128], B2), "pat": ([128, 128], B2), "dcon": ([128, 288], B2), "po": ([128, 288], B2), "px": ([128, 600], B2),
+    "cy": ([128, 2048], B2), "bm": ([128, 384], B2), "t32": ([128, 32], F4), "t24": ([128, 24], F4), "trs": ([128, 32], F4), "i18": ([128, 288], B2),
+    "bs": ([128, 198], B2), "nbb": ([128, 128], B2), "nlt": ([128, 128], B2), "nidf": ([128, 128], F4), "idk": ([128, 128], B2), "mkb": ([128, 384], B2),
+    "sel": ([128, 2048], B2), "nsel": ([128, 2048], B2), "jc0": ([128, 8], F4), "jc8": ([128, 8], B2), "mk": ([128, 1024], B2),
+    "mk3": ([128, 198], B2), "one": ([128, 128], B2), "neg": ([128, 128], B2), "onf": ([128, 128], F4),
 }
 SCRATCH = {"q_" + k: ("sbuf", v[0], v[1]) for k, v in SB.items()}
 SCRATCH.update({"q_p%d" % i: ("psum", [128, 8, 64] if i == 4 else [128, 512], F4) for i in range(8)})
 NDMA = 40
 SEMAPHORES = ["ev", "es", "et", "eg"] + [x + str(t) for x in "acl" for t in range(4)] + ["d%d" % i for i in range(NDMA)]
+TESTS = ((170, -8.0, OP.is_lt), (341, -8.0, OP.is_gt), (341, 40.0, OP.is_gt))
 ACTIVE = (("s", 0, 64), ("v", 64, 128), ("s", 128, 192), ("s", 192, 256))
-FROZEN = (("s", 0, 64, "v"), ("s", 64, 128, "v"), ("s", 128, 192, "v"), ("s", 192, 256, "v"))
+FROZEN = (("s", 0, 64), ("s", 64, 128), ("s", 128, 192), ("s", 192, 256))
 
-CY, CPE, PFIX, WAKE, WAKEX, SLACK, GAMMA, SIGMA, IND, SIND = 0.0009, 0.0004, 0.04, 0.2, 0.15, 0.05, 1.3, 2.8, 0.055, 0.15
+CY, CPE, PFIX, WAKE, WAKEX, GAMMA, SIGMA, IND, SIND, RW1, RW2, PASSES, NOISE, FT = 0.0009, 0.00065, 0.0, 0.22, 0.2, 1.3, 2.8, 0.055, 0.15, 3.5, 4.0, 200, 2.0, 128
+PLAN = []
 
 
 def rank_program(g, core, T, topo):
@@ -51,8 +55,8 @@ def rank_program(g, core, T, topo):
         lo = 0 if lo is None else lo
         return (n, t[0:P, lo:hi:step] if step != 1 else t[0:P, lo:hi], lo, hi, step, -(-(hi - lo) // step))
 
-    def r3(n, a, b, lo, hi, els):
-        return (n, T["q_" + n][:, a, b], lo, hi, 1, els)
+    def r3(n, a, b, lo, hi, els, step=1):
+        return (n, T["q_" + n][:, a, b], lo, hi, step, els)
 
     def ind(w, o):
         return ("@", w, o)
@@ -76,7 +80,7 @@ def rank_program(g, core, T, topo):
         req = {}
         own = "e" + q
         for (b, lo, hi, st, w) in acc:
-            bank = b[0] == "p" and len(b) == 2
+            bank = b[0] == "p" and len(b) == 2 and b[1].isdigit()
             for (src, l2, h2, s2, w2), n in log.get(b, {}).items():
                 if src == own:
                     if not (w or w2) or (w and q == "t") or not over((lo, hi, st), (l2, h2, s2)):
@@ -131,7 +135,7 @@ def rank_program(g, core, T, topo):
         if any(a[0] == "@" for a in xs):
             return IND + n * GAMMA * CY
         if name == "tt":
-            n *= 1 if any(len(b) == 2 and b[0] == "p" for b in names) else 2
+            n *= 2 if all(b in SB for b in names) else 1
         elif name in ("copy", "ts", "scan", "set") and two:
             n *= 0.5
         return max(n, 64) * CY
@@ -189,10 +193,10 @@ def rank_program(g, core, T, topo):
             q, acc = ops[i][0], ops[i][1]
             if q == "g":
                 if gl:
-                    pre[i][gl[-1]] = 0.0
+                    pre[i][gl[-1]] = ops[gl[-1]][2] - ops[gl[-1]][3]
                 gl.append(i)
             for (b, lo, hi, st, w) in acc:
-                bank = b[0] == "p" and len(b) == 2
+                bank = b not in SB
                 hs = hist.setdefault(b, ([], []))
                 for h in (hs[0], hs[1]) if (w or bank) else (hs[0],):
                     for (j, q2, l2, h2, s2, w2) in h:
@@ -210,33 +214,49 @@ def rank_program(g, core, T, topo):
         way = [0.0] * n
         for i in range(n - 1, -1, -1):
             way[i] = ops[i][3] + max([way[j] + pre[j][i] for j in post[i]], default=0.0)
-        left = [len(p) for p in pre]
-        ready = {q: {} for q in Q}
-        free = {q: 0.0 for q in Q}
-        end = [0.0] * n
-        for i in range(n):
-            if not left[i]:
-                ready[ops[i][0]][i] = 0.0
-        done = []
-        while len(done) < n:
-            best = None
-            for q in Q:
-                if ready[q]:
-                    t0 = min(max(free[q], x) for x in ready[q].values())
-                    i = max((i for i, x in ready[q].items() if max(free[q], x) <= t0 + SLACK), key=lambda k: way[k])
-                    s0 = max(free[q], ready[q][i])
-                    if best is None or s0 < best[0]:
-                        best = (s0, q, i)
-            s0, q, i = best
-            del ready[q][i]
-            free[q] = s0 + ops[i][2]
-            end[i] = s0 + ops[i][3]
-            done.append(i)
-            for j in post[i]:
-                left[j] -= 1
-                if not left[j]:
-                    ready[ops[j][0]][j] = max(end[k] + w for k, w in pre[j].items())
-        for i in done:
+
+        def place(prio, before, after, first):
+            left = [len(p) for p in before]
+            heap = sorted((prio[i], i) for i in range(n) if not left[i])
+            busy = {q: [] for q in Q}
+            start = [0.0] * n
+            while heap:
+                i = heap.pop(0)[1]
+                t = max([start[j] + x for j, x in before[i].items()], default=first[i])
+                b, d = busy[ops[i][0]], ops[i][2]
+                k = len(b)
+                while k and b[k - 1][1] > t:
+                    k -= 1
+                while k < len(b) and b[k][0] < t + d:
+                    t = max(t, b[k][1])
+                    k += 1
+                b.insert(k, (t, t + d))
+                start[i] = t
+                for j in after[i]:
+                    left[j] -= 1
+                    if not left[j]:
+                        k = len(heap)
+                        while k and heap[k - 1] > (prio[j], j):
+                            k -= 1
+                        heap.insert(k, (prio[j], j))
+            return start
+        fw = [{j: ops[j][3] + x for j, x in pre[i].items()} for i in range(n)]
+        bw = [{j: ops[i][3] - ops[i][2] + ops[j][2] + pre[j][i] for j in post[i]} for i in range(n)]
+        prio, best, x = [-y for y in way], None, 1
+        for p in range(0 if PLAN else PASSES):
+            start = place(prio, fw, post, [0.0] * n)
+            end = max(start[i] + ops[i][3] for i in range(n))
+            if best is None or end < best[0]:
+                best = (end, start)
+            key = []
+            for i in range(n):
+                x = x * 16807 % 2147483647
+                key.append(-(best[1][i] + ops[i][2]) + (NOISE * x / 2147483647 if p > 1 else 0))
+            back = place(key, bw, pre, [o[3] - o[2] for o in ops])
+            prio = [-(back[i] + ops[i][2]) for i in range(n)]
+        if not PLAN:
+            PLAN.extend(sorted(range(n), key=lambda i: (best[1][i], i)))
+        for i in PLAN:
             ops[i][4]()
 
     def v(*a): do("v", *a)
@@ -267,19 +287,23 @@ def rank_program(g, core, T, topo):
     iota(r("img"), [[1, 8], [0, 16]], 0, 0)
     iota(r("g8"), [[1, 8]], 0, 0)
     for b, n in ((0, 256), (ZB, 256), (DB0, 128)):
-        iota(r("w", b, b + n), [[0, n]], 8192, 0)
-    iota(r("mk", 0, 1024), [[0, 64], [64, 16]], 0, 0)
+        iota(r("w0", b, b + n), [[0, n]], 8192, 0)
+    iota(r("mk"), [[0, 64], [64, 16]], 0, 0)
     iota(r("imq"), [[0, 8], [1, 16]], 0, 0)
     iota(r("g8r"), [[0, 16], [1, 8]], 0, 0)
     iota(r("jc0"), [[256, 8]], 2048, 0)
+    iota(r("t32"), [[16, 2], [0, 4], [32, 4]], 0, 0)
+    iota(r("t24"), [[0, 4], [32, 3], [16, 2]], 32, 0)
+    iota(r("i18"), [[0, 16], [1, 18]], 0, 0)
     iota(r("jw", 0, 256), [[0, 256]], -20, 0)
     kx = lambda i: r("kx", i, i + 1)
     v("set", r("fl"), 0.0)
-    v("set", r("fl", 66, 67), 64.0)
-    v("set", r("fl", 132, 133), 128.0)
+    v("set", r("bs"), 0.0)
+    v("set", r("bs", 0, 1), -2048.0)
+    v("set", r("bs", 66, 67), -1024.0)
     v("set", r("mk3"), 1.0)
     v("set", r("mk3", 0, 198, 66), 0.0)
-    for i, c in ((7, -32.0), (20, -36.0), (21, 63.0), (22, 0.5), (23, 1.0)):
+    for i, c in ((20, -36.0), (21, 63.0), (23, 1.0)):
         v("set", kx(i), c)
     ts(r("ki", 1, 2), r("ki", 0, 1), 15, OP.bitwise_and)
     ts(r("ki", 2, 3), r("ki", 0, 1), 4, OP.arith_shift_right)
@@ -289,61 +313,43 @@ def rank_program(g, core, T, topo):
     ts(r("bb"), r("img"), gc, OP.is_equal)
     ts(r("gt"), r("im"), pc, OP.is_gt)
     v("tt", r("lt"), r("gt"), r("bb"), OP.mult)
+    act(r("nbb"), r("bb"), AF.Copy, scale=-1.0)
+    act(r("nlt"), r("lt"), AF.Copy, scale=-1.0)
     act(r("nid"), r("id"), AF.Copy, scale=-1.0 / 256)
     for d in range(1, 16):
         do("g", "asel", r("sd", 128 * d - 128, 128 * d), r("nid"), [[1, 128]], OP.not_equal, 1.0 / 256, -d, -1)
     for lo, hi in ((256, ZB), (ZB + 256, WW)):
         iota(r("rw", lo, hi), [[0, hi - lo]], 1, 0)
     iota(r("jw", 256, 1024), [[0, 768]], -20, 0)
+    for b, n in ((0, 256), (ZB, 256), (DB0, 128)):
+        iota(r("w1", b, b + n), [[0, n]], 8192, 0)
 
-    def new_states(t, xw):
-        if t == 0:
-            ts(r("fn"), xw, 0.0, OP.max)
-        else:
-            ts(r("p6", 64, 128), xw, 16.0, OP.add, 0.0, OP.max)
-            v("tt", r("fn"), r("p6", 64, 128), r("nt"), OP.mult)
-
-    def rank_stage(t, xw, then=lambda: None):
-        new_states(t, xw)
-        act(r("y"), r("fn"), AF.Square, bias=kx(7))
-        then()
-
-        def flags(seg, src, thr, st, ki):
-            c0 = st // 16
-            if st == 0:
-                ts(r("fl", seg + 1, seg + 65), r(src), thr, OP.is_lt)
-                return
-            if c0 < 63:
-                ts(r("fl", seg + 2, seg + 65 - c0), r(src, c0 + 1, 64), thr, OP.is_lt)
-            ts(r("fl", seg + 65 - c0, seg + 65), r(src, 0, c0), thr, OP.is_lt)
-            ts(r("fl", seg + 1, seg + 2), r(src, c0, c0 + 1), thr, OP.is_lt, kx(ki), OP.mult)
-            ts(r("fl", seg + 65, seg + 66), r(src, c0, c0 + 1), thr, OP.is_lt, kx(ki + 1), OP.mult)
-        a0, z0 = (170 * t) % 1024, (341 * t) % 1024
-        flags(0, "fn", 8.0, a0, 8 + (t - 1) * 4)
-        ts(r("fl", 133, 197), r("fn"), 56.0, OP.is_gt)
-        flags(66, "y", 512.0, z0, 10 + (t - 1) * 4)
-        pe(r("p5", 256, 454), r("bb"), r("fl"), True, True)
-        pe(r("p5", 0, 198), r("lt"), r("fl"), True, True)
+    def rank_stage(t):
+        xw = lambda lo, hi: r("p6", lo, hi)
+        for c, (step, thr, op) in enumerate(TESTS):
+            seg, c0, o = (0, 66, 198)[c], step * t % 1024 // 16, 198 * c + 66 * (t - 1)
+            if t == 0:
+                ts(r("fl", seg + 1, seg + 65), xw(0, 64), thr, op)
+            else:
+                v("tt", r("fl", seg + 1, seg + 65 - c0), xw(c0, 64), r("tp", o + 1, o + 65 - c0), op)
+                v("tt", r("fl", seg + 65 - c0, seg + 66), xw(0, c0 + 1), r("tp", o + 65 - c0, o + 66), op)
+        ts(r("fl", 133, 197), xw(0, 64), 40.0, OP.is_gt)
+        ts(r("fn"), xw(0, 64), 16.0, OP.add, 0.0, OP.max)
+        pe(r("p5", 256, 454), r("id"), r("bs"), True, False)
+        for o, m in ((256, "bb"), (0, "lt")):
+            pe(r("p5", o, o + 198), r(m), r("fl", 0, 198), o == 0, False)
+            pe(r("p5", o + 67, o + 132), r("n" + m), r("fl", 199, 264), False, True)
         v("scan", r("sc"), r("mk3"), r("p5", 256, 454), 0.0, OP.mult, OP.add)
+        v("tt", r("fl", 67, 132), r("fl", 67, 132), r("fl", 199, 264), OP.subtract)
         v("tt", r("p6", 256, 453), r("sc", 0, 197), r("p5", 1, 198), OP.add)
         v("tt", r("zz", 0, 197), r("p6", 256, 453), r("fl", 1, 198), OP.mult)
-
-        def add(lo, hi, src, at):
-            if hi > lo:
-                v("tt", r("pf", lo, hi), r(src[0], src[1] + lo, src[1] + hi), r("zz", at, at + hi - lo), OP.add)
-
-        def merge(seg, st, src):
-            c0 = st // 16
-            if st == 0:
-                add(0, 64, src, seg)
-                return
-            add(c0 + 1, 64, src, seg + 1)
-            add(0, c0, src, seg + 64 - c0)
-            add(c0, c0 + 1, src, seg)
-            add(c0, c0 + 1, ("pf", 0), seg + 64)
-        merge(0, a0, ("zz", 132))
-        merge(66, z0, ("pf", 0))
-        v("copy", r("pos"), r("pf"))
+        parts = [(0, 64, 132)]
+        for seg, step in ((0, 170), (66, 341)):
+            c0 = step * t % 1024 // 16
+            parts += [(c0, 64, seg), (0, c0 + 1, seg + 64 - c0)] if t else [(0, 64, seg)]
+        for i, (lo, hi, at) in enumerate(parts):
+            pe(r("p6", 128 + lo, 128 + hi), r("id"), r("zz", at, at + hi - lo), i == 0, i == len(parts) - 1)
+        ts(r("pos"), r("p6", 128, 192), 2048.0, OP.add)
 
     def consts():
         v("set", r("one"), 1.0)
@@ -353,83 +359,108 @@ def rank_program(g, core, T, topo):
         act(r("id8"), r("id"), AF.Copy, scale=-8.0)
         act(r("idv"), r("id"), AF.Copy, scale=-256.0)
         act(r("idf"), r("id"))
+        act(r("nidf"), r("id"), AF.Copy, scale=-1.0)
+        act(r("idk"), r("id"), AF.Copy, scale=-160.0)
         act(r("ih", 0, 128), r("id"))
         act(r("ih", 128, 256), r("id"), AF.Copy, scale=-64.0)
-        act(r("mkb"), r("mk", 0, 256), AF.Copy, scale=float(1 << 18))
+        act(r("mkb"), r("mk", 0, 384), AF.Copy, scale=float(1 << 18))
         ts(r("gi"), r("g8"), gc, OP.is_equal)
         ts(r("gif"), r("g8"), gc, OP.is_equal)
-        for c in range(2):
+        ts(r("gi64"), r("g8"), gc, OP.is_equal, 64.0, OP.mult)
+        for c in range(3):
             ts(r("g2", 8 * c, 8 * c + 8), r("g8"), gc, OP.is_equal, -8192.0, OP.mult)
         v("set", r("sel"), 0.0)
         for q in range(16):
             act(r("sel", q * 129, q * 128 + 128, 16), r("gi"))
         for i in range(4):
             ts(r("nsel", 512 * i, 512 * i + 512), r("sel", 512 * i, 512 * i + 512), -1.0, OP.mult)
-        ts(kx(0), qc, -512.0, OP.mult, 7680.0 - 160, OP.add)
+        ts(kx(0), qc, -512.0, OP.mult, 7680.0 - 128, OP.add)
         ts(kx(1), qc, -512.0, OP.mult, 7680.0 + 8192, OP.add)
-        ts(kx(2), qc, 64.0, OP.mult)
-        ts(kx(3), qc, 16.0, OP.add)
+        ts(kx(2), qc, 8192.0, OP.mult)
+        ts(kx(3), qc, -8192.0, OP.mult)
         ts(kx(4), qc, 16.0, OP.mult)
-        for c in range(2):
-            act(r("dg", 128 * c, 128 * c + 128), r("id"), AF.Identity, scale=kx(c))
-        for t in range(1, 4):
-            for c, st in enumerate(((170 * t) % 1024, (341 * t) % 1024)):
-                ts(kx(8 + (t - 1) * 4 + 2 * c), qc, float(st % 16), OP.is_ge)
-                ts(kx(9 + (t - 1) * 4 + 2 * c), qc, float(st % 16), OP.is_lt)
+        ts(kx(5), qc, -512.0, OP.mult, 7680.0, OP.add)
+        for c in range(3):
+            act(r("dg", 128 * c, 128 * c + 128), r("id"), AF.Identity, scale=kx((0, 1, 5)[c]))
+        for c, (step, thr, op) in enumerate(TESTS):
+            v("set", r("tp", 198 * c, 198 * c + 198), thr)
+            for t in range(1, 4):
+                o, e = 198 * c + 66 * (t - 1), 8192.0 * (step * t % 16 - 0.5)
+                up, down = (kx(2), -e), (kx(3), e)
+                for col, (x, y) in ((1, down if c else up), (65, up if c else down)):
+                    ts(r("tp", o + col, o + col + 1), x, y, OP.add, thr, OP.max if c else OP.min)
+        ts(r("bm", 0, 128), r("imq"), qc, OP.is_lt, 16.0, OP.mult)
+        ts(r("bm", 128, 256), r("bb"), -100.0, OP.mult, 100.0, OP.add)
+        v("tt", r("bm", 0, 128), r("bm", 0, 128), r("bm", 128, 256), OP.add)
+        v("tt", r("bm", 256, 384), r("bm", 0, 128), r("imq"), OP.add)
+        for d in range(16):
+            ts(r("cy", 128 * d, 128 * d + 128), r("bm", 256, 384), qc, OP.subtract, float(d), OP.is_equal)
+        ts(r("trs"), r("t32"), qc, OP.add, 1.0 / 16384, OP.mult)
+        for n, k in (("po", 18), ("px", 50)):
+            v("set", r(n), 0.0)
+            v("set", r(n, 0, None, k), float(1 << 20))
+        for s in range(2):
+            v("copy", r("po", 16 + s, None, 18), r("trs", 16 * s, 16 * s + 16))
+            ts(r("px", 48 + s, None, 50), r("t24", s, 24, 2), qc, OP.add, 1.0 / 16384, OP.mult)
+        v("set", r("ax"), 1.0)
         ts(r("qm"), r("imq"), qc, OP.is_equal)
-        for a in range(8):
-            act(r("ea", 128 * a, 128 * a + 128), r("qm"), AF.Identity, scale=r("gif", a, a + 1))
+        for a in range(16):
+            act(r("ea", 128 * a, 128 * a + 128), r("qm"), AF.Identity, scale=r("gif" if a > 7 else "gi64", a % 8, a % 8 + 1))
         ts(r("rp0"), r("g8r"), gc, OP.subtract)
         ts(r("ramp"), r("rp0"), 32768.0, OP.mult, -18432.0, OP.add)
         ts(r("pat"), r("g8r"), gc, OP.is_le, float(1 << 20), OP.mult)
-        ts(r("dcon"), r("mk", 0, 256), kx(2), OP.is_gt, 128.0, OP.mult)
+        ts(r("dcon"), r("i18"), qc, OP.is_gt, 128.0, OP.mult)
+        v("set", r("dcon", 0, None, 18), 128.0)
+        for s in range(2):
+            v("set", r("dcon", 16 + s, None, 18), 1.0 / 256)
         ts(r("imn"), r("im"), -256.0, OP.add)
-        ts(r("one0"), r("mk", 0, 256), 1.0, OP.is_lt)
         ts(r("jc8"), r("jc0"), kx(4), OP.add)
         v("copy", r("thf"), r("thi"))
         v("copy", r("thr"), r("thi"))
-        ts(r("nthr"), r("thf"), -1.0, OP.mult, 1.0, OP.add)
+        act(r("nthr"), r("thf"), AF.Identity, scale=-1.0, bias=kx(23))
 
-    ts(r("frb", P=64), r("fr0", P=64), 16.0, OP.mult)
+    ts(r("frb", P=64), r("fr0", P=64), 16.0, OP.mult, -16.0, OP.add)
     pe(r("p6", 0, 64), r("frb", P=64), ("id", T.q_id[0:64, 0:64], 0, 64, 1, 64), True, True)
     v("set", r("xt", XE - 16, XE), 63.0)
     v("set", r("xt", 0, XW0), 0.0)
-    rank_stage(0, r("p6", 0, 64))
+    rank_stage(0)
     POS = r("pos")
     XG = r("xt", XW0, XE)
     for i in range(4):
         o, x = r("xt", XW0 + 4096 + 1024 * i, XW0 + 5120 + 1024 * i), r("xt", XW0 + 1024 * i, XW0 + 1024 + 1024 * i)
-        if i % 2:
+        if i == 0:
             ts(o, x, -1.0, OP.mult, 63.0, OP.add)
         else:
             act(o, x, AF.Identity, scale=-1.0, bias=kx(21))
     consts()
 
+    al = slice(None)
     for t in range(4):
-        last = t == 3
-        v("copy", ind(r("w"), POS), r("cb" if t else "ci"))
+        last, w = t == 3, "w%d" % (t % 2)
+        v("copy", ind(r(w), POS), r("cb" if t else "ci"))
         for lo, hi in ((0, 64), (64, 256)):
-            v("copy", r("lua", lo, hi), r("w", lo, hi))
+            v("copy", r("lua", lo, hi), r(w, lo, hi))
         for e, lo, hi in ACTIVE:
             do(e, "act" if e == "s" else "copy", r("sa", 16 * lo, 16 * hi), ind(XG, r("lua", lo, hi)), *([AF.Copy] if e == "s" else []))
-        v("copy", r("luz"), r("w", ZB, ZB + 256))
-        for e, lo, hi, by in FROZEN:
+        v("copy", r("luz"), r(w, ZB, ZB + 256))
+        for e, lo, hi in FROZEN:
             if e == "s":
                 act(r("sz", 16 * lo, 16 * hi), ind(XG, r("luz", lo, hi)), AF.Relu, bias=r("nthr"))
             else:
                 ts(r("sz", 16 * lo, 16 * hi), ind(XG, r("luz", lo, hi)), r("thr"), OP.is_ge)
-        ts(r("dra"), r("zz", 132, 196), 1.0, OP.is_lt, 1e5, OP.mult)
+        ts(r("dra"), r("fl", 133, 197), 0.5, OP.is_lt, 1e5, OP.mult)
         v("tt", r("dr"), r("dra"), r("zz", 132, 196), OP.add)
         ts(r("hib"), r("lua"), 1.0 / 64, OP.mult, 128.0, OP.add)
-        v("tt", r("dj"), r("w", 1, 256, 2), r("w", 0, 256, 2), OP.subtract)
+        pe(r("p3", 256, 384), r("idf"), r(w, 1, 256, 2), True, False)
+        pe(r("p3", 256, 384), r("nidf"), r(w, 0, 256, 2), False, True)
 
         for h, bk in enumerate(("p0", "p2")):
             lo, hi = 128 * h, 128 * h + 128
-            pe(r(bk, 0, 256), r("one", 0, 128), r("dg"), True, False)
+            pe(r(bk, 0, 384), r("one"), r("dg"), True, False)
             pe(r(bk, 0, 256), r("hib", lo, hi), r("ih"), False, False)
-            pe(r(bk, 128, 256), r("w", lo, hi), r("idf"), False, False)
+            pe(r(bk, 128, 256), r(w, lo, hi), r("idf"), False, False)
             for a in (lo, lo + 64):
-                v("scan", r("mx", 16 * a, 16 * a + 1024), r("mk", 0, 1024), r("sa", 16 * a, 16 * a + 1024), 0.0, OP.min, OP.max)
+                v("scan", r("mx", 16 * a, 16 * a + 1024), r("mk"), r("sa", 16 * a, 16 * a + 1024), 0.0, OP.min, OP.max)
             o = r("p3", lo // 2, hi // 2)
             for k in range(16):
                 pe(o, r("sel", 128 * k, 128 * k + 128), r("sa", 16 * lo + 16 + k, 16 * hi, 32), k == 0, False)
@@ -441,22 +472,19 @@ def rank_program(g, core, T, topo):
             for h, bk in enumerate(("p0", "p2")):
                 if k == 15:
                     pe(r(bk, 0, 128), r("vn", 128 * h, 128 * h + 128), r("idv"), False, False)
-                pe(r(bk, k, 256, 16), r("sm", 256 * k + 128 * h, 256 * k + 128 * h + 128), r("g2"), False, k == 15)
+                pe(r(bk, k, 384, 16), r("sm", 256 * k + 128 * h, 256 * k + 128 * h + 128), r("g2"), False, k == 15)
             if k == 1:
                 ts(r("vn"), r("p1", 0, 256), 40.0, OP.is_gt, -1.0, OP.mult)
         for h, bk in enumerate(("p0", "p2")):
-            v("scan", r("scn", 256 * h, 256 * h + 256), r("mkb"), r(bk, 0, 256), 0.0, OP.min, OP.max)
+            v("scan", r3("scn", h, al, 384 * h, 384 * h + 384, 384), r("mkb"), r(bk, 0, 384), 0.0, OP.min, OP.max)
         act(r("rw", 0, 256), r("p1", 0, 256), AF.Relu, bias=kx(20))
-        al = slice(None)
-        ts(r("di"), r("scn", 15, 512, 16), 32.0, OP.add)
-        ts(r3("dd", al, al, 0, 32, 32), r("di"), 511, OP.bitwise_and)
-        ts(r3("df", slice(0, 2), al, 0, 16, 16), r3("dd", al, slice(0, 8), 0, 32, 16), 64.0, OP.mult)
-        ts(r3("df", slice(2, 4), al, 16, 32, 16), r3("dd", al, slice(8, 16), 0, 32, 16), -32.0, OP.add)
-        pw = r3("p4", slice(0, 2), al, 0, 128, 128)
-        pe(pw, r("id"), r("ramp"), True, False)
+        for c in range(2):
+            v("tt", r3("df", slice(2 * c, 2 * c + 2), al, 16 * c, 16 * c + 16, 16), r3("scn", al, slice(128 * c + 15, 128 * c + 128, 16), 0, 768, 16),
+              r3("scn", al, slice(271, 384, 16), 0, 768, 16), OP.subtract)
+        pe(r3("p4", slice(0, 2), al, 0, 128, 128), r("id"), r("ramp"), True, False)
         for c in range(2):
             for a in range(8):
-                pe(r3("p4", slice(0, 2), slice(8 * a, 8 * a + 8), 0, 128, 16), r("ea", 128 * a, 128 * a + 128),
+                pe(r3("p4", slice(0, 2), slice(8 * a, 8 * a + 8), 0, 128, 16), r("ea", 1024 * c + 128 * a, 1024 * c + 128 * a + 128),
                    r3("df", slice(2 * c, 2 * c + 2), al, 16 * c, 16 * c + 16, 16), False, c == 1 and a == 7)
         for h in range(2):
             v("scan", r("hs", 64 * h, 64 * h + 64), r("pat", 0, 64), r3("p4", h, al, 64 * h, 64 * h + 64, 64), 0.0, OP.add, OP.min)
@@ -464,89 +492,100 @@ def rank_program(g, core, T, topo):
         ts(r("g1"), ch, 2048.0, OP.is_ge, -4096.0, OP.mult)
         v("tt", r("key"), ch, r("g1"), OP.add)
         ts(r("cu"), ch, 2048.0, OP.add)
-        v("tt", r("cm"), r("key"), r("g1"), OP.add)
+        v("tt", r("k32"), ch, r("g1"), OP.add)
+        v("tt", r("cm"), r("k32"), r("g1"), OP.add)
+        ts(r("x0", 0, 16), ch, 2048.0 + XW0, OP.add, 1.0 / 16384, OP.mult)
+        ts(r("x0", 16, 32), r("cm"), 6144.0 + XW0, OP.add, 1.0 / 16384, OP.mult)
+        v("tt", r("x1"), r("x0"), r("trs"), OP.max)
         act(r("sch"), ind(XG, r("cu")))
         pe(r("p0", 256, 512), r("id8"), r("fa"), True, False)
         pe(r("p0", 256, 512), r("id"), r("sch"), False, True)
-        nv1, nv2 = r3("nv", al, slice(0, 16), 0, 512, 256), r3("nv", al, slice(16, 32), 0, 512, 256)
+        nv1, nv2 = r3("nv", al, slice(0, 64), 0, 512, 256), r3("nv", al, slice(64, 128), 0, 512, 256)
         act(nv2, r("p0", 256, 512), AF.Relu, bias=kx(21), scale=-1.0)
         act(nv1, nv2, AF.Identity, bias=kx(21), scale=-1.0)
-        pe(r("p5", 0, 256), r("id"), r("dcon"), True, False)
+        for d in range(16):
+            pe(r("p2", 256 + d, 512, 16), r("cy", 128 * d, 128 * d + 128), r("key"), True, True)
+        pe(r("p5", 0, 288), r("id"), r("dcon"), True, False)
         for d in range(1, 16):
-            pe(r("p5", d, 256, 16), r("sd", 128 * d - 128, 128 * d), r("key"), False, d == 15)
-        v("scan", r("pr"), r("p5", 0, 256), r("one0"), 0.0, OP.mult, OP.add)
-        ts(r("wm"), r("pr", 15, 256, 16), 0.0, OP.is_equal, -1e5, OP.mult)
-        v("tt", r("x1", 0, 16), ch, r("wm"), OP.add)
-        v("tt", r("x1", 16, 32), r("cm"), r("wm"), OP.add)
-        ts(r("off", 0, 32, 2), r("x1", 0, 16), 2048.0 + XW0, OP.add, qc, OP.max)
-        ts(r("off", 1, 32, 2), r("x1", 16, 32), 6144.0 + XW0, OP.add, kx(3), OP.max)
-        for a in range(15, -1, -1):
-            v("copy", ind(r("xt"), r("off", 2 * a, 2 * a + 2)), r3("nv", a, al, 0, 512, 32))
+            pe(r("p5", d, 288, 18), r("sd", 128 * d - 128, 128 * d), r("key"), False, d == 15)
+        act(r("ao"), r("p5", 0, 288), AF.Abs, scale=256.0)
+        for a in range(16):
+            c, j = a // 4, a % 4
+            if j:
+                o = 50 * (3 * c + j - 1)
+                act(r("ax", o, o + 16 * j), r("p2", 256 + 64 * c, 256 + 16 * a), AF.Abs, scale=-1.0, bias=r("k32", a, a + 1))
+        v("scan", r("ro"), r("po"), r("ao"), 0.0, OP.max, OP.min)
+        v("scan", r("rx"), r("px"), r("ax"), 0.0, OP.max, OP.min)
+        for s in range(2):
+            v("tt", r3("xa", al, slice(4 * s, 4 * s + 4), 16 * s, 16 * s + 16, 16), r("x1", 16 * s, 16 * s + 16), r("ro", 16 + s, None, 18), OP.min)
+        for s in range(2):
+            x = r3("xa", al, slice(4 * s + 1, 4 * s + 4), 16 * s, 16 * s + 16, 12)
+            v("tt", x, x, r("rx", 48 + s, None, 50), OP.min)
+        ts(r("off"), r3("xa", al, al, 0, 32, 32), 16384.0, OP.mult)
+        for c in range(3, -1, -1):
+            v("copy", ind(r("xt"), r("off", 8 * c, 8 * c + 8)), r3("nv", c, al, 0, 512, 128))
         if last:
             for i in range(2):
                 dma("y", T.yx[:, 2048 * i:2048 * i + 2048], r("xt", XW0 + 2048 * i, XW0 + 2048 * i + 2048))
 
-        ts(r("p3", 128, 256), r("p3", 0, 128), 0.0, OP.is_gt)
-        v("tt", r("je"), r("dj"), r("p3", 128, 256), OP.mult)
+        ts(r("jm"), r("p3", 0, 128), 0.0, OP.is_gt)
+        v("tt", r("je"), r("p3", 256, 384), r("jm"), OP.mult)
         v("scan", r("jb"), r("vn", 0, 256, 2), r("vn", 1, 256, 2), 0.0, OP.min, OP.mult)
         jt = r("jt", 128 * t, 128 * t + 128)
         v("scan", jt, r("jb"), r("neg"), -128.0, OP.add, OP.add)
-        send(r("cn", 8 * t, 8 * t + 8), r("jt", 128 * t + 120, 128 * t + 128), "c%d" % t, t, 4.0)
+        send(r("cn", 8 * t, 8 * t + 8), r("jt", 128 * t + 120, 128 * t + 128), "c%d" % t, t, RW1)
         v("scan", r("ju"), r("jb"), jt, 0.0, OP.max, OP.mult)
         pe(r("p6", 0, 8), r("id"), r("jc8"), True, False)
         for q in range(16):
             pe(r("p6", 0, 8), r("sel", 128 * q, 128 * q + 128), r("ju", q, 128, 16), False, q == 15)
         ts(r("jo"), r("p6", 0, 8), 1.0 / 16, OP.mult)
-        v("tt", ind(r("jw", 256 * t, 256 * t + 256), r("jo")), r("je"), r("w", 0, 256, 2), OP.add)
-        send(r("jl", 128 * t, 128 * t + 128), r("jw", 256 * t, 256 * t + 128), "a%d" % t, t, 5.0)
+        v("tt", ind(r("jw", 256 * t, 256 * t + 256), r("jo")), r("je"), r(w, 0, 256, 2), OP.add)
+        send(r("jl", 128 * t, 128 * t + 128), r("jw", 256 * t, 256 * t + 128), "a%d" % t, t, RW2)
 
-        for e, lo, hi, by in FROZEN:
-            if by == "t":
+        for e, lo, hi in FROZEN:
+            if lo < FT:
                 for k in range(16):
                     pe(r("p7", lo, hi), r("id"), r("sz", 16 * lo + k, 16 * hi, 16), k == 0, k == 15)
             else:
-                v("scan", r("mz", 16 * lo, 16 * hi), r("mk", 0, 16 * (hi - lo)), r("sz", 16 * lo, 16 * hi), 0.0, OP.min, OP.max)
-        n = max([0] + [hi for e, lo, hi, by in FROZEN if by == "t"])
-        if n:
-            act(r("fz", 0, n), r("p7", 0, n), AF.Relu, bias=kx(23), scale=-1.0)
-        if n < 256:
-            ts(r("fz", n, 256), r("mz", 16 * n + 15, 4096, 16), 0.5, OP.is_lt)
+                v("scan", r("mx", 16 * lo, 16 * hi), r("mk", 0, 16 * (hi - lo)), r("sz", 16 * lo, 16 * hi), 0.0, OP.min, OP.max)
+        if FT:
+            act(r("fz", 0, FT), r("p7", 0, FT), AF.Relu, bias=kx(23), scale=-1.0)
+        if FT < 256:
+            ts(r("fz", FT, 256), r("mx", 16 * FT + 15, 4096, 16), 0.5, OP.is_lt)
         pe(r("p1", 256, 512), r("bb9"), r("fz"), True, True)
         act(r("rw", ZB, ZB + 256), r("p1", 256, 512), AF.Relu, bias=kx(20), scale=-1.0)
         act(r("rg"), ind(r("rw"), POS))
         if not last:
-            act(r("junk", 0, 256), r("vn"), AF.Copy, accum_out=r("vs"))
+            act(r("junk"), r("vn"), AF.Copy, accum_out=r("vs"))
 
         jl = r("jl", 128 * t, 128 * t + 128)
         cn = r("cn", 8 * t + 7, 8 * t + 8)
-        ts(r("nt"), r("dr"), -2304.0, OP.add, cn, OP.is_ge)
+        ts(r("tk"), r("dr"), -256.0, OP.add, cn, OP.is_lt)
         ts(r("p7", 256, 384), r("imn"), cn, OP.is_lt, -16384.0, OP.mult)
-        v("tt", r("p7", 384, 512), r("w", DB0, DB0 + 128), r("p7", 256, 384), OP.add)
-        v("tt", r("w", DB0, DB0 + 128), r("p7", 384, 512), jl, OP.max)
+        v("tt", r("p7", 384, 512), r(w, DB0, DB0 + 128), r("p7", 256, 384), OP.add)
+        v("tt", r(w, DB0, DB0 + 128), r("p7", 384, 512), jl, OP.max)
 
-        def clauses_back():
-            if last:
-                act(r("cb", 0, 512), ind(r("w"), r("pos", 0, 32)))
-                v("copy", r("cb", 512, 1024), ind(r("w"), r("pos", 32, 64)))
-                dma("s", T.yc[:, 0:512], r("cb", 0, 512))
-                dma("y", T.yc[:, 512:1024], r("cb", 512, 1024))
-                return
-            act(r("cb"), ind(r("w"), POS))
-            for b in (0, ZB):
-                act(r("w", b, b + 256), r("one"), AF.Copy, scale=8192.0)
         if last:
-            clauses_back()
+            act(r("cb", 0, 512), ind(r(w), r("pos", 0, 32)))
+            v("copy", r("cb", 512, 1024), ind(r(w), r("pos", 32, 64)))
+            dma("s", T.yc[:, 0:512], r("cb", 0, 512))
+            dma("y", T.yc[:, 512:1024], r("cb", 512, 1024))
         pe(r("p6", 0, 64), r("id"), r("fn"), True, False)
+        pe(r("p6", 0, 64), r("idk"), r("tk"), False, False)
         for q in range(16):
             pe(r("p6", 0, 64), r("nsel", 128 * q, 128 * q + 128), r("rg", q, 1024, 16), False, q == 15)
         if not last:
-            pe(r("p3", 300, 301), r("onf"), r("vs"), True, True)
-            v("copy", r("ai", 0, 1), r("p3", 300, 301))
+            pe(r("p3", 400, 401), r("onf"), r("vs"), True, True)
+            v("copy", r("ai", 0, 1), r("p3", 400, 401))
             ts(r("ai", 1, 2), r("ai", 0, 1), 3, OP.bitwise_and)
             v("tt", r("thr"), r("ai", 1, 2), r("thf"), OP.add)
-            ts(r("nthr"), r("thr"), -1.0, OP.mult, 1.0, OP.add)
-            rank_stage(t + 1, r("p6", 0, 64), clauses_back)
-    new_states(4, r("p6", 0, 64))
+            act(r("nthr"), r("thr"), AF.Identity, scale=-1.0, bias=kx(23))
+            act(r("cb"), ind(r(w), POS))
+            if t < 2:
+                for b in (0, ZB):
+                    iota(r(w, b, b + 256), [[0, 256]], 8192, 0)
+            rank_stage(t + 1)
+    ts(r("fn"), r("p6", 0, 64), 16.0, OP.add, 0.0, OP.max)
     pe(r("p5", 0, 128, P=64), r("fn"), r("id"), True, True)
     ts(r("fo", P=64), r("p5", 0, 128, P=64), 1.0 / 16, OP.mult)
     for gr in range(8):

@@ -2,41 +2,45 @@ from concourse.mybir import AluOpType as OP, ActivationFunctionType as AF
 
 F4, B2, H2, I4, U2 = "float32", "bfloat16", "float16", "int32", "uint16"
 XW0, XE = 128, 8336
-ZB, DB0, WW = 1024, 2048, 3072
+IZ, ID, IW = 1040, 2080, 3328
+CE, CW = 2064, 2192
+M = ([128, 128], B2)
 SB = {
-    "xt": ([128, XE], B2), "ci": ([128, 1024], I4), "cb": ([128, 1024], F4), "w0": ([128, WW], F4), "w1": ([128, WW], F4), "rw": ([128, WW], B2),
+    "xt": ([128, XE], B2), "ci": ([128, CE], I4), "ct": ([128, CW], F4), "fn": ([128, 64], B2), "fo": ([64, 128], F4),
     "thi": ([128, 1], I4), "thf": ([128, 1], F4), "thr": ([128, 1], F4), "nthr": ([128, 1], F4), "fr0": ([64, 128], I4), "frb": ([64, 128], B2),
-    "fn": ([128, 64], B2), "fl": ([128, 264], B2), "sc": ([128, 198], F4), "zz": ([128, 198], H2), "tp": ([128, 594], B2),
-    "pos": ([128, 64], U2), "fo": ([64, 128], F4),
-    "lua": ([128, 256], U2), "luz": ([128, 256], U2), "sa": ([128, 4096], B2), "sz": ([128, 4096], B2), "mx": ([128, 4096], B2),
+    "fl": ([128, 264], B2), "sc": ([128, 208], H2), "ve": ([128, 208], H2), "sv": ([128, 208], B2), "mo": ([128, 14], U2),
+    "iw0": ([128, IW], B2), "iw1": ([128, IW], B2), "fs": ([128, 640], B2), "bt": ([128, 640], B2), "sl": ([128, 32], U2),
+    "th2": ([128, 198], F4), "i0": ([128, 132], B2), "il": ([128, 132], B2), "ev": ([128, 144], B2), "eo": ([128, 10], U2), "dp": ([128, 8], F4),
+    "lua": ([128, 256], U2), "luz": ([128, 256], U2), "lf": ([128, 256], F4), "sa": ([128, 4096], B2), "sz": ([128, 4096], B2), "mx": ([128, 4096], B2),
     "fa": ([128, 256], B2), "fz": ([128, 256], B2), "sm": ([128, 4096], B2), "vn": ([128, 256], B2), "hib": ([128, 256], B2),
     "scn": ([128, 2, 384], F4), "df": ([128, 4, 8], H2), "hs": ([128, 128], F4),
     "g1": ([128, 16], F4), "key": ([128, 16], H2), "cm": ([128, 16], F4), "cu": ([128, 16], U2), "k32": ([128, 16], F4),
-    "ao": ([128, 288], B2), "ro": ([128, 288], B2), "ax": ([128, 600], B2), "rx": ([128, 600], B2),
-    "x0": ([128, 32], F4), "x1": ([128, 32], F4), "xa": ([128, 4, 8], F4), "off": ([128, 32], U2), "sch": ([128, 256], B2), "nv": ([128, 4, 128], B2),
-    "junk": ([128, 256], B2), "dra": ([128, 64], F4), "dr": ([128, 64], F4), "tk": ([128, 64], B2), "vs": ([128, 1], F4), "ai": ([128, 2], I4),
-    "jm": ([128, 128], B2), "je": ([128, 128], F4), "jb": ([128, 128], B2), "jt": ([128, 512], B2), "cn": ([128, 32], B2), "ju": ([128, 128], B2),
-    "jo": ([128, 8], U2), "jw": ([128, 1024], F4), "jl": ([128, 512], F4), "rg": ([128, 1024], B2),
-    "im": ([128, 128], F4), "img": ([128, 128], F4), "imq": ([128, 128], B2), "imn": ([128, 128], B2), "g8r": ([128, 128], B2), "g8": ([128, 8], F4),
-    "ki": ([128, 8], I4), "kf": ([128, 8], F4), "kx": ([128, 32], F4), "gi": ([128, 8], B2), "gif": ([128, 8], F4), "g2": ([128, 24], B2),
-    "bb": ([128, 128], B2), "bb9": ([128, 128], B2), "gt": ([128, 128], B2), "lt": ([128, 128], B2), "id": ([128, 128], B2),
-    "idf": ([128, 128], F4), "ih": ([128, 256], B2), "dg": ([128, 384], B2), "idv": ([128, 128], B2), "id8": ([128, 128], B2),
-    "nid": ([128, 128], B2), "sd": ([128, 1920], B2), "qm": ([128, 128], B2), "ea": ([128, 2048], B2), "gi64": ([128, 8], F4), "ramp": ([128, 128], B2),
-    "rp0": ([128, 128], B2), "pat": ([128, 128], B2), "dcon": ([128, 288], B2), "po": ([128, 288], B2), "px": ([128, 600], B2),
-    "cy": ([128, 2048], B2), "bm": ([128, 384], B2), "t32": ([128, 32], F4), "t24": ([128, 24], F4), "trs": ([128, 32], F4), "i18": ([128, 288], B2),
-    "bs": ([128, 198], B2), "nbb": ([128, 128], B2), "nlt": ([128, 128], B2), "nidf": ([128, 128], F4), "idk": ([128, 128], B2), "mkb": ([128, 384], B2),
-    "sel": ([128, 2048], B2), "nsel": ([128, 2048], B2), "jc0": ([128, 8], F4), "jc8": ([128, 8], B2), "mk": ([128, 1024], B2),
-    "mk3": ([128, 198], B2), "one": ([128, 128], B2), "neg": ([128, 128], B2), "onf": ([128, 128], F4),
+    "ax": ([128, 1056], B2), "rx": ([128, 1056], B2), "x0": ([128, 32], F4), "x1": ([128, 32], F4), "xa": ([128, 4, 8], F4),
+    "off": ([128, 32], U2), "sch": ([128, 256], B2), "nv": ([128, 4, 128], B2), "st": ([128, 512], F4), "kl": ([128, 144], B2),
+    "junk": ([128, 256], B2), "tk": ([128, 64], B2), "vs": ([128, 1], F4), "ai": ([128, 2], I4),
+    "jm": M, "je": ([128, 128], F4), "jb": M, "jt": ([128, 512], B2), "cn": ([128, 32], B2), "ju": M,
+    "jo": ([128, 8], U2), "jw": ([128, 1024], F4), "jl": ([128, 512], F4),
+    "c4": ([128, 1], F4), "du": ([128, 8], F4), "dy": ([128, 16], F4), "do": ([128, 8], U2),
+    "im": ([128, 128], F4), "img": ([128, 128], F4), "g8": ([128, 8], F4), "ki": ([128, 8], I4), "kf": ([128, 8], F4), "kx": ([128, 32], F4),
+    "g2": ([128, 24], B2), "idf": ([128, 128], F4), "nidf": ([128, 128], F4), "onf": ([128, 128], F4), "ih": ([128, 256], B2), "dg": ([128, 384], B2),
+    "ea": ([128, 2048], B2), "cy": ([128, 2048], B2), "zr": ([128, 1024], B2), "px": ([128, 1056], B2), "i66": ([128, 264], B2),
+    "t32": ([128, 32], F4), "trs": ([128, 32], F4), "bs": ([128, 198], B2), "mk": ([128, 1024], B2), "mkb": ([128, 384], B2), "mk3": ([128, 198], B2),
+    "sel": ([128, 432], B2), "jc0": ([128, 8], F4), "jc8": ([128, 8], B2), "jn": ([128, 8], F4), "trd": ([128, 8], F4), "tp": ([128, 594], B2),
+    "svc": ([128, 832], B2), "tr0": ([128, 208], F4), "trc": ([128, 208], H2), "ij": ([128, 208], B2), "inc": ([128, 256], B2),
+    "rr": ([128, 256], B2), "ec": ([128, 9], B2),
 }
+POOL = {k: 128 * i for i, k in enumerate("bk nbk lti nlti m3 nm3 nid1 bq nbq id16 g8r bb bb9 gt lt id idv id8 ramp rp0 pat nbb nlt idk one neg".split())}
+SB["mat"] = ([128, 128 * len(POOL)], B2)
 SCRATCH = {"q_" + k: ("sbuf", v[0], v[1]) for k, v in SB.items()}
 SCRATCH.update({"q_p%d" % i: ("psum", [128, 8, 64] if i == 4 else [128, 512], F4) for i in range(8)})
 NDMA = 40
 SEMAPHORES = ["ev", "es", "et", "eg"] + [x + str(t) for x in "acl" for t in range(4)] + ["d%d" % i for i in range(NDMA)]
-TESTS = ((170, -8.0, OP.is_lt), (341, -8.0, OP.is_gt), (341, 40.0, OP.is_gt))
-ACTIVE = (("s", 0, 64), ("v", 64, 128), ("s", 128, 192), ("s", 192, 256))
+TESTS = ((170, 8.0, OP.is_lt), (341, 8.0, OP.is_gt), (341, 56.0, OP.is_gt))
+ACTIVE = (("s", 0, 48), ("v", 48, 128), ("s", 128, 192), ("s", 192, 256))
 FROZEN = (("s", 0, 64), ("s", 64, 128), ("s", 128, 192), ("s", 192, 256))
 
-CY, CPE, PFIX, WAKE, WAKEX, GAMMA, SIGMA, IND, SIND, RW1, RW2, PASSES, NOISE, FT = 0.0009, 0.00065, 0.0, 0.22, 0.2, 1.3, 2.8, 0.055, 0.15, 3.5, 4.0, 200, 2.0, 128
+CY, CPE, FIX, PFIX, WAKE, WAKEX, GAMMA, SIGMA, IND, SIND, RW1, RW2, PASSES, NOISE, DENS, GRAIN, SEED, FIRST, FT = 0.00088, 0.00046, 0.02, 0.008, 0.17, 0.17, 1.5, 2.7, 0.055, 0.15, 3.0, 3.5, 250, 3.0, 4, 8, 9, 3.0, 192
+CASES = (({}, -1.5, 0.3), ({"r": 1.5}, 1.5, 0.2), ({"c": 1.3, "i": 1.65, "o": 1.9}, 0.0, 0.15), ({"i": 0.75, "o": 0.7, "w": 1.5}, -1.0, 0.3))
 PLAN = []
 
 
@@ -50,13 +54,15 @@ def rank_program(g, core, T, topo):
     snap, log, nd = {}, {}, [0]
 
     def r(n, lo=None, hi=None, step=1, P=128):
+        if n in POOL:
+            return r("mat", POOL[n] + (lo or 0), POOL[n] + (hi or 128), step, P)
         t = T["q_" + n]
         hi = t.shape[1] if hi is None else hi
         lo = 0 if lo is None else lo
         return (n, t[0:P, lo:hi:step] if step != 1 else t[0:P, lo:hi], lo, hi, step, -(-(hi - lo) // step))
 
-    def r3(n, a, b, lo, hi, els, step=1):
-        return (n, T["q_" + n][:, a, b], lo, hi, step, els)
+    def r3(n, a, b, lo, hi, els):
+        return (n, T["q_" + n][:, a, b], lo, hi, 1, els)
 
     def ind(w, o):
         return ("@", w, o)
@@ -80,7 +86,7 @@ def rank_program(g, core, T, topo):
         req = {}
         own = "e" + q
         for (b, lo, hi, st, w) in acc:
-            bank = b[0] == "p" and len(b) == 2 and b[1].isdigit()
+            bank = b not in SB
             for (src, l2, h2, s2, w2), n in log.get(b, {}).items():
                 if src == own:
                     if not (w or w2) or (w and q == "t") or not over((lo, hi, st), (l2, h2, s2)):
@@ -116,7 +122,7 @@ def rank_program(g, core, T, topo):
                 kk[k] = a
         return acc, real, kk
 
-    ops = []
+    ops, marks, later = [], [], []
 
     def cols(a):
         return 16 * a[2][5] if a[0] == "@" else a[5]
@@ -138,7 +144,7 @@ def rank_program(g, core, T, topo):
             n *= 2 if all(b in SB for b in names) else 1
         elif name in ("copy", "ts", "scan", "set") and two:
             n *= 0.5
-        return max(n, 64) * CY
+        return max(n, 64) * CY + FIX
 
     def do(q, name, *args, **kw):
         acc, real, kk = flat(args, kw)
@@ -155,7 +161,8 @@ def rank_program(g, core, T, topo):
             snap[(src, cnt[q])] = dict(know[q])
             note(src, cnt[q], acc)
         c = cost(q, name, args)
-        ops.append((q, acc, c, c, issue))
+        kind = "o" if args[0][0] == "@" else "i" if any(isinstance(a, tuple) and a[0] == "@" for a in args) else "c"
+        ops.append((q, acc, c, c, issue, kind))
 
     def dma(q, out, in_):
         acc, ap = [], []
@@ -171,7 +178,7 @@ def rank_program(g, core, T, topo):
             Q[q].dma_start(ap[0], ap[1]).then_inc(T.sem[x], 16)
             snap[(x, 16)] = dict(know[q])
             note(x, 16, acc)
-        ops.append((q, acc, 0.06, 2.0 + (acc[0][2] - acc[0][1]) / 700, issue))
+        ops.append((q, acc, 0.06, 2.0 + (acc[0][2] - acc[0][1]) / 700, issue, "d"))
 
     def send(out, in_, sem, t, way):
         dst = T.cores[(rank + 1 + t % 3) % len(T.cores)]
@@ -183,18 +190,18 @@ def rank_program(g, core, T, topo):
             deps("g", [ro])
             g.remote_dma(out[1], in_[1], T.sem[sem], T.sem["l%d" % t], pid, rid, topo.mask(core, dst))
             note(sem, ne, [wo])
-        ops.append(("g", [ro, wo], 1.0, way, issue))
+        more = FIRST if sem == "c0" else 0
+        ops.append(("g", [ro, wo], 1.0 + more, way + more, issue, "r"))
+
+    def behind(j):
+        later.append((len(ops) - 1, j))
 
     def order():
         n = len(ops)
         pre = [{} for _ in range(n)]
-        hist, gl = {}, []
+        hist = {}
         for i in range(n):
             q, acc = ops[i][0], ops[i][1]
-            if q == "g":
-                if gl:
-                    pre[i][gl[-1]] = ops[gl[-1]][2] - ops[gl[-1]][3]
-                gl.append(i)
             for (b, lo, hi, st, w) in acc:
                 bank = b not in SB
                 hs = hist.setdefault(b, ([], []))
@@ -206,54 +213,89 @@ def rank_program(g, core, T, topo):
                             pre[i][j] = WAKE if q == q2 else WAKEX
             for (b, lo, hi, st, w) in acc:
                 hist[b][0 if w else 1].append((i, q, lo, hi, st, w))
-        post = [[] for _ in range(n)]
+        for i, j in later:
+            pre[i].setdefault(j, 0.0)
+        above = [0] * n
         for i in range(n):
             pre[i].pop(i, None)
+            seen = 0
+            for j in sorted(pre[i], reverse=True):
+                if seen >> j & 1:
+                    del pre[i][j]
+                seen |= above[j] | 1 << j
+            above[i] = seen
+        post = [[] for _ in range(n)]
+        for i in range(n):
             for j in pre[i]:
                 post[j].append(i)
-        way = [0.0] * n
-        for i in range(n - 1, -1, -1):
-            way[i] = ops[i][3] + max([way[j] + pre[j][i] for j in post[i]], default=0.0)
+        qs, dur = [o[0] for o in ops], [o[2] for o in ops]
+        fw = [[(j, ops[j][3] + x) for j, x in pre[i].items()] for i in range(n)]
+        bw = [[(j, ops[i][3] - dur[i] + dur[j] + pre[j][i]) for j in post[i]] for i in range(n)]
 
-        def place(prio, before, after, first):
-            left = [len(p) for p in before]
-            heap = sorted((prio[i], i) for i in range(n) if not left[i])
+        def place(key, before, along, first):
+            for i in along:
+                for j, _ in before[i]:
+                    if key[j] >= key[i]:
+                        key[i] = key[j] + 1e-6
             busy = {q: [] for q in Q}
             start = [0.0] * n
-            while heap:
-                i = heap.pop(0)[1]
-                t = max([start[j] + x for j, x in before[i].items()], default=first[i])
-                b, d = busy[ops[i][0]], ops[i][2]
+            for i in sorted(along, key=lambda i: key[i]):
+                t = first[i]
+                for j, x in before[i]:
+                    if start[j] + x > t:
+                        t = start[j] + x
+                b, d = busy[qs[i]], dur[i]
                 k = len(b)
                 while k and b[k - 1][1] > t:
                     k -= 1
                 while k < len(b) and b[k][0] < t + d:
-                    t = max(t, b[k][1])
+                    if b[k][1] > t:
+                        t = b[k][1]
                     k += 1
                 b.insert(k, (t, t + d))
                 start[i] = t
-                for j in after[i]:
-                    left[j] -= 1
-                    if not left[j]:
-                        k = len(heap)
-                        while k and heap[k - 1] > (prio[j], j):
-                            k -= 1
-                        heap.insert(k, (prio[j], j))
             return start
-        fw = [{j: ops[j][3] + x for j, x in pre[i].items()} for i in range(n)]
-        bw = [{j: ops[i][3] - ops[i][2] + ops[j][2] + pre[j][i] for j in post[i]} for i in range(n)]
-        prio, best, x = [-y for y in way], None, 1
+        up, down, zero, tail = range(n), range(n - 1, -1, -1), [0.0] * n, [o[3] - o[2] for o in ops]
+        way = [0.0] * n
+        for i in down:
+            way[i] = max([way[j] + x for j, x in bw[i]], default=tail[i])
+        tag, seen = [], {}
+        for i in up:
+            if i in marks:
+                seen = {}
+            k = (qs[i], ops[i][1][0][0].replace("iw1", "iw0"), i < marks[0])
+            seen[k] = seen.get(k, 0) + 1
+            tag.append(k + (seen[k] // GRAIN,))
+        cases = []
+        for factor, more, weight in CASES:
+            d = [dur[i] * factor.get(ops[i][5], 1) for i in up]
+            e = [d[i] + tail[i] + (more if ops[i][5] == "r" else 0) for i in up]
+            cases.append((d, e, [[(j, e[j] + y * factor.get("w", 1)) for j, y in pre[i].items()] for i in up], weight))
+
+        def length(line, d, e, before, weight):
+            free, start = {q: 0.0 for q in Q}, [0.0] * n
+            for i in line:
+                t = free[qs[i]]
+                for j, y in before[i]:
+                    if start[j] + y > t:
+                        t = start[j] + y
+                start[i] = t
+                free[qs[i]] = t + d[i]
+            return weight * max(start[i] + e[i] for i in up)
+        key, best, x = [-way[i] - dur[i] for i in up], None, SEED
         for p in range(0 if PLAN else PASSES):
-            start = place(prio, fw, post, [0.0] * n)
-            end = max(start[i] + ops[i][3] for i in range(n))
+            start = place(key, fw, up, zero)
+            line = sorted(up, key=lambda i: (start[i], i))
+            end = sum(length(line, *c) for c in cases)
             if best is None or end < best[0]:
                 best = (end, start)
-            key = []
-            for i in range(n):
-                x = x * 16807 % 2147483647
-                key.append(-(best[1][i] + ops[i][2]) + (NOISE * x / 2147483647 if p > 1 else 0))
-            back = place(key, bw, pre, [o[3] - o[2] for o in ops])
-            prio = [-(back[i] + ops[i][2]) for i in range(n)]
+            shake = {}
+            for k in tag:
+                if k not in shake:
+                    x = x * 16807 % 2147483647
+                    shake[k] = NOISE * (x % 1000) / 1000 if p > 1 and x % 7 < DENS else 0
+            back = place([shake[tag[i]] - best[1][i] - dur[i] for i in up], bw, down, tail)
+            key = [-back[i] - dur[i] for i in up]
         if not PLAN:
             PLAN.extend(sorted(range(n), key=lambda i: (best[1][i], i)))
         for i in PLAN:
@@ -277,33 +319,37 @@ def rank_program(g, core, T, topo):
 
     for gr in range(8):
         dma("y" if gr % 2 == 0 else "s", r("fr0", 16 * gr, 16 * gr + 16, P=64), T.fr[gr:gr + 1, :])
-    dma("s", r("ci"), T.cl[:, :])
-    for i in range(2):
-        dma("y", r("xt", XW0 + 2048 * i, XW0 + 2048 * i + 2048), T.xv[:, 2048 * i:2048 * i + 2048])
+    dma("s", r("ci", 0, 1024), T.cl[:, :])
+    for i in range(4):
+        dma("y", r("xt", XW0 + 1024 * i, XW0 + 1024 * i + 1024), T.xv[:, 1024 * i:1024 * i + 1024])
     dma("s", r("thi"), T.th[:, :])
 
     iota(r("ki", 0, 1), [[1, 1]], 0, 1)
     iota(r("im"), [[1, 128]], 0, 0)
     iota(r("img"), [[1, 8], [0, 16]], 0, 0)
     iota(r("g8"), [[1, 8]], 0, 0)
-    for b, n in ((0, 256), (ZB, 256), (DB0, 128)):
-        iota(r("w0", b, b + n), [[0, n]], 8192, 0)
+    for w in ("iw0", "iw1"):
+        for b, n in ((0, 256), (IZ, 256), (ID, 128)):
+            iota(r(w, b, b + n), [[0, n]], 16384, 0)
+    iota(r("tr0"), [[1, 208]], 1072, 0)
+    iota(r("ij", 0, 198), [[0, 3], [16, 66]], -16, 0)
+    iota(r("rr"), [[-1, 256]], 256, 0)
     iota(r("mk"), [[0, 64], [64, 16]], 0, 0)
-    iota(r("imq"), [[0, 8], [1, 16]], 0, 0)
     iota(r("g8r"), [[0, 16], [1, 8]], 0, 0)
     iota(r("jc0"), [[256, 8]], 2048, 0)
     iota(r("t32"), [[16, 2], [0, 4], [32, 4]], 0, 0)
-    iota(r("t24"), [[0, 4], [32, 3], [16, 2]], 32, 0)
-    iota(r("i18"), [[0, 16], [1, 18]], 0, 0)
+    iota(r("i66"), [[0, 4], [-1, 66]], 16, 0)
     iota(r("jw", 0, 256), [[0, 256]], -20, 0)
     kx = lambda i: r("kx", i, i + 1)
     v("set", r("fl"), 0.0)
     v("set", r("bs"), 0.0)
     v("set", r("bs", 0, 1), -2048.0)
-    v("set", r("bs", 66, 67), -1024.0)
+    v("set", r("bs", 66, 67), IZ - 2048.0)
+    v("set", r("bs", 132, 133), ID - 2048.0)
     v("set", r("mk3"), 1.0)
     v("set", r("mk3", 0, 198, 66), 0.0)
-    for i, c in ((20, -36.0), (21, 63.0), (23, 1.0)):
+    for i, c in ((21, 63.0), (23, 1.0), (24, -2048 - 4.5 / 32), (25, IZ - 2048 - 4.5 / 32), (26, ID - 2048.0), (27, 256 - 2048.0),
+                 (28, 256 + IZ - 2048.0), (22, 128.0), (29, (2048.0 + XW0) / 16384), (30, (6144.0 + XW0) / 16384)):
         v("set", kx(i), c)
     ts(r("ki", 1, 2), r("ki", 0, 1), 15, OP.bitwise_and)
     ts(r("ki", 2, 3), r("ki", 0, 1), 4, OP.arith_shift_right)
@@ -315,17 +361,53 @@ def rank_program(g, core, T, topo):
     v("tt", r("lt"), r("gt"), r("bb"), OP.mult)
     act(r("nbb"), r("bb"), AF.Copy, scale=-1.0)
     act(r("nlt"), r("lt"), AF.Copy, scale=-1.0)
-    act(r("nid"), r("id"), AF.Copy, scale=-1.0 / 256)
-    for d in range(1, 16):
-        do("g", "asel", r("sd", 128 * d - 128, 128 * d), r("nid"), [[1, 128]], OP.not_equal, 1.0 / 256, -d, -1)
-    for lo, hi in ((256, ZB), (ZB + 256, WW)):
-        iota(r("rw", lo, hi), [[0, hi - lo]], 1, 0)
     iota(r("jw", 256, 1024), [[0, 768]], -20, 0)
-    for b, n in ((0, 256), (ZB, 256), (DB0, 128)):
-        iota(r("w1", b, b + n), [[0, n]], 8192, 0)
+    v("set", r("sel"), 0.0)
+    ts(kx(6), qc, 15.0, OP.is_equal, -1.0, OP.mult)
+    ts(kx(7), kx(6), 2.0, OP.mult, 1.0, OP.add)
+    ts(kx(8), kx(6), 8192.0, OP.mult)
+    ts(kx(9), kx(6), 1.0, OP.add)
+    for i, c in enumerate((1.0, -1.0, kx(7))):
+        ts(r("sel", 144 * i + 15, 144 * i + 143, 16), r("g8"), gc, OP.is_equal, c, OP.mult)
+    sel = lambda q, i=0: r("sel", 144 * i + 15 - q, 144 * i + 143 - q)
+    act(r("idf"), r("id"))
+    act(r("idv"), r("id"), AF.Copy, scale=-256.0)
+    act(r("nid1"), r("id"), AF.Copy, scale=-1.0)
+    act(r("bk"), r("bb"), AF.Copy, scale=-4096.0)
+    act(r("nbk"), r("bb"), AF.Copy, scale=4096.0)
+    v("tt", r("lti"), r("lt"), r("id"), OP.add)
+    v("set", r("lti", 15, 128, 16), 0.0)
+    act(r("nlti"), r("lti"), AF.Copy, scale=-1.0)
+    v("tt", r("m3"), r("nlt"), r("idv"), OP.subtract)
+    act(r("nm3"), r("m3"), AF.Copy, scale=-1.0)
+    act(r("inc"), r("rr"), AF.Identity, scale=0.0, bias=kx(9))
+    v("set", r("tr0", 66, 208, 66), -4096.0)
+    v("copy", r("trc"), r("tr0"))
+    v("set", r("ij", 198, 208), 0.0)
+    v("set", r("sc"), 0.0)
+    v("set", r("ev", 132, 144), 0.0)
+    v("set", r("ec", 0, 4), 0.0)
+    ts(r("ec", 4, 5), qc, 1.5, OP.is_gt, 4096.0, OP.mult)
+    v("set", r("ec", 5, 9), 4096.0)
+    v("set", r("ci", CE - 1, CE), 8192)
+    v("set", r("ct", CE - 1, CE), 8192.0)
+    ts(kx(10), kx(6), 2049.0, OP.mult, 1.0, OP.add)
+    ts(kx(11), kx(6), 4097.0, OP.mult, 1.0, OP.add)
+    for t in range(4):
+        for c, step in enumerate((170, 341, 0)):
+            b = kx(9)
+            if step * t:
+                b = kx(10 + 2 * t + c)
+                ts(b, kx(6), 1.0 + step * t % 1024 // 16 * 16, OP.mult, 1.0, OP.add)
+            lo, hi = 66 * c, 66 * c + (66 if c < 2 else 76)
+            act(r("svc", 208 * t + lo, 208 * t + hi), r("ij", lo, hi), AF.Identity, scale=kx(6), bias=b)
+    for lo, n in ((0, 1), (1, 3)):
+        for c in range(1, 4):
+            o = 208 * lo + 66 * c
+            ts(r("svc", o, o + 208 * (n - 1) + 1, 208), r("g8", 0, n), 0.0, OP.mult, kx(10 + c // 3), OP.add)
 
-    def rank_stage(t):
-        xw = lambda lo, hi: r("p6", lo, hi)
+    def lists(t):
+        xw, iw = lambda lo, hi: r("p6", lo, hi), "iw%d" % (t % 2)
         for c, (step, thr, op) in enumerate(TESTS):
             seg, c0, o = (0, 66, 198)[c], step * t % 1024 // 16, 198 * c + 66 * (t - 1)
             if t == 0:
@@ -333,23 +415,48 @@ def rank_program(g, core, T, topo):
             else:
                 v("tt", r("fl", seg + 1, seg + 65 - c0), xw(c0, 64), r("tp", o + 1, o + 65 - c0), op)
                 v("tt", r("fl", seg + 65 - c0, seg + 66), xw(0, c0 + 1), r("tp", o + 65 - c0, o + 66), op)
-        ts(r("fl", 133, 197), xw(0, 64), 40.0, OP.is_gt)
-        ts(r("fn"), xw(0, 64), 16.0, OP.add, 0.0, OP.max)
+        ts(r("fl", 133, 197), xw(0, 64), 56.0, OP.is_gt)
+        act(r("fn"), xw(0, 64), AF.Relu)
+
+        def product(bk, o, m, minus, last):
+            pe(r(bk, o, o + 198), r(m), r("fl", 0, 198), bk == "p3", False)
+            pe(r(bk, o + 67, o + 132), r(minus), r("fl", 199, 264), False, last)
         pe(r("p5", 256, 454), r("id"), r("bs"), True, False)
-        for o, m in ((256, "bb"), (0, "lt")):
-            pe(r("p5", o, o + 198), r(m), r("fl", 0, 198), o == 0, False)
-            pe(r("p5", o + 67, o + 132), r("n" + m), r("fl", 199, 264), False, True)
-        v("scan", r("sc"), r("mk3"), r("p5", 256, 454), 0.0, OP.mult, OP.add)
-        v("tt", r("fl", 67, 132), r("fl", 67, 132), r("fl", 199, 264), OP.subtract)
-        v("tt", r("p6", 256, 453), r("sc", 0, 197), r("p5", 1, 198), OP.add)
-        v("tt", r("zz", 0, 197), r("p6", 256, 453), r("fl", 1, 198), OP.mult)
-        parts = [(0, 64, 132)]
-        for seg, step in ((0, 170), (66, 341)):
-            c0 = step * t % 1024 // 16
-            parts += [(c0, 64, seg), (0, c0 + 1, seg + 64 - c0)] if t else [(0, 64, seg)]
-        for i, (lo, hi, at) in enumerate(parts):
-            pe(r("p6", 128 + lo, 128 + hi), r("id"), r("zz", at, at + hi - lo), i == 0, i == len(parts) - 1)
-        ts(r("pos"), r("p6", 128, 192), 2048.0, OP.add)
+        product("p5", 256, "bb", "nbb", True)
+        pe(r("p1", 0, 208), r("id"), r("trc"), True, False)
+        product("p1", 0, "bk", "nbk", True)
+        pe(r("p7", 0, 208), r("id"), r("svc", 208 * t, 208 * t + 208), True, False)
+        product("p7", 0, "nlti", "lti", True)
+        act(r("sv"), r("p7", 0, 208))
+        v("scan", r("sc", 1, 199), r("mk3"), r("p5", 256, 454), 0.0, OP.mult, OP.add)
+        v("tt", r("ve"), r("p1", 0, 208), r("sc"), OP.max)
+        for q in range(16):
+            pe(r("p6", 128, 141), sel(q), r("ve", q, 208, 16), q == 0, q == 15)
+        ts(r("mo", 0, 13), r("p6", 128, 141), 1.0 / 16, OP.mult, 2048.0, OP.add)
+        v("copy", ind(r(iw), r("mo", 0, 13)), r("sv"))
+        for b, lo, n in ((0, 0, 256), (IZ, 256, 256), (ID, 512, 128)):
+            v("scan", r("fs", lo, lo + n), r("inc", 0, n), r(iw, b, b + n), 16384.0, OP.add, OP.min)
+            if t < 2:
+                iota(r(iw, b, b + n), [[0, n]], 16384, 0)
+        ts(r("bt"), r("fs"), kx(8), OP.max, 1.0, OP.min)
+        for q in range(16):
+            pe(r("p6", 160, 200), sel(q, 2), r("bt", q, 640, 16), q == 0, q == 15)
+        ts(r("sl"), r("p6", 160, 192), 0.0, OP.add)
+        v("tt", r("dp"), r("p6", 192, 200), r("trd"), OP.min)
+        product("p3", 0, "m3", "nm3", False)
+        pe(r("p3", 0, 198), r("nid1"), r("sc", 0, 198), False, True)
+        for c in range(3):
+            act(r("th2", 66 * c, 66 * c + 66), r("p3", 66 * c, 66 * c + 66), AF.Identity, bias=kx(24 + c))
+        act(r("i0"), r("th2", 0, 132), AF.Relu)
+        act(r("il"), r("i0"), AF.Sign)
+        for c in range(2):
+            act(r("ev", 66 * c, 66 * c + 66), r("sc", 66 * c + 1, 66 * c + 67), AF.Relu, scale=-1.0, bias=kx(27 + c))
+        pe(r("p5", 0, 9), r("id"), r("ec"), True, False)
+        for q in range(16):
+            pe(r("p5", 0, 9), sel(q, 1), r("ev", q, 144, 16), False, q == 15)
+        ts(r("eo", 0, 9), r("p5", 0, 9), 1.0 / 16, OP.mult, 255.0, OP.add)
+
+    made = []
 
     def consts():
         v("set", r("one"), 1.0)
@@ -357,28 +464,29 @@ def rank_program(g, core, T, topo):
         v("set", r("onf"), -1.0 / 16)
         act(r("bb9"), r("bb"), AF.Copy, scale=-9.0)
         act(r("id8"), r("id"), AF.Copy, scale=-8.0)
-        act(r("idv"), r("id"), AF.Copy, scale=-256.0)
-        act(r("idf"), r("id"))
+        act(r("id16"), r("id"), AF.Copy, scale=16.0)
+        act(r("bq"), r("bb"), AF.Copy, scale=1.0 / 32)
+        act(r("nbq"), r("bb"), AF.Copy, scale=-1.0 / 32)
+        v("copy", r("ct", 0, 1024), r("ci", 0, 1024))
         act(r("nidf"), r("id"), AF.Copy, scale=-1.0)
         act(r("idk"), r("id"), AF.Copy, scale=-160.0)
         act(r("ih", 0, 128), r("id"))
         act(r("ih", 128, 256), r("id"), AF.Copy, scale=-64.0)
         act(r("mkb"), r("mk", 0, 384), AF.Copy, scale=float(1 << 18))
-        ts(r("gi"), r("g8"), gc, OP.is_equal)
-        ts(r("gif"), r("g8"), gc, OP.is_equal)
-        ts(r("gi64"), r("g8"), gc, OP.is_equal, 64.0, OP.mult)
         for c in range(3):
             ts(r("g2", 8 * c, 8 * c + 8), r("g8"), gc, OP.is_equal, -8192.0, OP.mult)
-        v("set", r("sel"), 0.0)
-        for q in range(16):
-            act(r("sel", q * 129, q * 128 + 128, 16), r("gi"))
-        for i in range(4):
-            ts(r("nsel", 512 * i, 512 * i + 512), r("sel", 512 * i, 512 * i + 512), -1.0, OP.mult)
+        zero = r("zr")
+        for c in range(2):
+            do("g", "asel", r("cy", 1024 * c, 1024 * c + 1024), zero, [[1, 8], [-16, 8], [0, 16]], OP.not_equal, 1.0, 8 * c - 15, 1)
+            made.append(len(ops) - 1)
+        do("g", "asel", r("ea", 1024, 2048), zero, [[-16, 8], [0, 8], [-1, 16]], OP.not_equal, 1.0, 0, 1)
+        made.append(len(ops) - 1)
+        ts(r("ea", 0, 1024), r("ea", 1024, 2048), 64.0, OP.mult)
+        v("set", r("ax"), 1.0)
         ts(kx(0), qc, -512.0, OP.mult, 7680.0 - 128, OP.add)
         ts(kx(1), qc, -512.0, OP.mult, 7680.0 + 8192, OP.add)
         ts(kx(2), qc, 8192.0, OP.mult)
         ts(kx(3), qc, -8192.0, OP.mult)
-        ts(kx(4), qc, 16.0, OP.mult)
         ts(kx(5), qc, -512.0, OP.mult, 7680.0, OP.add)
         for c in range(3):
             act(r("dg", 128 * c, 128 * c + 128), r("id"), AF.Identity, scale=kx((0, 1, 5)[c]))
@@ -389,42 +497,30 @@ def rank_program(g, core, T, topo):
                 up, down = (kx(2), -e), (kx(3), e)
                 for col, (x, y) in ((1, down if c else up), (65, up if c else down)):
                     ts(r("tp", o + col, o + col + 1), x, y, OP.add, thr, OP.max if c else OP.min)
-        ts(r("bm", 0, 128), r("imq"), qc, OP.is_lt, 16.0, OP.mult)
-        ts(r("bm", 128, 256), r("bb"), -100.0, OP.mult, 100.0, OP.add)
-        v("tt", r("bm", 0, 128), r("bm", 0, 128), r("bm", 128, 256), OP.add)
-        v("tt", r("bm", 256, 384), r("bm", 0, 128), r("imq"), OP.add)
-        for d in range(16):
-            ts(r("cy", 128 * d, 128 * d + 128), r("bm", 256, 384), qc, OP.subtract, float(d), OP.is_equal)
         ts(r("trs"), r("t32"), qc, OP.add, 1.0 / 16384, OP.mult)
-        for n, k in (("po", 18), ("px", 50)):
-            v("set", r(n), 0.0)
-            v("set", r(n, 0, None, k), float(1 << 20))
+        ts(r("px", 0, 264), r("i66"), qc, OP.is_equal, float(1 << 20), OP.mult)
         for s in range(2):
-            v("copy", r("po", 16 + s, None, 18), r("trs", 16 * s, 16 * s + 16))
-            ts(r("px", 48 + s, None, 50), r("t24", s, 24, 2), qc, OP.add, 1.0 / 16384, OP.mult)
-        v("set", r("ax"), 1.0)
-        ts(r("qm"), r("imq"), qc, OP.is_equal)
-        for a in range(16):
-            act(r("ea", 128 * a, 128 * a + 128), r("qm"), AF.Identity, scale=r("gif" if a > 7 else "gi64", a % 8, a % 8 + 1))
+            v("copy", r("px", 64 + s, 264, 66), r("trs", 16 * s, 16 * s + 4))
+        for c in range(1, 4):
+            dma("y", r("px", 264 * c, 264 * c + 264), r("px", 0, 264))
         ts(r("rp0"), r("g8r"), gc, OP.subtract)
         ts(r("ramp"), r("rp0"), 32768.0, OP.mult, -18432.0, OP.add)
         ts(r("pat"), r("g8r"), gc, OP.is_le, float(1 << 20), OP.mult)
-        ts(r("dcon"), r("i18"), qc, OP.is_gt, 128.0, OP.mult)
-        v("set", r("dcon", 0, None, 18), 128.0)
-        for s in range(2):
-            v("set", r("dcon", 16 + s, None, 18), 1.0 / 256)
-        ts(r("imn"), r("im"), -256.0, OP.add)
-        ts(r("jc8"), r("jc0"), kx(4), OP.add)
+        ts(r("jn"), r("jc8"), 1.0 / 16, OP.mult, -384.0, OP.add)
         v("copy", r("thf"), r("thi"))
         v("copy", r("thr"), r("thi"))
         act(r("nthr"), r("thf"), AF.Identity, scale=-1.0, bias=kx(23))
 
-    ts(r("frb", P=64), r("fr0", P=64), 16.0, OP.mult, -16.0, OP.add)
-    pe(r("p6", 0, 64), r("frb", P=64), ("id", T.q_id[0:64, 0:64], 0, 64, 1, 64), True, True)
+    ts(kx(4), qc, 16.0, OP.mult)
+    ts(r("jc8"), r("jc0"), kx(4), OP.add)
+    ts(r("trd"), r("jc8"), 1.0 / 16, OP.mult, CE - 128.0, OP.add)
+    v("set", r("zr"), 0.0)
+    ts(r("frb", P=64), r("fr0", P=64), 16.0, OP.mult)
+    behind(len(ops) - 2)
+    pe(r("p6", 0, 64), r("frb", P=64), r("id", 0, 64, P=64), True, True)
     v("set", r("xt", XE - 16, XE), 63.0)
     v("set", r("xt", 0, XW0), 0.0)
-    rank_stage(0)
-    POS = r("pos")
+    lists(0)
     XG = r("xt", XW0, XE)
     for i in range(4):
         o, x = r("xt", XW0 + 4096 + 1024 * i, XW0 + 5120 + 1024 * i), r("xt", XW0 + 1024 * i, XW0 + 1024 + 1024 * i)
@@ -436,37 +532,43 @@ def rank_program(g, core, T, topo):
 
     al = slice(None)
     for t in range(4):
-        last, w = t == 3, "w%d" % (t % 2)
-        v("copy", ind(r(w), POS), r("cb" if t else "ci"))
+        last = t == 3
+        marks.append(len(ops))
+        CG = r("ct" if t else "ci", 0, CE)
         for lo, hi in ((0, 64), (64, 256)):
-            v("copy", r("lua", lo, hi), r(w, lo, hi))
+            v("copy", r("lua", lo, hi), ind(CG, r("sl", lo // 16, hi // 16)))
+        if t:
+            act(r("lf"), ind(CG, r("sl", 0, 16)))
+        else:
+            v("copy", r("lf"), r("lua"))
         for e, lo, hi in ACTIVE:
             do(e, "act" if e == "s" else "copy", r("sa", 16 * lo, 16 * hi), ind(XG, r("lua", lo, hi)), *([AF.Copy] if e == "s" else []))
-        v("copy", r("luz"), r(w, ZB, ZB + 256))
+        v("copy", r("luz"), ind(CG, r("sl", 16, 32)))
         for e, lo, hi in FROZEN:
             if e == "s":
                 act(r("sz", 16 * lo, 16 * hi), ind(XG, r("luz", lo, hi)), AF.Relu, bias=r("nthr"))
             else:
                 ts(r("sz", 16 * lo, 16 * hi), ind(XG, r("luz", lo, hi)), r("thr"), OP.is_ge)
-        ts(r("dra"), r("fl", 133, 197), 0.5, OP.is_lt, 1e5, OP.mult)
-        v("tt", r("dr"), r("dra"), r("zz", 132, 196), OP.add)
-        ts(r("hib"), r("lua"), 1.0 / 64, OP.mult, 128.0, OP.add)
-        pe(r("p3", 256, 384), r("idf"), r(w, 1, 256, 2), True, False)
-        pe(r("p3", 256, 384), r("nidf"), r(w, 0, 256, 2), False, True)
+        act(r("hib"), r("lf"), AF.Identity, scale=1.0 / 64, bias=kx(22))
+        pe(r("p3", 256, 384), r("idf"), r("lf", 1, 256, 2), True, False)
+        pe(r("p3", 256, 384), r("nidf"), r("lf", 0, 256, 2), False, True)
 
         for h, bk in enumerate(("p0", "p2")):
             lo, hi = 128 * h, 128 * h + 128
             pe(r(bk, 0, 384), r("one"), r("dg"), True, False)
             pe(r(bk, 0, 256), r("hib", lo, hi), r("ih"), False, False)
-            pe(r(bk, 128, 256), r(w, lo, hi), r("idf"), False, False)
+            pe(r(bk, 128, 256), r("lf", lo, hi), r("idf"), False, False)
             for a in (lo, lo + 64):
                 v("scan", r("mx", 16 * a, 16 * a + 1024), r("mk"), r("sa", 16 * a, 16 * a + 1024), 0.0, OP.min, OP.max)
             o = r("p3", lo // 2, hi // 2)
             for k in range(16):
-                pe(o, r("sel", 128 * k, 128 * k + 128), r("sa", 16 * lo + 16 + k, 16 * hi, 32), k == 0, False)
-                pe(o, r("nsel", 128 * k, 128 * k + 128), r("sa", 16 * lo + k, 16 * hi, 32), False, k == 15)
+                pe(o, sel(k), r("sa", 16 * lo + 16 + k, 16 * hi, 32), k == 0, False)
+                pe(o, sel(k, 1), r("sa", 16 * lo + k, 16 * hi, 32), False, k == 15)
         ts(r("fa"), r("mx", 15, 4096, 16), r("thr"), OP.is_lt, -1.0, OP.mult)
-        pe(r("p1", 0, 256), r("bb9"), r("fa"), True, True)
+        pe(r("p7", 256, 512), r("bb9"), r("fa"), True, True)
+        pe(r("p1", 0, 256), r("id"), r("rr"), True, False)
+        pe(r("p1", 0, 256), r("bq"), r("fa"), False, True)
+        v("scan", r("st", 0, 256), r("bt", 0, 256), r("p1", 0, 256), 0.0, OP.mult, OP.max)
         for k in range(16):
             v("scan", r("sm", 256 * k, 256 * k + 256), r("sa", k, 4096, 16), r("fa"), 0.0, OP.max, OP.mult)
             for h, bk in enumerate(("p0", "p2")):
@@ -474,17 +576,16 @@ def rank_program(g, core, T, topo):
                     pe(r(bk, 0, 128), r("vn", 128 * h, 128 * h + 128), r("idv"), False, False)
                 pe(r(bk, k, 384, 16), r("sm", 256 * k + 128 * h, 256 * k + 128 * h + 128), r("g2"), False, k == 15)
             if k == 1:
-                ts(r("vn"), r("p1", 0, 256), 40.0, OP.is_gt, -1.0, OP.mult)
+                ts(r("vn"), r("p7", 256, 512), 40.0, OP.is_gt, -1.0, OP.mult)
         for h, bk in enumerate(("p0", "p2")):
             v("scan", r3("scn", h, al, 384 * h, 384 * h + 384, 384), r("mkb"), r(bk, 0, 384), 0.0, OP.min, OP.max)
-        act(r("rw", 0, 256), r("p1", 0, 256), AF.Relu, bias=kx(20))
         for c in range(2):
             v("tt", r3("df", slice(2 * c, 2 * c + 2), al, 16 * c, 16 * c + 16, 16), r3("scn", al, slice(128 * c + 15, 128 * c + 128, 16), 0, 768, 16),
               r3("scn", al, slice(271, 384, 16), 0, 768, 16), OP.subtract)
         pe(r3("p4", slice(0, 2), al, 0, 128, 128), r("id"), r("ramp"), True, False)
         for c in range(2):
             for a in range(8):
-                pe(r3("p4", slice(0, 2), slice(8 * a, 8 * a + 8), 0, 128, 16), r("ea", 1024 * c + 128 * a, 1024 * c + 128 * a + 128),
+                pe(r3("p4", slice(0, 2), slice(8 * (a ^ 3), 8 * (a ^ 3) + 8), 0, 128, 16), r("ea", 1024 * c + 128 * a, 1024 * c + 128 * a + 128),
                    r3("df", slice(2 * c, 2 * c + 2), al, 16 * c, 16 * c + 16, 16), False, c == 1 and a == 7)
         for h in range(2):
             v("scan", r("hs", 64 * h, 64 * h + 64), r("pat", 0, 64), r3("p4", h, al, 64 * h, 64 * h + 64, 64), 0.0, OP.add, OP.min)
@@ -494,33 +595,23 @@ def rank_program(g, core, T, topo):
         ts(r("cu"), ch, 2048.0, OP.add)
         v("tt", r("k32"), ch, r("g1"), OP.add)
         v("tt", r("cm"), r("k32"), r("g1"), OP.add)
-        ts(r("x0", 0, 16), ch, 2048.0 + XW0, OP.add, 1.0 / 16384, OP.mult)
-        ts(r("x0", 16, 32), r("cm"), 6144.0 + XW0, OP.add, 1.0 / 16384, OP.mult)
+        act(r("x0", 0, 16), ch, AF.Identity, scale=1.0 / 16384, bias=kx(29))
+        act(r("x0", 16, 32), r("cm"), AF.Identity, scale=1.0 / 16384, bias=kx(30))
         v("tt", r("x1"), r("x0"), r("trs"), OP.max)
         act(r("sch"), ind(XG, r("cu")))
-        pe(r("p0", 256, 512), r("id8"), r("fa"), True, False)
+        for a in range(16):
+            pe(r("p0", 256 + 16 * a, 272 + 16 * a), r("id8"), r("fa", 16 * (a ^ 3), 16 * (a ^ 3) + 16), a == 0, False)
         pe(r("p0", 256, 512), r("id"), r("sch"), False, True)
         nv1, nv2 = r3("nv", al, slice(0, 64), 0, 512, 256), r3("nv", al, slice(64, 128), 0, 512, 256)
         act(nv2, r("p0", 256, 512), AF.Relu, bias=kx(21), scale=-1.0)
         act(nv1, nv2, AF.Identity, bias=kx(21), scale=-1.0)
         for d in range(16):
             pe(r("p2", 256 + d, 512, 16), r("cy", 128 * d, 128 * d + 128), r("key"), True, True)
-        pe(r("p5", 0, 288), r("id"), r("dcon"), True, False)
-        for d in range(1, 16):
-            pe(r("p5", d, 288, 18), r("sd", 128 * d - 128, 128 * d), r("key"), False, d == 15)
-        act(r("ao"), r("p5", 0, 288), AF.Abs, scale=256.0)
         for a in range(16):
-            c, j = a // 4, a % 4
-            if j:
-                o = 50 * (3 * c + j - 1)
-                act(r("ax", o, o + 16 * j), r("p2", 256 + 64 * c, 256 + 16 * a), AF.Abs, scale=-1.0, bias=r("k32", a, a + 1))
-        v("scan", r("ro"), r("po"), r("ao"), 0.0, OP.max, OP.min)
+            act(r("ax", 66 * a, 66 * a + 64 - a % 4 * 16), r("p2", 256 + 16 * a, 320 + a // 4 * 64), AF.Abs, scale=-1.0, bias=r("k32", a, a + 1))
         v("scan", r("rx"), r("px"), r("ax"), 0.0, OP.max, OP.min)
         for s in range(2):
-            v("tt", r3("xa", al, slice(4 * s, 4 * s + 4), 16 * s, 16 * s + 16, 16), r("x1", 16 * s, 16 * s + 16), r("ro", 16 + s, None, 18), OP.min)
-        for s in range(2):
-            x = r3("xa", al, slice(4 * s + 1, 4 * s + 4), 16 * s, 16 * s + 16, 12)
-            v("tt", x, x, r("rx", 48 + s, None, 50), OP.min)
+            v("tt", r3("xa", al, slice(4 * s, 4 * s + 4), 16 * s, 16 * s + 16, 16), r("x1", 16 * s, 16 * s + 16), r("rx", 64 + s, None, 66), OP.min)
         ts(r("off"), r3("xa", al, al, 0, 32, 32), 16384.0, OP.mult)
         for c in range(3, -1, -1):
             v("copy", ind(r("xt"), r("off", 8 * c, 8 * c + 8)), r3("nv", c, al, 0, 512, 128))
@@ -534,12 +625,15 @@ def rank_program(g, core, T, topo):
         jt = r("jt", 128 * t, 128 * t + 128)
         v("scan", jt, r("jb"), r("neg"), -128.0, OP.add, OP.add)
         send(r("cn", 8 * t, 8 * t + 8), r("jt", 128 * t + 120, 128 * t + 128), "c%d" % t, t, RW1)
+        for j in made if t == 0 else ():
+            behind(j)
         v("scan", r("ju"), r("jb"), jt, 0.0, OP.max, OP.mult)
         pe(r("p6", 0, 8), r("id"), r("jc8"), True, False)
         for q in range(16):
-            pe(r("p6", 0, 8), r("sel", 128 * q, 128 * q + 128), r("ju", q, 128, 16), False, q == 15)
+            pe(r("p6", 0, 8), sel(q), r("ju", q, 128, 16), False, q == 15)
         ts(r("jo"), r("p6", 0, 8), 1.0 / 16, OP.mult)
-        v("tt", ind(r("jw", 256 * t, 256 * t + 256), r("jo")), r("je"), r(w, 0, 256, 2), OP.add)
+        v("tt", ind(r("jw", 256 * t, 256 * t + 256), r("jo")), r("je"), r("lf", 0, 256, 2), OP.add)
+        sent = len(ops) - 1
         send(r("jl", 128 * t, 128 * t + 128), r("jw", 256 * t, 256 * t + 128), "a%d" % t, t, RW2)
 
         for e, lo, hi in FROZEN:
@@ -552,40 +646,46 @@ def rank_program(g, core, T, topo):
             act(r("fz", 0, FT), r("p7", 0, FT), AF.Relu, bias=kx(23), scale=-1.0)
         if FT < 256:
             ts(r("fz", FT, 256), r("mx", 16 * FT + 15, 4096, 16), 0.5, OP.is_lt)
-        pe(r("p1", 256, 512), r("bb9"), r("fz"), True, True)
-        act(r("rw", ZB, ZB + 256), r("p1", 256, 512), AF.Relu, bias=kx(20), scale=-1.0)
-        act(r("rg"), ind(r("rw"), POS))
+        pe(r("p1", 256, 512), r("id"), r("rr"), True, False)
+        pe(r("p1", 256, 512), r("nbq"), r("fz"), False, True)
+        v("scan", r("st", 256, 512), r("bt", 256, 512), r("p1", 256, 512), 0.0, OP.mult, OP.max)
+        v("tt", r("kl"), ind(r("st"), r("eo", 0, 9)), r("th2", 0, 144), OP.is_lt)
         if not last:
             act(r("junk"), r("vn"), AF.Copy, accum_out=r("vs"))
 
         jl = r("jl", 128 * t, 128 * t + 128)
         cn = r("cn", 8 * t + 7, 8 * t + 8)
-        ts(r("tk"), r("dr"), -256.0, OP.add, cn, OP.is_lt)
-        ts(r("p7", 256, 384), r("imn"), cn, OP.is_lt, -16384.0, OP.mult)
-        v("tt", r("p7", 384, 512), r(w, DB0, DB0 + 128), r("p7", 256, 384), OP.add)
-        v("tt", r(w, DB0, DB0 + 128), r("p7", 384, 512), jl, OP.max)
-
+        act(r("c4"), cn, AF.Copy, scale=4096.0)
+        behind(sent)
+        ts(r("tk"), r("th2", 133, 197), cn, OP.add, 0.0, OP.is_gt)
+        behind(sent)
+        act(r("du"), r("jn"), AF.Relu, scale=-4096.0, bias=r("c4"))
+        v("tt", r("dy", 0, 8), r("trd"), r("du"), OP.subtract)
+        v("tt", r("dy", 8, 16), r("dy", 0, 8), r("dp"), OP.max)
+        v("copy", r("do"), r("dy", 8, 16))
+        v("copy", ind(r("ct"), r("do")), jl)
         if last:
-            act(r("cb", 0, 512), ind(r(w), r("pos", 0, 32)))
-            v("copy", r("cb", 512, 1024), ind(r(w), r("pos", 32, 64)))
-            dma("s", T.yc[:, 0:512], r("cb", 0, 512))
-            dma("y", T.yc[:, 512:1024], r("cb", 512, 1024))
-        pe(r("p6", 0, 64), r("id"), r("fn"), True, False)
-        pe(r("p6", 0, 64), r("idk"), r("tk"), False, False)
-        for q in range(16):
-            pe(r("p6", 0, 64), r("nsel", 128 * q, 128 * q + 128), r("rg", q, 1024, 16), False, q == 15)
+            dma("s", T.yc[:, 0:512], r("ct", 0, 512))
+            dma("y", T.yc[:, 512:1024], r("ct", 512, 1024))
+        else:
+            n = 341 * (t + 1) // 16 * 16 + 16
+            act(r("ct", 1024, 1024 + n), r("ct", 0, n))
+
+        parts = [("id", "fn", 0, 64, 0), ("idk", "tk", 0, 64, 0)]
+        for m, x in (("id16", "il"), ("idk", "kl")):
+            for seg, step in ((1, 170), (67, 341)):
+                c0 = step * t % 1024 // 16
+                parts += [(m, x, c0, 64, seg), (m, x, 0, c0 + 1, seg + 64 - c0)] if t else [(m, x, 0, 64, seg)]
+        for i, (m, x, lo, hi, at) in enumerate(parts):
+            pe(r("p6", lo, hi), r(m), r(x, at, at + hi - lo), i == 0, i == len(parts) - 1)
         if not last:
             pe(r("p3", 400, 401), r("onf"), r("vs"), True, True)
             v("copy", r("ai", 0, 1), r("p3", 400, 401))
             ts(r("ai", 1, 2), r("ai", 0, 1), 3, OP.bitwise_and)
             v("tt", r("thr"), r("ai", 1, 2), r("thf"), OP.add)
             act(r("nthr"), r("thr"), AF.Identity, scale=-1.0, bias=kx(23))
-            act(r("cb"), ind(r(w), POS))
-            if t < 2:
-                for b in (0, ZB):
-                    iota(r(w, b, b + 256), [[0, 256]], 8192, 0)
-            rank_stage(t + 1)
-    ts(r("fn"), r("p6", 0, 64), 16.0, OP.add, 0.0, OP.max)
+            lists(t + 1)
+    ts(r("fn"), r("p6", 0, 64), 0.0, OP.max)
     pe(r("p5", 0, 128, P=64), r("fn"), r("id"), True, True)
     ts(r("fo", P=64), r("p5", 0, 128, P=64), 1.0 / 16, OP.mult)
     for gr in range(8):

@@ -15,19 +15,19 @@ SB = {
     "fa": ([128, 256], B2), "fz": ([128, 256], B2), "sm": ([128, 4096], B2), "vn": ([128, 256], B2), "hib": ([128, 256], B2),
     "scn": ([128, 2, 384], F4), "df": ([128, 4, 8], H2), "hs": ([128, 128], F4),
     "g1": ([128, 16], F4), "key": ([128, 16], H2), "cm": ([128, 16], F4), "cu": ([128, 16], U2), "k32": ([128, 16], F4),
-    "ax": ([128, 1056], B2), "rx": ([128, 1056], B2), "x0": ([128, 32], F4), "x1": ([128, 32], F4), "xa": ([128, 4, 8], F4),
+    "ax": ([128, 1072], B2), "rx": ([128, 1072], B2), "x0": ([128, 32], F4), "xa": ([128, 4, 8], F4),
     "off": ([128, 32], U2), "sch": ([128, 256], B2), "nv": ([128, 4, 128], B2), "st": ([128, 512], F4), "kl": ([128, 144], B2),
-    "junk": ([128, 256], B2), "tk": ([128, 64], B2), "vs": ([128, 1], F4), "ai": ([128, 2], I4),
+    "junk": ([128, 256], B2), "tk": ([128, 64], B2), "vs": ([128, 1], F4),
     "jm": M, "je": ([128, 128], F4), "jb": M, "jt": ([128, 512], B2), "cn": ([128, 32], B2), "ju": M,
     "jo": ([128, 8], U2), "jw": ([128, 1024], F4), "jl": ([128, 512], F4),
-    "c4": ([128, 1], F4), "du": ([128, 8], F4), "dy": ([128, 16], F4), "do": ([128, 8], U2),
+    "c4": ([128, 1], F4), "du": ([128, 8], F4), "dy": ([128, 8], F4), "do": ([128, 8], U2),
     "im": ([128, 128], F4), "img": ([128, 128], F4), "g8": ([128, 8], F4), "ki": ([128, 8], I4), "kf": ([128, 8], F4), "kx": ([128, 32], F4),
     "g2": ([128, 24], B2), "idf": ([128, 128], F4), "nidf": ([128, 128], F4), "onf": ([128, 128], F4), "ih": ([128, 256], B2), "dg": ([128, 384], B2),
-    "ea": ([128, 2048], B2), "cy": ([128, 2048], B2), "zr": ([128, 1024], B2), "px": ([128, 1056], B2), "i66": ([128, 264], B2),
+    "ea": ([128, 2048], B2), "cy": ([128, 2048], B2), "zr": ([128, 1024], B2), "px": ([128, 1088], B2), "i66": ([128, 272], B2),
     "t32": ([128, 32], F4), "trs": ([128, 32], F4), "bs": ([128, 198], B2), "mk": ([128, 1024], B2), "mkb": ([128, 384], B2), "mk3": ([128, 198], B2),
     "sel": ([128, 432], B2), "jc0": ([128, 8], F4), "jc8": ([128, 8], B2), "jn": ([128, 8], F4), "trd": ([128, 8], F4), "tp": ([128, 594], B2),
     "svc": ([128, 832], B2), "tr0": ([128, 208], F4), "trc": ([128, 208], H2), "ij": ([128, 208], B2), "inc": ([128, 256], B2),
-    "rr": ([128, 256], B2), "ec": ([128, 9], B2),
+    "rr": ([128, 256], B2), "un": ([128, 16], F4), "al": ([128, 64], U2), "aw": ([128, 4], F4), "ec": ([128, 9], B2),
 }
 POOL = {k: 128 * i for i, k in enumerate("bk nbk lti nlti m3 nm3 nid1 bq nbq id16 g8r bb bb9 gt lt id idv id8 ramp rp0 pat nbb nlt idk one neg".split())}
 SB["mat"] = ([128, 128 * len(POOL)], B2)
@@ -37,10 +37,11 @@ NDMA = 40
 SEMAPHORES = ["ev", "es", "et", "eg"] + [x + str(t) for x in "acl" for t in range(4)] + ["d%d" % i for i in range(NDMA)]
 TESTS = ((170, 8.0, OP.is_lt), (341, 8.0, OP.is_gt), (341, 56.0, OP.is_gt))
 ACTIVE = (("s", 0, 48), ("v", 48, 128), ("s", 128, 192), ("s", 192, 256))
+HALVES = (3,)
 FROZEN = (("s", 0, 64), ("s", 64, 128), ("s", 128, 192), ("s", 192, 256))
 
-CY, CPE, FIX, PFIX, WAKE, WAKEX, GAMMA, SIGMA, IND, SIND, RW1, RW2, PASSES, NOISE, DENS, GRAIN, SEED, FIRST, FT = 0.00088, 0.00046, 0.02, 0.008, 0.17, 0.17, 1.5, 2.7, 0.055, 0.15, 3.0, 3.5, 250, 3.0, 4, 8, 9, 3.0, 192
-CASES = (({}, -1.5, 0.3), ({"r": 1.5}, 1.5, 0.2), ({"c": 1.3, "i": 1.65, "o": 1.9}, 0.0, 0.15), ({"i": 0.75, "o": 0.7, "w": 1.5}, -1.0, 0.3))
+CY, CPE, FIX, PFIX, WAKE, WAKEX, GAMMA, SIGMA, IND, SIND, RW1, RW2, PASSES, NOISE, DENS, GRAIN, SEED, MOVES, HEAT, FIRST, FT = 0.00088, 0.00046, 0.02, 0.008, 0.17, 0.17, 1.5, 2.7, 0.055, 0.15, 4.0, 4.5, 200, 3.0, 4, 8, 3, 5000, 0.02, 3.0, 192
+CASES = (({}, -2.5, 0.3), ({"r": 1.5}, 1, 0.25), ({"c": 1.3, "i": 1.65, "o": 1.9}, -1, 0.15), ({"i": 0.75, "o": 0.7, "w": 1.5}, -2, 0.3))
 PLAN = []
 
 
@@ -265,7 +266,7 @@ def rank_program(g, core, T, topo):
                 seen = {}
             k = (qs[i], ops[i][1][0][0].replace("iw1", "iw0"), i < marks[0])
             seen[k] = seen.get(k, 0) + 1
-            tag.append(k + (seen[k] // GRAIN,))
+            tag.append(k + (seen[k] // (GRAIN if i >= marks[0] else 2),))
         cases = []
         for factor, more, weight in CASES:
             d = [dur[i] * factor.get(ops[i][5], 1) for i in up]
@@ -296,8 +297,49 @@ def rank_program(g, core, T, topo):
                     shake[k] = NOISE * (x % 1000) / 1000 if p > 1 and x % 7 < DENS else 0
             back = place([shake[tag[i]] - best[1][i] - dur[i] for i in up], bw, down, tail)
             key = [-back[i] - dur[i] for i in up]
+
+        def times(line, d, e, before, weight):
+            free, last, start, held = {q: 0.0 for q in Q}, {q: -1 for q in Q}, [0.0] * n, [-1] * n
+            for i in line:
+                q = qs[i]
+                t, h = free[q], last[q]
+                for j, y in before[i]:
+                    if start[j] + y >= t:
+                        t, h = start[j] + y, j
+                start[i], held[i] = t, h
+                free[q], last[q] = t + d[i], i
+            return start, held
         if not PLAN:
-            PLAN.extend(sorted(range(n), key=lambda i: (best[1][i], i)))
+            now = best[0]
+            line = top = sorted(up, key=lambda i: (best[1][i], i))
+            least, arcs = now, []
+            for p in range(MOVES):
+                if not arcs:
+                    c = cases[p % len(cases)]
+                    start, held = times(line, *c)
+                    line = sorted(line, key=lambda i: start[i])
+                    i = max(up, key=lambda i: start[i] + c[1][i])
+                    while held[i] >= 0:
+                        if held[i] not in pre[i]:
+                            arcs.append((held[i], i))
+                        i = held[i]
+                x = x * 16807 % 2147483647
+                a, b = arcs.pop(x % len(arcs))
+                ia, ib = line.index(a), line.index(b)
+                for _ in range(x >> 8 & 3):
+                    k = ia - 1
+                    while k >= 0 and qs[line[k]] != qs[a]:
+                        k -= 1
+                    if k >= 0 and not above[b] >> line[k] & 1:
+                        ia = k
+                mid = line[ia:ib]
+                new = line[:ia] + [k for k in mid if above[b] >> k & 1] + [b] + [k for k in mid if not above[b] >> k & 1] + line[ib + 1:]
+                end = sum(length(new, *c) for c in cases)
+                if end < now + HEAT * (1 - p / MOVES) * (x >> 12 & 15) / 15:
+                    now, line, arcs = end, new, []
+                    if end < least:
+                        least, top = end, new
+            PLAN.extend(top)
         for i in PLAN:
             ops[i][4]()
 
@@ -330,7 +372,7 @@ def rank_program(g, core, T, topo):
     iota(r("g8"), [[1, 8]], 0, 0)
     for w in ("iw0", "iw1"):
         for b, n in ((0, 256), (IZ, 256), (ID, 128)):
-            iota(r(w, b, b + n), [[0, n]], 16384, 0)
+            iota(r(w, b, b + n), [[0, n]], 1, 0)
     iota(r("tr0"), [[1, 208]], 1072, 0)
     iota(r("ij", 0, 198), [[0, 3], [16, 66]], -16, 0)
     iota(r("rr"), [[-1, 256]], 256, 0)
@@ -338,7 +380,7 @@ def rank_program(g, core, T, topo):
     iota(r("g8r"), [[0, 16], [1, 8]], 0, 0)
     iota(r("jc0"), [[256, 8]], 2048, 0)
     iota(r("t32"), [[16, 2], [0, 4], [32, 4]], 0, 0)
-    iota(r("i66"), [[0, 4], [-1, 66]], 16, 0)
+    iota(r("i66", 0, 268), [[0, 4], [-1, 67]], 16, 0)
     iota(r("jw", 0, 256), [[0, 256]], -20, 0)
     kx = lambda i: r("kx", i, i + 1)
     v("set", r("fl"), 0.0)
@@ -348,9 +390,6 @@ def rank_program(g, core, T, topo):
     v("set", r("bs", 132, 133), ID - 2048.0)
     v("set", r("mk3"), 1.0)
     v("set", r("mk3", 0, 198, 66), 0.0)
-    for i, c in ((21, 63.0), (23, 1.0), (24, -2048 - 4.5 / 32), (25, IZ - 2048 - 4.5 / 32), (26, ID - 2048.0), (27, 256 - 2048.0),
-                 (28, 256 + IZ - 2048.0), (22, 128.0), (29, (2048.0 + XW0) / 16384), (30, (6144.0 + XW0) / 16384)):
-        v("set", kx(i), c)
     ts(r("ki", 1, 2), r("ki", 0, 1), 15, OP.bitwise_and)
     ts(r("ki", 2, 3), r("ki", 0, 1), 4, OP.arith_shift_right)
     v("copy", r("kf", 0, 3), r("ki", 0, 3))
@@ -365,9 +404,8 @@ def rank_program(g, core, T, topo):
     v("set", r("sel"), 0.0)
     ts(kx(6), qc, 15.0, OP.is_equal, -1.0, OP.mult)
     ts(kx(7), kx(6), 2.0, OP.mult, 1.0, OP.add)
-    ts(kx(8), kx(6), 8192.0, OP.mult)
     ts(kx(9), kx(6), 1.0, OP.add)
-    for i, c in enumerate((1.0, -1.0, kx(7))):
+    for i, c in enumerate((1.0, -1.0)):
         ts(r("sel", 144 * i + 15, 144 * i + 143, 16), r("g8"), gc, OP.is_equal, c, OP.mult)
     sel = lambda q, i=0: r("sel", 144 * i + 15 - q, 144 * i + 143 - q)
     act(r("idf"), r("id"))
@@ -406,6 +444,8 @@ def rank_program(g, core, T, topo):
             o = 208 * lo + 66 * c
             ts(r("svc", o, o + 208 * (n - 1) + 1, 208), r("g8", 0, n), 0.0, OP.mult, kx(10 + c // 3), OP.add)
 
+    early = []
+
     def lists(t):
         xw, iw = lambda lo, hi: r("p6", lo, hi), "iw%d" % (t % 2)
         for c, (step, thr, op) in enumerate(TESTS):
@@ -434,24 +474,29 @@ def rank_program(g, core, T, topo):
             pe(r("p6", 128, 141), sel(q), r("ve", q, 208, 16), q == 0, q == 15)
         ts(r("mo", 0, 13), r("p6", 128, 141), 1.0 / 16, OP.mult, 2048.0, OP.add)
         v("copy", ind(r(iw), r("mo", 0, 13)), r("sv"))
+        for j in early if t == 0 else ():
+            behind(j)
         for b, lo, n in ((0, 0, 256), (IZ, 256, 256), (ID, 512, 128)):
-            v("scan", r("fs", lo, lo + n), r("inc", 0, n), r(iw, b, b + n), 16384.0, OP.add, OP.min)
+            v("scan", r("fs", lo, lo + n), r("inc", 0, n), r(iw, b, b + n), 1.0, OP.add, OP.min)
             if t < 2:
-                iota(r(iw, b, b + n), [[0, n]], 16384, 0)
-        ts(r("bt"), r("fs"), kx(8), OP.max, 1.0, OP.min)
+                iota(r(iw, b, b + n), [[0, n]], 1, 0)
+        ts(r("bt", 0, 256), r("fs", 0, 256), kx(7), OP.mult, 0.0, OP.max)
+        act(r("bt", 256, 640), r("fs", 256, 640), AF.Relu, scale=kx(7))
         for q in range(16):
-            pe(r("p6", 160, 200), sel(q, 2), r("bt", q, 640, 16), q == 0, q == 15)
+            pe(r("p6", 160, 200), sel(q), r("bt", q, 640, 16), q == 0, q == 15)
         ts(r("sl"), r("p6", 160, 192), 0.0, OP.add)
-        v("tt", r("dp"), r("p6", 192, 200), r("trd"), OP.min)
+        listed = len(ops) - 1
+        act(r("dp"), r("p6", 192, 200))
         product("p3", 0, "m3", "nm3", False)
         pe(r("p3", 0, 198), r("nid1"), r("sc", 0, 198), False, True)
         for c in range(3):
-            act(r("th2", 66 * c, 66 * c + 66), r("p3", 66 * c, 66 * c + 66), AF.Identity, bias=kx(24 + c))
+            act(r("th2", 66 * c, 66 * c + 66), r("p3", 66 * c, 66 * c + 66), AF.Identity, bias=(-2048 - 4.5 / 32, IZ - 2048 - 4.5 / 32, ID - 2048.0)[c])
         act(r("i0"), r("th2", 0, 132), AF.Relu)
         act(r("il"), r("i0"), AF.Sign)
         for c in range(2):
-            act(r("ev", 66 * c, 66 * c + 66), r("sc", 66 * c + 1, 66 * c + 67), AF.Relu, scale=-1.0, bias=kx(27 + c))
+            act(r("ev", 66 * c, 66 * c + 66), r("sc", 66 * c + 1, 66 * c + 67), AF.Relu, scale=-1.0, bias=256.0 + IZ * c - 2048)
         pe(r("p5", 0, 9), r("id"), r("ec"), True, False)
+        behind(listed)
         for q in range(16):
             pe(r("p5", 0, 9), sel(q, 1), r("ev", q, 144, 16), False, q == 15)
         ts(r("eo", 0, 9), r("p5", 0, 9), 1.0 / 16, OP.mult, 255.0, OP.add)
@@ -467,7 +512,9 @@ def rank_program(g, core, T, topo):
         act(r("id16"), r("id"), AF.Copy, scale=16.0)
         act(r("bq"), r("bb"), AF.Copy, scale=1.0 / 32)
         act(r("nbq"), r("bb"), AF.Copy, scale=-1.0 / 32)
-        v("copy", r("ct", 0, 1024), r("ci", 0, 1024))
+        iota(r("junk", 0, 64), [[1, 64]], 0, 0)
+        ts(r("al"), r("junk", 0, 64), 16.0, OP.mult, qc, OP.add)
+        act(r("ct", 0, 1024), ind(r("ci", 0, 1024), r("al")))
         act(r("nidf"), r("id"), AF.Copy, scale=-1.0)
         act(r("idk"), r("id"), AF.Copy, scale=-160.0)
         act(r("ih", 0, 128), r("id"))
@@ -482,52 +529,51 @@ def rank_program(g, core, T, topo):
         do("g", "asel", r("ea", 1024, 2048), zero, [[-16, 8], [0, 8], [-1, 16]], OP.not_equal, 1.0, 0, 1)
         made.append(len(ops) - 1)
         ts(r("ea", 0, 1024), r("ea", 1024, 2048), 64.0, OP.mult)
-        v("set", r("ax"), 1.0)
+        iota(r("ax"), [[0, 1072]], 1, 0)
         ts(kx(0), qc, -512.0, OP.mult, 7680.0 - 128, OP.add)
         ts(kx(1), qc, -512.0, OP.mult, 7680.0 + 8192, OP.add)
-        ts(kx(2), qc, 8192.0, OP.mult)
-        ts(kx(3), qc, -8192.0, OP.mult)
+        ts(r("un"), r("im", 0, 16), qc, OP.is_gt)
         ts(kx(5), qc, -512.0, OP.mult, 7680.0, OP.add)
         for c in range(3):
             act(r("dg", 128 * c, 128 * c + 128), r("id"), AF.Identity, scale=kx((0, 1, 5)[c]))
         for c, (step, thr, op) in enumerate(TESTS):
-            v("set", r("tp", 198 * c, 198 * c + 198), thr)
+            act(r("tp", 198 * c, 198 * c + 198), r("mk3"), AF.Identity, scale=0.0, bias=thr)
             for t in range(1, 4):
-                o, e = 198 * c + 66 * (t - 1), 8192.0 * (step * t % 16 - 0.5)
-                up, down = (kx(2), -e), (kx(3), e)
-                for col, (x, y) in ((1, down if c else up), (65, up if c else down)):
-                    ts(r("tp", o + col, o + col + 1), x, y, OP.add, thr, OP.max if c else OP.min)
+                o, far, below = 198 * c + 66 * (t - 1), 32768.0 if c else -32768.0, r("un", step * t % 16, step * t % 16 + 1)
+                act(r("tp", o + 1, o + 2), below, AF.Identity, scale=far, bias=thr)
+                act(r("tp", o + 65, o + 66), below, AF.Identity, scale=-far, bias=thr + far)
         ts(r("trs"), r("t32"), qc, OP.add, 1.0 / 16384, OP.mult)
-        ts(r("px", 0, 264), r("i66"), qc, OP.is_equal, float(1 << 20), OP.mult)
+        ts(r("px", 0, 268), r("i66", 0, 268), qc, OP.is_equal, float(1 << 20), OP.mult)
         for s in range(2):
-            v("copy", r("px", 64 + s, 264, 66), r("trs", 16 * s, 16 * s + 4))
+            v("copy", r("px", 65 + s, 268, 67), r("trs", 16 * s, 16 * s + 4))
         for c in range(1, 4):
-            dma("y", r("px", 264 * c, 264 * c + 264), r("px", 0, 264))
+            dma("y", r("px", 268 * c, 268 * c + 268), r("px", 0, 268))
         ts(r("rp0"), r("g8r"), gc, OP.subtract)
         ts(r("ramp"), r("rp0"), 32768.0, OP.mult, -18432.0, OP.add)
         ts(r("pat"), r("g8r"), gc, OP.is_le, float(1 << 20), OP.mult)
-        ts(r("jn"), r("jc8"), 1.0 / 16, OP.mult, -384.0, OP.add)
+        ts(r("jn"), r("jc8"), 1.0 / 16, OP.mult, -383.0, OP.add)
         v("copy", r("thf"), r("thi"))
         v("copy", r("thr"), r("thi"))
-        act(r("nthr"), r("thf"), AF.Identity, scale=-1.0, bias=kx(23))
+        act(r("nthr"), r("thf"), AF.Identity, scale=-1.0, bias=1.0)
 
     ts(kx(4), qc, 16.0, OP.mult)
     ts(r("jc8"), r("jc0"), kx(4), OP.add)
     ts(r("trd"), r("jc8"), 1.0 / 16, OP.mult, CE - 128.0, OP.add)
     v("set", r("zr"), 0.0)
+    early.append(len(ops) - 1)
     ts(r("frb", P=64), r("fr0", P=64), 16.0, OP.mult)
-    behind(len(ops) - 2)
     pe(r("p6", 0, 64), r("frb", P=64), r("id", 0, 64, P=64), True, True)
     v("set", r("xt", XE - 16, XE), 63.0)
     v("set", r("xt", 0, XW0), 0.0)
-    lists(0)
     XG = r("xt", XW0, XE)
     for i in range(4):
         o, x = r("xt", XW0 + 4096 + 1024 * i, XW0 + 5120 + 1024 * i), r("xt", XW0 + 1024 * i, XW0 + 1024 + 1024 * i)
         if i == 0:
             ts(o, x, -1.0, OP.mult, 63.0, OP.add)
+            early.append(len(ops) - 1)
         else:
-            act(o, x, AF.Identity, scale=-1.0, bias=kx(21))
+            act(o, x, AF.Identity, scale=-1.0, bias=63.0)
+    lists(0)
     consts()
 
     al = slice(None)
@@ -549,7 +595,10 @@ def rank_program(g, core, T, topo):
                 act(r("sz", 16 * lo, 16 * hi), ind(XG, r("luz", lo, hi)), AF.Relu, bias=r("nthr"))
             else:
                 ts(r("sz", 16 * lo, 16 * hi), ind(XG, r("luz", lo, hi)), r("thr"), OP.is_ge)
-        act(r("hib"), r("lf"), AF.Identity, scale=1.0 / 64, bias=kx(22))
+        if t:
+            act(r("hib"), r("lf"), AF.Identity, scale=1.0 / 64, bias=128.0)
+        else:
+            ts(r("hib"), r("lua"), 1.0 / 64, OP.mult, 128.0, OP.add)
         pe(r("p3", 256, 384), r("idf"), r("lf", 1, 256, 2), True, False)
         pe(r("p3", 256, 384), r("nidf"), r("lf", 0, 256, 2), False, True)
 
@@ -568,7 +617,7 @@ def rank_program(g, core, T, topo):
         pe(r("p7", 256, 512), r("bb9"), r("fa"), True, True)
         pe(r("p1", 0, 256), r("id"), r("rr"), True, False)
         pe(r("p1", 0, 256), r("bq"), r("fa"), False, True)
-        v("scan", r("st", 0, 256), r("bt", 0, 256), r("p1", 0, 256), 0.0, OP.mult, OP.max)
+        v("scan", r("st", 0, 256), r("fs", 0, 256), r("p1", 0, 256), 0.0, OP.mult, OP.max)
         for k in range(16):
             v("scan", r("sm", 256 * k, 256 * k + 256), r("sa", k, 4096, 16), r("fa"), 0.0, OP.max, OP.mult)
             for h, bk in enumerate(("p0", "p2")):
@@ -593,28 +642,31 @@ def rank_program(g, core, T, topo):
         ts(r("g1"), ch, 2048.0, OP.is_ge, -4096.0, OP.mult)
         v("tt", r("key"), ch, r("g1"), OP.add)
         ts(r("cu"), ch, 2048.0, OP.add)
-        v("tt", r("k32"), ch, r("g1"), OP.add)
-        v("tt", r("cm"), r("k32"), r("g1"), OP.add)
-        act(r("x0", 0, 16), ch, AF.Identity, scale=1.0 / 16384, bias=kx(29))
-        act(r("x0", 16, 32), r("cm"), AF.Identity, scale=1.0 / 16384, bias=kx(30))
-        v("tt", r("x1"), r("x0"), r("trs"), OP.max)
+        act(r("k32"), r("key"))
+        v("tt", r("cm"), r("key"), r("g1"), OP.add)
+        act(r("x0", 0, 16), ch, AF.Abs, scale=1.0 / 16384, bias=(2048.0 + XW0) / 16384)
+        act(r("x0", 16, 32), r("cm"), AF.Abs, scale=1.0 / 16384, bias=(6144.0 + XW0) / 16384)
+        act(r("ax", 64, None, 67), ch, AF.Relu, bias=4096.0)
         act(r("sch"), ind(XG, r("cu")))
         for a in range(16):
             pe(r("p0", 256 + 16 * a, 272 + 16 * a), r("id8"), r("fa", 16 * (a ^ 3), 16 * (a ^ 3) + 16), a == 0, False)
         pe(r("p0", 256, 512), r("id"), r("sch"), False, True)
         nv1, nv2 = r3("nv", al, slice(0, 64), 0, 512, 256), r3("nv", al, slice(64, 128), 0, 512, 256)
-        act(nv2, r("p0", 256, 512), AF.Relu, bias=kx(21), scale=-1.0)
-        act(nv1, nv2, AF.Identity, bias=kx(21), scale=-1.0)
+        act(nv2, r("p0", 256, 512), AF.Relu, bias=63.0, scale=-1.0)
+        act(nv1, nv2, AF.Identity, bias=63.0, scale=-1.0)
         for d in range(16):
             pe(r("p2", 256 + d, 512, 16), r("cy", 128 * d, 128 * d + 128), r("key"), True, True)
-        for a in range(16):
-            act(r("ax", 66 * a, 66 * a + 64 - a % 4 * 16), r("p2", 256 + 16 * a, 320 + a // 4 * 64), AF.Abs, scale=-1.0, bias=r("k32", a, a + 1))
-        v("scan", r("rx"), r("px"), r("ax"), 0.0, OP.max, OP.min)
-        for s in range(2):
-            v("tt", r3("xa", al, slice(4 * s, 4 * s + 4), 16 * s, 16 * s + 16, 16), r("x1", 16 * s, 16 * s + 16), r("rx", 64 + s, None, 66), OP.min)
-        ts(r("off"), r3("xa", al, al, 0, 32, 32), 16384.0, OP.mult)
-        for c in range(3, -1, -1):
-            v("copy", ind(r("xt"), r("off", 8 * c, 8 * c + 8)), r3("nv", c, al, 0, 512, 128))
+        for c0, c1 in ((2, 4), (0, 2)) if t in HALVES else ((0, 4),):
+            for a in range(4 * c0, 4 * c1):
+                act(r("ax", 67 * a, 67 * a + 64 - a % 4 * 16), r("p2", 256 + 16 * a, 320 + a // 4 * 64), AF.Abs, scale=-1.0, bias=r("k32", a, a + 1))
+            lo, hi, n = 268 * c0, 268 * c1, 4 * (c1 - c0)
+            v("scan", r("rx", lo, hi), r("px", lo, hi), r("ax", lo, hi), 0.0, OP.max, OP.min)
+            for s in range(2):
+                o = 8 * c0 + n * s
+                v("tt", r3("xa", slice(c0, c1), slice(4 * s, 4 * s + 4), o, o + n, n), r("x0", 16 * s + 4 * c0, 16 * s + 4 * c1), r("rx", lo + 65 + s, hi, 67), OP.min)
+            ts(r("off", 8 * c0, 8 * c1), r3("xa", slice(c0, c1), al, 8 * c0, 8 * c1, 2 * n), 16384.0, OP.mult)
+            for c in range(c1 - 1, c0 - 1, -1):
+                v("copy", ind(r("xt"), r("off", 8 * c, 8 * c + 8)), r3("nv", c, al, 0, 512, 128))
         if last:
             for i in range(2):
                 dma("y", T.yx[:, 2048 * i:2048 * i + 2048], r("xt", XW0 + 2048 * i, XW0 + 2048 * i + 2048))
@@ -643,26 +695,27 @@ def rank_program(g, core, T, topo):
             else:
                 v("scan", r("mx", 16 * lo, 16 * hi), r("mk", 0, 16 * (hi - lo)), r("sz", 16 * lo, 16 * hi), 0.0, OP.min, OP.max)
         if FT:
-            act(r("fz", 0, FT), r("p7", 0, FT), AF.Relu, bias=kx(23), scale=-1.0)
+            act(r("fz", 0, FT), r("p7", 0, FT), AF.Relu, bias=1.0, scale=-1.0)
         if FT < 256:
             ts(r("fz", FT, 256), r("mx", 16 * FT + 15, 4096, 16), 0.5, OP.is_lt)
         pe(r("p1", 256, 512), r("id"), r("rr"), True, False)
         pe(r("p1", 256, 512), r("nbq"), r("fz"), False, True)
-        v("scan", r("st", 256, 512), r("bt", 256, 512), r("p1", 256, 512), 0.0, OP.mult, OP.max)
+        v("scan", r("st", 256, 512), r("fs", 256, 512), r("p1", 256, 512), 0.0, OP.mult, OP.max)
         v("tt", r("kl"), ind(r("st"), r("eo", 0, 9)), r("th2", 0, 144), OP.is_lt)
         if not last:
             act(r("junk"), r("vn"), AF.Copy, accum_out=r("vs"))
 
         jl = r("jl", 128 * t, 128 * t + 128)
         cn = r("cn", 8 * t + 7, 8 * t + 8)
-        act(r("c4"), cn, AF.Copy, scale=4096.0)
+        act(r("c4"), cn, AF.Copy, scale=-4096.0)
         behind(sent)
-        ts(r("tk"), r("th2", 133, 197), cn, OP.add, 0.0, OP.is_gt)
+        act(r("tk"), r("th2", 133, 197), AF.Relu, bias=cn)
         behind(sent)
-        act(r("du"), r("jn"), AF.Relu, scale=-4096.0, bias=r("c4"))
-        v("tt", r("dy", 0, 8), r("trd"), r("du"), OP.subtract)
-        v("tt", r("dy", 8, 16), r("dy", 0, 8), r("dp"), OP.max)
-        v("copy", r("do"), r("dy", 8, 16))
+        act(r("du"), r("jn"), AF.Relu, scale=4096.0, bias=r("c4"))
+        pe(r("p5", 16, 24), r("idf"), r("dp"), True, False)
+        pe(r("p5", 16, 24), r("idf"), r("du"), False, True)
+        v("tt", r("dy"), r("p5", 16, 24), r("trd"), OP.min)
+        v("copy", r("do"), r("dy"))
         v("copy", ind(r("ct"), r("do")), jl)
         if last:
             dma("s", T.yc[:, 0:512], r("ct", 0, 512))
@@ -680,10 +733,13 @@ def rank_program(g, core, T, topo):
             pe(r("p6", lo, hi), r(m), r(x, at, at + hi - lo), i == 0, i == len(parts) - 1)
         if not last:
             pe(r("p3", 400, 401), r("onf"), r("vs"), True, True)
-            v("copy", r("ai", 0, 1), r("p3", 400, 401))
-            ts(r("ai", 1, 2), r("ai", 0, 1), 3, OP.bitwise_and)
-            v("tt", r("thr"), r("ai", 1, 2), r("thf"), OP.add)
-            act(r("nthr"), r("thr"), AF.Identity, scale=-1.0, bias=kx(23))
+            aw = [r("aw", i, i + 1) for i in range(4)]
+            act(aw[0], r("p3", 400, 401), AF.Identity, scale=0.25, bias=-0.375)
+            act(aw[1], r("p3", 400, 401), AF.Identity, bias=r("thf"))
+            act(aw[2], aw[0], AF.Identity, bias=12582912.0)
+            act(aw[3], aw[2], AF.Identity, scale=-4.0, bias=4 * 12582912.0)
+            act(r("thr"), aw[3], AF.Identity, bias=aw[1])
+            act(r("nthr"), r("thr"), AF.Identity, scale=-1.0, bias=1.0)
             lists(t + 1)
     ts(r("fn"), r("p6", 0, 64), 0.0, OP.max)
     pe(r("p5", 0, 128, P=64), r("fn"), r("id"), True, True)

from concourse.mybir import AluOpType as OP, ActivationFunctionType as AF

F4, B2, H2, I4, U2 = "float32", "bfloat16", "float16", "int32", "uint16"
XW0, XE = 128, 8336
IZ, ID, IW = 1040, 2080, 3328
CE, CW = 2064, 2192
M = ([128, 128], B2)
SB = {
    "xt": ([128, XE], B2), "ci": ([128, CE], I4), "ct": ([128, CW], F4), "fn": ([128, 64], B2), "fo": ([64, 128], F4),
    "thi": ([128, 1], I4), "thf": ([128, 1], F4), "thr": ([128, 1], F4), "nthr": ([128, 1], F4), "fr0": ([64, 128], I4), "frb": ([64, 128], B2),
    "fl": ([128, 264], B2), "sc": ([128, 208], H2), "ve": ([128, 208], H2), "sv": ([128, 208], B2), "mo": ([128, 14], U2),
    "iw0": ([128, IW], B2), "iw1": ([128, IW], B2), "fs": ([128, 640], B2), "bt": ([128, 640], B2), "sl": ([128, 32], U2),
    "th2": ([128, 198], F4), "i0": ([128, 132], B2), "il": ([128, 132], B2), "ev": ([128, 144], B2), "eo": ([128, 10], U2), "dp": ([128, 8], F4),
    "lua": ([128, 256], U2), "luz": ([128, 256], U2), "lf": ([128, 256], F4), "sa": ([128, 4096], B2), "sz": ([128, 4096], B2), "mx": ([128, 4096], B2),
    "fa": ([128, 256], B2), "fz": ([128, 256], B2), "sm": ([128, 4096], B2), "vn": ([128, 256], B2), "hib": ([128, 256], B2),
    "scn": ([128, 2, 384], F4), "df": ([128, 4, 8], H2), "hs": ([128, 128], F4),
    "g1": ([128, 16], F4), "key": ([128, 16], H2), "cm": ([128, 16], F4), "cu": ([128, 16], U2), "k32": ([128, 16], F4),
    "ax": ([128, 1072], B2), "rx": ([128, 1072], B2), "x0": ([128, 32], F4), "xa": ([128, 4, 8], F4),
    "off": ([128, 32], U2), "sch": ([128, 256], B2), "nv": ([128, 4, 128], B2), "st": ([128, 512], F4), "kl": ([128, 144], B2),
    "junk": ([128, 256], B2), "tk": ([128, 64], B2), "vs": ([128, 1], F4),
    "jm": M, "je": ([128, 128], F4), "jb": M, "jt": ([128, 512], B2), "cn": ([128, 32], B2), "ju": M,
    "jo": ([128, 8], U2), "jw": ([128, 1024], F4), "jl": ([128, 512], F4),
    "c4": ([128, 1], F4), "du": ([128, 8], F4), "dy": ([128, 8], F4), "do": ([128, 8], U2),
    "im": ([128, 128], F4), "img": ([128, 128], F4), "g8": ([128, 8], F4), "ki": ([128, 8], I4), "kf": ([128, 8], F4), "kx": ([128, 32], F4),
    "g2": ([128, 24], B2), "idf": ([128, 128], F4), "nidf": ([128, 128], F4), "onf": ([128, 128], F4), "ih": ([128, 256], B2), "dg": ([128, 384], B2),
    "ea": ([128, 2048], B2), "cy": ([128, 2048], B2), "zr": ([128, 1024], B2), "px": ([128, 1088], B2), "i66": ([128, 272], B2),
    "t32": ([128, 32], F4), "trs": ([128, 32], F4), "bs": ([128, 198], B2), "mk": ([128, 1024], B2), "mkb": ([128, 384], B2), "mk3": ([128, 198], B2),
    "sel": ([128, 432], B2), "jc0": ([128, 8], F4), "jc8": ([128, 8], B2), "jn": ([128, 8], F4), "trd": ([128, 8], F4), "tp": ([128, 594], B2),
    "svc": ([128, 832], B2), "tr0": ([128, 208], F4), "trc": ([128, 208], H2), "ij": ([128, 208], B2), "inc": ([128, 256], B2),
    "rr": ([128, 256], B2), "un": ([128, 16], F4), "al": ([128, 64], U2), "aw": ([128, 4], F4), "ec": ([128, 9], B2),
}
POOL = {k: 128 * i for i, k in enumerate("bk nbk lti nlti m3 nm3 nid1 bq nbq id16 g8r bb bb9 gt lt id idv id8 ramp rp0 pat nbb nlt idk one neg".split())}
SB["mat"] = ([128, 128 * len(POOL)], B2)
SCRATCH = {"q_" + k: ("sbuf", v[0], v[1]) for k, v in SB.items()}
SCRATCH.update({"q_p%d" % i: ("psum", [128, 8, 64] if i == 4 else [128, 512], F4) for i in range(8)})
NDMA = 40
SEMAPHORES = ["ev", "es", "et", "eg"] + [x + str(t) for x in "acl" for t in range(4)] + ["d%d" % i for i in range(NDMA)]
TESTS = ((170, 8.0, OP.is_lt), (341, 8.0, OP.is_gt), (341, 56.0, OP.is_gt))
ACTIVE = (("s", 0, 48), ("v", 48, 128), ("s", 128, 192), ("s", 192, 256))
HALVES = (3,)
FROZEN = (("s", 0, 64), ("s", 64, 128), ("s", 128, 192), ("s", 192, 256))

CY, CPE, FIX, PFIX, WAKE, WAKEX, GAMMA, SIGMA, IND, SIND, RW1, RW2, PASSES, NOISE, DENS, GRAIN, SEED, MOVES, HEAT, FIRST, FT = 0.00088, 0.00046, 0.02, 0.008, 0.17, 0.17, 1.5, 2.7, 0.055, 0.15, 4.0, 4.5, 200, 3.0, 4, 8, 3, 5000, 0.02, 3.0, 192
CASES = (({}, -2.5, 0.3), ({"r": 1.5}, 1, 0.25), ({"c": 1.3, "i": 1.65, "o": 1.9}, -1, 0.15), ({"i": 0.75, "o": 0.7, "w": 1.5}, -2, 0.3))
PLAN = []


def rank_program(g, core, T, topo):
    rank = T.rank_of(core)
    if rank is None:
        return
    Q = {"v": g.vector, "s": g.scalar, "t": g.tensor, "g": g, "y": g.sync}
    cnt = {q: 0 for q in Q}
    know = {q: {} for q in Q}
    snap, log, nd = {}, {}, [0]

    def r(n, lo=None, hi=None, step=1, P=128):
        if n in POOL:
            return r("mat", POOL[n] + (lo or 0), POOL[n] + (hi or 128), step, P)
        t = T["q_" + n]
        hi = t.shape[1] if hi is None else hi
        lo = 0 if lo is None else lo
        return (n, t[0:P, lo:hi:step] if step != 1 else t[0:P, lo:hi], lo, hi, step, -(-(hi - lo) // step))

    def r3(n, a, b, lo, hi, els):
        return (n, T["q_" + n][:, a, b], lo, hi, 1, els)

    def ind(w, o):
        return ("@", w, o)

    def over(a, b):
        if a[0] >= b[1] or b[0] >= a[1]:
            return False
        return not (a[2] == b[2] and a[2] > 1 and (a[0] - b[0]) % a[2])

    def need(q, src, n):
        k = know[q]
        if k.get(src, 0) >= n:
            return
        Q[q].wait_ge(T.sem[src], n)
        k[src] = n
        for s2, n2 in snap.get((src, n), {}).items():
            if k.get(s2, 0) < n2:
                k[s2] = n2

    def deps(q, acc):
        req = {}
        own = "e" + q
        for (b, lo, hi, st, w) in acc:
            bank = b not in SB
            for (src, l2, h2, s2, w2), n in log.get(b, {}).items():
                if src == own:
                    if not (w or w2) or (w and q == "t") or not over((lo, hi, st), (l2, h2, s2)):
                        continue
                elif not bank and (not (w or w2) or not over((lo, hi, st), (l2, h2, s2))):
                    continue
                if req.get(src, 0) < n:
                    req[src] = n
        for src in sorted(req, key=lambda x: (x[0] != "e", x)):
            need(q, src, req[src])

    def note(src, n, acc):
        for (b, lo, hi, st, w) in acc:
            log.setdefault(b, {})[(src, lo, hi, st, w)] = n

    def flat(args, kw):
        acc, real, kk = [], [], {}
        for i, a in enumerate(args):
            if isinstance(a, tuple) and a[0] == "@":
                acc.append((a[1][0],) + a[1][2:5] + (i == 0,))
                acc.append((a[2][0],) + a[2][2:5] + (False,))
                real.append(a[1][1].indirect(a[2][1]))
            elif isinstance(a, tuple):
                acc.append((a[0],) + a[2:5] + (i == 0,))
                real.append(a[1])
            else:
                real.append(a)
        for k, a in kw.items():
            if isinstance(a, tuple):
                acc.append((a[0],) + a[2:5] + (k == "accum_out",))
                kk[k] = a[1]
            else:
                kk[k] = a
        return acc, real, kk

    ops, marks, later = [], [], []

    def cols(a):
        return 16 * a[2][5] if a[0] == "@" else a[5]

    def cost(q, name, args):
        xs = [a for a in args if isinstance(a, tuple)]
        n = max(cols(a) for a in xs[1:]) if len(xs) > 1 else cols(xs[0])
        names = [a[1][0] if a[0] == "@" else a[0] for a in xs if a[0] == "@" or a[5] > 1]
        two = all(b in SB and SB[b][1] in (B2, U2, H2) for b in names)
        if name == "mm":
            return max(64, cols(args[2])) * (4 if SB[args[2][0]][1] == F4 else 1) * CPE + PFIX
        if q == "g":
            return 0.15 + 2 * cols(args[0]) * CY
        if args[0][0] == "@":
            return SIND + n * SIGMA * CY
        if any(a[0] == "@" for a in xs):
            return IND + n * GAMMA * CY
        if name == "tt":
            n *= 2 if all(b in SB for b in names) else 1
        elif name in ("copy", "ts", "scan", "set") and two:
            n *= 0.5
        return max(n, 64) * CY + FIX

    def do(q, name, *args, **kw):
        acc, real, kk = flat(args, kw)
        e = Q[q]
        f = {"copy": lambda: e.tensor_copy(*real), "tt": lambda: e.tensor_tensor(*real), "ts": lambda: e.tensor_scalar(*real),
             "set": lambda: e.memset(*real), "scan": lambda: e.tensor_tensor_scan(*real), "act": lambda: e.activation(*real, **kk),
             "mm": lambda: e.matmul(*real), "iota": lambda: e.iota(*real, **kk), "asel": lambda: e.affine_select(*real)}[name]

        def issue():
            deps(q, acc)
            cnt[q] += 1
            src = "e" + q
            f().then_inc(T.sem[src], 1)
            snap[(src, cnt[q])] = dict(know[q])
            note(src, cnt[q], acc)
        c = cost(q, name, args)
        kind = "o" if args[0][0] == "@" else "i" if any(isinstance(a, tuple) and a[0] == "@" for a in args) else "c"
        ops.append((q, acc, c, c, issue, kind))

    def dma(q, out, in_):
        acc, ap = [], []
        for i, a in enumerate((out, in_)):
            ap.append(a[1] if isinstance(a, tuple) else a)
            if isinstance(a, tuple):
                acc.append((a[0],) + a[2:5] + (i == 0,))

        def issue():
            deps(q, acc)
            x = "d%d" % nd[0]
            nd[0] += 1
            Q[q].dma_start(ap[0], ap[1]).then_inc(T.sem[x], 16)
            snap[(x, 16)] = dict(know[q])
            note(x, 16, acc)
        ops.append((q, acc, 0.06, 2.0 + (acc[0][2] - acc[0][1]) / 700, issue, "d"))

    def send(out, in_, sem, t, way):
        dst = T.cores[(rank + 1 + t % 3) % len(T.cores)]
        rid, pid, _ = topo.addr(dst)
        ne = len(topo.engines(T.cores[(rank - 1 - t % 3) % len(T.cores)], core))
        ro, wo = (in_[0],) + in_[2:5] + (False,), (out[0],) + out[2:5] + (True,)

        def issue():
            deps("g", [ro])
            g.remote_dma(out[1], in_[1], T.sem[sem], T.sem["l%d" % t], pid, rid, topo.mask(core, dst))
            note(sem, ne, [wo])
        more = FIRST if sem == "c0" else 0
        ops.append(("g", [ro, wo], 1.0 + more, way + more, issue, "r"))

    def behind(j):
        later.append((len(ops) - 1, j))

    def order():
        n = len(ops)
        pre = [{} for _ in range(n)]
        hist = {}
        for i in range(n):
            q, acc = ops[i][0], ops[i][1]
            for (b, lo, hi, st, w) in acc:
                bank = b not in SB
                hs = hist.setdefault(b, ([], []))
                for h in (hs[0], hs[1]) if (w or bank) else (hs[0],):
                    for (j, q2, l2, h2, s2, w2) in h:
                        if bank and q == "t" and q2 == "t":
                            pre[i].setdefault(j, 0.0)
                        elif (bank and q != q2) or ((w or w2) and over((lo, hi, st), (l2, h2, s2))):
                            pre[i][j] = WAKE if q == q2 else WAKEX
            for (b, lo, hi, st, w) in acc:
                hist[b][0 if w else 1].append((i, q, lo, hi, st, w))
        for i, j in later:
            pre[i].setdefault(j, 0.0)
        above = [0] * n
        for i in range(n):
            pre[i].pop(i, None)
            seen = 0
            for j in sorted(pre[i], reverse=True):
                if seen >> j & 1:
                    del pre[i][j]
                seen |= above[j] | 1 << j
            above[i] = seen
        post = [[] for _ in range(n)]
        for i in range(n):
            for j in pre[i]:
                post[j].append(i)
        qs, dur = [o[0] for o in ops], [o[2] for o in ops]
        fw = [[(j, ops[j][3] + x) for j, x in pre[i].items()] for i in range(n)]
        bw = [[(j, ops[i][3] - dur[i] + dur[j] + pre[j][i]) for j in post[i]] for i in range(n)]

        def place(key, before, along, first):
            for i in along:
                for j, _ in before[i]:
                    if key[j] >= key[i]:
                        key[i] = key[j] + 1e-6
            busy = {q: [] for q in Q}
            start = [0.0] * n
            for i in sorted(along, key=lambda i: key[i]):
                t = first[i]
                for j, x in before[i]:
                    if start[j] + x > t:
                        t = start[j] + x
                b, d = busy[qs[i]], dur[i]
                k = len(b)
                while k and b[k - 1][1] > t:
                    k -= 1
                while k < len(b) and b[k][0] < t + d:
                    if b[k][1] > t:
                        t = b[k][1]
                    k += 1
                b.insert(k, (t, t + d))
                start[i] = t
            return start
        up, down, zero, tail = range(n), range(n - 1, -1, -1), [0.0] * n, [o[3] - o[2] for o in ops]
        way = [0.0] * n
        for i in down:
            way[i] = max([way[j] + x for j, x in bw[i]], default=tail[i])
        tag, seen = [], {}
        for i in up:
            if i in marks:
                seen = {}
            k = (qs[i], ops[i][1][0][0].replace("iw1", "iw0"), i < marks[0])
            seen[k] = seen.get(k, 0) + 1
            tag.append(k + (seen[k] // (GRAIN if i >= marks[0] else 2),))
        cases = []
        for factor, more, weight in CASES:
            d = [dur[i] * factor.get(ops[i][5], 1) for i in up]
            e = [d[i] + tail[i] + (more if ops[i][5] == "r" else 0) for i in up]
            cases.append((d, e, [[(j, e[j] + y * factor.get("w", 1)) for j, y in pre[i].items()] for i in up], weight))

        def length(line, d, e, before, weight):
            free, start = {q: 0.0 for q in Q}, [0.0] * n
            for i in line:
                t = free[qs[i]]
                for j, y in before[i]:
                    if start[j] + y > t:
                        t = start[j] + y
                start[i] = t
                free[qs[i]] = t + d[i]
            return weight * max(start[i] + e[i] for i in up)
        key, best, x = [-way[i] - dur[i] for i in up], None, SEED
        for p in range(0 if PLAN else PASSES):
            start = place(key, fw, up, zero)
            line = sorted(up, key=lambda i: (start[i], i))
            end = sum(length(line, *c) for c in cases)
            if best is None or end < best[0]:
                best = (end, start)
            shake = {}
            for k in tag:
                if k not in shake:
                    x = x * 16807 % 2147483647
                    shake[k] = NOISE * (x % 1000) / 1000 if p > 1 and x % 7 < DENS else 0
            back = place([shake[tag[i]] - best[1][i] - dur[i] for i in up], bw, down, tail)
            key = [-back[i] - dur[i] for i in up]

        def times(line, d, e, before, weight):
            free, last, start, held = {q: 0.0 for q in Q}, {q: -1 for q in Q}, [0.0] * n, [-1] * n
            for i in line:
                q = qs[i]
                t, h = free[q], last[q]
                for j, y in before[i]:
                    if start[j] + y >= t:
                        t, h = start[j] + y, j
                start[i], held[i] = t, h
                free[q], last[q] = t + d[i], i
            return start, held
        if not PLAN:
            now = best[0]
            line = top = sorted(up, key=lambda i: (best[1][i], i))
            least, arcs = now, []
            for p in range(MOVES):
                if not arcs:
                    c = cases[p % len(cases)]
                    start, held = times(line, *c)
                    line = sorted(line, key=lambda i: start[i])
                    i = max(up, key=lambda i: start[i] + c[1][i])
                    while held[i] >= 0:
                        if held[i] not in pre[i]:
                            arcs.append((held[i], i))
                        i = held[i]
                x = x * 16807 % 2147483647
                a, b = arcs.pop(x % len(arcs))
                ia, ib = line.index(a), line.index(b)
                for _ in range(x >> 8 & 3):
                    k = ia - 1
                    while k >= 0 and qs[line[k]] != qs[a]:
                        k -= 1
                    if k >= 0 and not above[b] >> line[k] & 1:
                        ia = k
                mid = line[ia:ib]
                new = line[:ia] + [k for k in mid if above[b] >> k & 1] + [b] + [k for k in mid if not above[b] >> k & 1] + line[ib + 1:]
                end = sum(length(new, *c) for c in cases)
                if end < now + HEAT * (1 - p / MOVES) * (x >> 12 & 15) / 15:
                    now, line, arcs = end, new, []
                    if end < least:
                        least, top = end, new
            PLAN.extend(top)
        for i in PLAN:
            ops[i][4]()

    def v(*a): do("v", *a)
    def pe(*a): do("t", "mm", *a)
    def act(out, in_, f=AF.Copy, **k): do("s", "act", out, in_, f, **k)

    def ts(out, in0, s1, op0, s2=None, op1=None):
        if op1 is None:
            v("ts", out, in0, s1, None, op0)
        else:
            v("ts", out, in0, s1, s2, op0, op1)

    def iota(out, pat, base, ch):
        if out[0] == "ki":
            do("g", "iota", out, pat, base, ch)
        else:
            do("g", "iota", out, pat, base, ch, allow_small_or_imprecise_dtypes=True)

    for gr in range(8):
        dma("y" if gr % 2 == 0 else "s", r("fr0", 16 * gr, 16 * gr + 16, P=64), T.fr[gr:gr + 1, :])
    dma("s", r("ci", 0, 1024), T.cl[:, :])
    for i in range(4):
        dma("y", r("xt", XW0 + 1024 * i, XW0 + 1024 * i + 1024), T.xv[:, 1024 * i:1024 * i + 1024])
    dma("s", r("thi"), T.th[:, :])

    iota(r("ki", 0, 1), [[1, 1]], 0, 1)
    iota(r("im"), [[1, 128]], 0, 0)
    iota(r("img"), [[1, 8], [0, 16]], 0, 0)
    iota(r("g8"), [[1, 8]], 0, 0)
    for w in ("iw0", "iw1"):
        for b, n in ((0, 256), (IZ, 256), (ID, 128)):
            iota(r(w, b, b + n), [[0, n]], 1, 0)
    iota(r("tr0"), [[1, 208]], 1072, 0)
    iota(r("ij", 0, 198), [[0, 3], [16, 66]], -16, 0)
    iota(r("rr"), [[-1, 256]], 256, 0)
    iota(r("mk"), [[0, 64], [64, 16]], 0, 0)
    iota(r("g8r"), [[0, 16], [1, 8]], 0, 0)
    iota(r("jc0"), [[256, 8]], 2048, 0)
    iota(r("t32"), [[16, 2], [0, 4], [32, 4]], 0, 0)
    iota(r("i66", 0, 268), [[0, 4], [-1, 67]], 16, 0)
    iota(r("jw", 0, 256), [[0, 256]], -20, 0)
    kx = lambda i: r("kx", i, i + 1)
    v("set", r("fl"), 0.0)
    v("set", r("bs"), 0.0)
    v("set", r("bs", 0, 1), -2048.0)
    v("set", r("bs", 66, 67), IZ - 2048.0)
    v("set", r("bs", 132, 133), ID - 2048.0)
    v("set", r("mk3"), 1.0)
    v("set", r("mk3", 0, 198, 66), 0.0)
    ts(r("ki", 1, 2), r("ki", 0, 1), 15, OP.bitwise_and)
    ts(r("ki", 2, 3), r("ki", 0, 1), 4, OP.arith_shift_right)
    v("copy", r("kf", 0, 3), r("ki", 0, 3))
    pc, qc, gc = [r("kf", i, i + 1) for i in range(3)]
    ts(r("id"), r("im"), pc, OP.is_equal)
    ts(r("bb"), r("img"), gc, OP.is_equal)
    ts(r("gt"), r("im"), pc, OP.is_gt)
    v("tt", r("lt"), r("gt"), r("bb"), OP.mult)
    act(r("nbb"), r("bb"), AF.Copy, scale=-1.0)
    act(r("nlt"), r("lt"), AF.Copy, scale=-1.0)
    iota(r("jw", 256, 1024), [[0, 768]], -20, 0)
    v("set", r("sel"), 0.0)
    ts(kx(6), qc, 15.0, OP.is_equal, -1.0, OP.mult)
    ts(kx(7), kx(6), 2.0, OP.mult, 1.0, OP.add)
    ts(kx(9), kx(6), 1.0, OP.add)
    for i, c in enumerate((1.0, -1.0)):
        ts(r("sel", 144 * i + 15, 144 * i + 143, 16), r("g8"), gc, OP.is_equal, c, OP.mult)
    sel = lambda q, i=0: r("sel", 144 * i + 15 - q, 144 * i + 143 - q)
    act(r("idf"), r("id"))
    act(r("idv"), r("id"), AF.Copy, scale=-256.0)
    act(r("nid1"), r("id"), AF.Copy, scale=-1.0)
    act(r("bk"), r("bb"), AF.Copy, scale=-4096.0)
    act(r("nbk"), r("bb"), AF.Copy, scale=4096.0)
    v("tt", r("lti"), r("lt"), r("id"), OP.add)
    v("set", r("lti", 15, 128, 16), 0.0)
    act(r("nlti"), r("lti"), AF.Copy, scale=-1.0)
    v("tt", r("m3"), r("nlt"), r("idv"), OP.subtract)
    act(r("nm3"), r("m3"), AF.Copy, scale=-1.0)
    act(r("inc"), r("rr"), AF.Identity, scale=0.0, bias=kx(9))
    v("set", r("tr0", 66, 208, 66), -4096.0)
    v("copy", r("trc"), r("tr0"))
    v("set", r("ij", 198, 208), 0.0)
    v("set", r("sc"), 0.0)
    v("set", r("ev", 132, 144), 0.0)
    v("set", r("ec", 0, 4), 0.0)
    ts(r("ec", 4, 5), qc, 1.5, OP.is_gt, 4096.0, OP.mult)
    v("set", r("ec", 5, 9), 4096.0)
    v("set", r("ci", CE - 1, CE), 8192)
    v("set", r("ct", CE - 1, CE), 8192.0)
    ts(kx(10), kx(6), 2049.0, OP.mult, 1.0, OP.add)
    ts(kx(11), kx(6), 4097.0, OP.mult, 1.0, OP.add)
    for t in range(4):
        for c, step in enumerate((170, 341, 0)):
            b = kx(9)
            if step * t:
                b = kx(10 + 2 * t + c)
                ts(b, kx(6), 1.0 + step * t % 1024 // 16 * 16, OP.mult, 1.0, OP.add)
            lo, hi = 66 * c, 66 * c + (66 if c < 2 else 76)
            act(r("svc", 208 * t + lo, 208 * t + hi), r("ij", lo, hi), AF.Identity, scale=kx(6), bias=b)
    for lo, n in ((0, 1), (1, 3)):
        for c in range(1, 4):
            o = 208 * lo + 66 * c
            ts(r("svc", o, o + 208 * (n - 1) + 1, 208), r("g8", 0, n), 0.0, OP.mult, kx(10 + c // 3), OP.add)

    early = []

    def lists(t):
        xw, iw = lambda lo, hi: r("p6", lo, hi), "iw%d" % (t % 2)
        for c, (step, thr, op) in enumerate(TESTS):
            seg, c0, o = (0, 66, 198)[c], step * t % 1024 // 16, 198 * c + 66 * (t - 1)
            if t == 0:
                ts(r("fl", seg + 1, seg + 65), xw(0, 64), thr, op)
            else:
                v("tt", r("fl", seg + 1, seg + 65 - c0), xw(c0, 64), r("tp", o + 1, o + 65 - c0), op)
                v("tt", r("fl", seg + 65 - c0, seg + 66), xw(0, c0 + 1), r("tp", o + 65 - c0, o + 66), op)
        ts(r("fl", 133, 197), xw(0, 64), 56.0, OP.is_gt)
        act(r("fn"), xw(0, 64), AF.Relu)

        def product(bk, o, m, minus, last):
            pe(r(bk, o, o + 198), r(m), r("fl", 0, 198), bk == "p3", False)
            pe(r(bk, o + 67, o + 132), r(minus), r("fl", 199, 264), False, last)
        pe(r("p5", 256, 454), r("id"), r("bs"), True, False)
        product("p5", 256, "bb", "nbb", True)
        pe(r("p1", 0, 208), r("id"), r("trc"), True, False)
        product("p1", 0, "bk", "nbk", True)
        pe(r("p7", 0, 208), r("id"), r("svc", 208 * t, 208 * t + 208), True, False)
        product("p7", 0, "nlti", "lti", True)
        act(r("sv"), r("p7", 0, 208))
        v("scan", r("sc", 1, 199), r("mk3"), r("p5", 256, 454), 0.0, OP.mult, OP.add)
        v("tt", r("ve"), r("p1", 0, 208), r("sc"), OP.max)
        for q in range(16):
            pe(r("p6", 128, 141), sel(q), r("ve", q, 208, 16), q == 0, q == 15)
        ts(r("mo", 0, 13), r("p6", 128, 141), 1.0 / 16, OP.mult, 2048.0, OP.add)
        v("copy", ind(r(iw), r("mo", 0, 13)), r("sv"))
        for j in early if t == 0 else ():
            behind(j)
        for b, lo, n in ((0, 0, 256), (IZ, 256, 256), (ID, 512, 128)):
            v("scan", r("fs", lo, lo + n), r("inc", 0, n), r(iw, b, b + n), 1.0, OP.add, OP.min)
            if t < 2:
                iota(r(iw, b, b + n), [[0, n]], 1, 0)
        ts(r("bt", 0, 256), r("fs", 0, 256), kx(7), OP.mult, 0.0, OP.max)
        act(r("bt", 256, 640), r("fs", 256, 640), AF.Relu, scale=kx(7))
        for q in range(16):
            pe(r("p6", 160, 200), sel(q), r("bt", q, 640, 16), q == 0, q == 15)
        ts(r("sl"), r("p6", 160, 192), 0.0, OP.add)
        listed = len(ops) - 1
        act(r("dp"), r("p6", 192, 200))
        product("p3", 0, "m3", "nm3", False)
        pe(r("p3", 0, 198), r("nid1"), r("sc", 0, 198), False, True)
        for c in range(3):
            act(r("th2", 66 * c, 66 * c + 66), r("p3", 66 * c, 66 * c + 66), AF.Identity, bias=(-2048 - 4.5 / 32, IZ - 2048 - 4.5 / 32, ID - 2048.0)[c])
        act(r("i0"), r("th2", 0, 132), AF.Relu)
        act(r("il"), r("i0"), AF.Sign)
        for c in range(2):
            act(r("ev", 66 * c, 66 * c + 66), r("sc", 66 * c + 1, 66 * c + 67), AF.Relu, scale=-1.0, bias=256.0 + IZ * c - 2048)
        pe(r("p5", 0, 9), r("id"), r("ec"), True, False)
        behind(listed)
        for q in range(16):
            pe(r("p5", 0, 9), sel(q, 1), r("ev", q, 144, 16), False, q == 15)
        ts(r("eo", 0, 9), r("p5", 0, 9), 1.0 / 16, OP.mult, 255.0, OP.add)

    made = []

    def consts():
        v("set", r("one"), 1.0)
        v("set", r("neg"), -1.0)
        v("set", r("onf"), -1.0 / 16)
        act(r("bb9"), r("bb"), AF.Copy, scale=-9.0)
        act(r("id8"), r("id"), AF.Copy, scale=-8.0)
        act(r("id16"), r("id"), AF.Copy, scale=16.0)
        act(r("bq"), r("bb"), AF.Copy, scale=1.0 / 32)
        act(r("nbq"), r("bb"), AF.Copy, scale=-1.0 / 32)
        iota(r("junk", 0, 64), [[1, 64]], 0, 0)
        ts(r("al"), r("junk", 0, 64), 16.0, OP.mult, qc, OP.add)
        act(r("ct", 0, 1024), ind(r("ci", 0, 1024), r("al")))
        act(r("nidf"), r("id"), AF.Copy, scale=-1.0)
        act(r("idk"), r("id"), AF.Copy, scale=-160.0)
        act(r("ih", 0, 128), r("id"))
        act(r("ih", 128, 256), r("id"), AF.Copy, scale=-64.0)
        act(r("mkb"), r("mk", 0, 384), AF.Copy, scale=float(1 << 18))
        for c in range(3):
            ts(r("g2", 8 * c, 8 * c + 8), r("g8"), gc, OP.is_equal, -8192.0, OP.mult)
        zero = r("zr")
        for c in range(2):
            do("g", "asel", r("cy", 1024 * c, 1024 * c + 1024), zero, [[1, 8], [-16, 8], [0, 16]], OP.not_equal, 1.0, 8 * c - 15, 1)
            made.append(len(ops) - 1)
        do("g", "asel", r("ea", 1024, 2048), zero, [[-16, 8], [0, 8], [-1, 16]], OP.not_equal, 1.0, 0, 1)
        made.append(len(ops) - 1)
        ts(r("ea", 0, 1024), r("ea", 1024, 2048), 64.0, OP.mult)
        iota(r("ax"), [[0, 1072]], 1, 0)
        ts(kx(0), qc, -512.0, OP.mult, 7680.0 - 128, OP.add)
        ts(kx(1), qc, -512.0, OP.mult, 7680.0 + 8192, OP.add)
        ts(r("un"), r("im", 0, 16), qc, OP.is_gt)
        ts(kx(5), qc, -512.0, OP.mult, 7680.0, OP.add)
        for c in range(3):
            act(r("dg", 128 * c, 128 * c + 128), r("id"), AF.Identity, scale=kx((0, 1, 5)[c]))
        for c, (step, thr, op) in enumerate(TESTS):
            act(r("tp", 198 * c, 198 * c + 198), r("mk3"), AF.Identity, scale=0.0, bias=thr)
            for t in range(1, 4):
                o, far, below = 198 * c + 66 * (t - 1), 32768.0 if c else -32768.0, r("un", step * t % 16, step * t % 16 + 1)
                act(r("tp", o + 1, o + 2), below, AF.Identity, scale=far, bias=thr)
                act(r("tp", o + 65, o + 66), below, AF.Identity, scale=-far, bias=thr + far)
        ts(r("trs"), r("t32"), qc, OP.add, 1.0 / 16384, OP.mult)
        ts(r("px", 0, 268), r("i66", 0, 268), qc, OP.is_equal, float(1 << 20), OP.mult)
        for s in range(2):
            v("copy", r("px", 65 + s, 268, 67), r("trs", 16 * s, 16 * s + 4))
        for c in range(1, 4):
            dma("y", r("px", 268 * c, 268 * c + 268), r("px", 0, 268))
        ts(r("rp0"), r("g8r"), gc, OP.subtract)
        ts(r("ramp"), r("rp0"), 32768.0, OP.mult, -18432.0, OP.add)
        ts(r("pat"), r("g8r"), gc, OP.is_le, float(1 << 20), OP.mult)
        ts(r("jn"), r("jc8"), 1.0 / 16, OP.mult, -383.0, OP.add)
        v("copy", r("thf"), r("thi"))
        v("copy", r("thr"), r("thi"))
        act(r("nthr"), r("thf"), AF.Identity, scale=-1.0, bias=1.0)

    ts(kx(4), qc, 16.0, OP.mult)
    ts(r("jc8"), r("jc0"), kx(4), OP.add)
    ts(r("trd"), r("jc8"), 1.0 / 16, OP.mult, CE - 128.0, OP.add)
    v("set", r("zr"), 0.0)
    early.append(len(ops) - 1)
    ts(r("frb", P=64), r("fr0", P=64), 16.0, OP.mult)
    pe(r("p6", 0, 64), r("frb", P=64), r("id", 0, 64, P=64), True, True)
    v("set", r("xt", XE - 16, XE), 63.0)
    v("set", r("xt", 0, XW0), 0.0)
    XG = r("xt", XW0, XE)
    for i in range(4):
        o, x = r("xt", XW0 + 4096 + 1024 * i, XW0 + 5120 + 1024 * i), r("xt", XW0 + 1024 * i, XW0 + 1024 + 1024 * i)
        if i == 0:
            ts(o, x, -1.0, OP.mult, 63.0, OP.add)
            early.append(len(ops) - 1)
        else:
            act(o, x, AF.Identity, scale=-1.0, bias=63.0)
    lists(0)
    consts()

    al = slice(None)
    for t in range(4):
        last = t == 3
        marks.append(len(ops))
        CG = r("ct" if t else "ci", 0, CE)
        for lo, hi in ((0, 64), (64, 256)):
            v("copy", r("lua", lo, hi), ind(CG, r("sl", lo // 16, hi // 16)))
        if t:
            act(r("lf"), ind(CG, r("sl", 0, 16)))
        else:
            v("copy", r("lf"), r("lua"))
        for e, lo, hi in ACTIVE:
            do(e, "act" if e == "s" else "copy", r("sa", 16 * lo, 16 * hi), ind(XG, r("lua", lo, hi)), *([AF.Copy] if e == "s" else []))
        v("copy", r("luz"), ind(CG, r("sl", 16, 32)))
        for e, lo, hi in FROZEN:
            if e == "s":
                act(r("sz", 16 * lo, 16 * hi), ind(XG, r("luz", lo, hi)), AF.Relu, bias=r("nthr"))
            else:
                ts(r("sz", 16 * lo, 16 * hi), ind(XG, r("luz", lo, hi)), r("thr"), OP.is_ge)
        if t:
            act(r("hib"), r("lf"), AF.Identity, scale=1.0 / 64, bias=128.0)
        else:
            ts(r("hib"), r("lua"), 1.0 / 64, OP.mult, 128.0, OP.add)
        pe(r("p3", 256, 384), r("idf"), r("lf", 1, 256, 2), True, False)
        pe(r("p3", 256, 384), r("nidf"), r("lf", 0, 256, 2), False, True)

        for h, bk in enumerate(("p0", "p2")):
            lo, hi = 128 * h, 128 * h + 128
            pe(r(bk, 0, 384), r("one"), r("dg"), True, False)
            pe(r(bk, 0, 256), r("hib", lo, hi), r("ih"), False, False)
            pe(r(bk, 128, 256), r("lf", lo, hi), r("idf"), False, False)
            for a in (lo, lo + 64):
                v("scan", r("mx", 16 * a, 16 * a + 1024), r("mk"), r("sa", 16 * a, 16 * a + 1024), 0.0, OP.min, OP.max)
            o = r("p3", lo // 2, hi // 2)
            for k in range(16):
                pe(o, sel(k), r("sa", 16 * lo + 16 + k, 16 * hi, 32), k == 0, False)
                pe(o, sel(k, 1), r("sa", 16 * lo + k, 16 * hi, 32), False, k == 15)
        ts(r("fa"), r("mx", 15, 4096, 16), r("thr"), OP.is_lt, -1.0, OP.mult)
        pe(r("p7", 256, 512), r("bb9"), r("fa"), True, True)
        pe(r("p1", 0, 256), r("id"), r("rr"), True, False)
        pe(r("p1", 0, 256), r("bq"), r("fa"), False, True)
        v("scan", r("st", 0, 256), r("fs", 0, 256), r("p1", 0, 256), 0.0, OP.mult, OP.max)
        for k in range(16):
            v("scan", r("sm", 256 * k, 256 * k + 256), r("sa", k, 4096, 16), r("fa"), 0.0, OP.max, OP.mult)
            for h, bk in enumerate(("p0", "p2")):
                if k == 15:
                    pe(r(bk, 0, 128), r("vn", 128 * h, 128 * h + 128), r("idv"), False, False)
                pe(r(bk, k, 384, 16), r("sm", 256 * k + 128 * h, 256 * k + 128 * h + 128), r("g2"), False, k == 15)
            if k == 1:
                ts(r("vn"), r("p7", 256, 512), 40.0, OP.is_gt, -1.0, OP.mult)
        for h, bk in enumerate(("p0", "p2")):
            v("scan", r3("scn", h, al, 384 * h, 384 * h + 384, 384), r("mkb"), r(bk, 0, 384), 0.0, OP.min, OP.max)
        for c in range(2):
            v("tt", r3("df", slice(2 * c, 2 * c + 2), al, 16 * c, 16 * c + 16, 16), r3("scn", al, slice(128 * c + 15, 128 * c + 128, 16), 0, 768, 16),
              r3("scn", al, slice(271, 384, 16), 0, 768, 16), OP.subtract)
        pe(r3("p4", slice(0, 2), al, 0, 128, 128), r("id"), r("ramp"), True, False)
        for c in range(2):
            for a in range(8):
                pe(r3("p4", slice(0, 2), slice(8 * (a ^ 3), 8 * (a ^ 3) + 8), 0, 128, 16), r("ea", 1024 * c + 128 * a, 1024 * c + 128 * a + 128),
                   r3("df", slice(2 * c, 2 * c + 2), al, 16 * c, 16 * c + 16, 16), False, c == 1 and a == 7)
        for h in range(2):
            v("scan", r("hs", 64 * h, 64 * h + 64), r("pat", 0, 64), r3("p4", h, al, 64 * h, 64 * h + 64, 64), 0.0, OP.add, OP.min)
        ch = r("hs", 7, 128, 8)
        ts(r("g1"), ch, 2048.0, OP.is_ge, -4096.0, OP.mult)
        v("tt", r("key"), ch, r("g1"), OP.add)
        ts(r("cu"), ch, 2048.0, OP.add)
        act(r("k32"), r("key"))
        v("tt", r("cm"), r("key"), r("g1"), OP.add)
        act(r("x0", 0, 16), ch, AF.Abs, scale=1.0 / 16384, bias=(2048.0 + XW0) / 16384)
        act(r("x0", 16, 32), r("cm"), AF.Abs, scale=1.0 / 16384, bias=(6144.0 + XW0) / 16384)
        act(r("ax", 64, None, 67), ch, AF.Relu, bias=4096.0)
        act(r("sch"), ind(XG, r("cu")))
        for a in range(16):
            pe(r("p0", 256 + 16 * a, 272 + 16 * a), r("id8"), r("fa", 16 * (a ^ 3), 16 * (a ^ 3) + 16), a == 0, False)
        pe(r("p0", 256, 512), r("id"), r("sch"), False, True)
        nv1, nv2 = r3("nv", al, slice(0, 64), 0, 512, 256), r3("nv", al, slice(64, 128), 0, 512, 256)
        act(nv2, r("p0", 256, 512), AF.Relu, bias=63.0, scale=-1.0)
        act(nv1, nv2, AF.Identity, bias=63.0, scale=-1.0)
        for d in range(16):
            pe(r("p2", 256 + d, 512, 16), r("cy", 128 * d, 128 * d + 128), r("key"), True, True)
        for c0, c1 in ((2, 4), (0, 2)) if t in HALVES else ((0, 4),):
            for a in range(4 * c0, 4 * c1):
                act(r("ax", 67 * a, 67 * a + 64 - a % 4 * 16), r("p2", 256 + 16 * a, 320 + a // 4 * 64), AF.Abs, scale=-1.0, bias=r("k32", a, a + 1))
            lo, hi, n = 268 * c0, 268 * c1, 4 * (c1 - c0)
            v("scan", r("rx", lo, hi), r("px", lo, hi), r("ax", lo, hi), 0.0, OP.max, OP.min)
            for s in range(2):
                o = 8 * c0 + n * s
                v("tt", r3("xa", slice(c0, c1), slice(4 * s, 4 * s + 4), o, o + n, n), r("x0", 16 * s + 4 * c0, 16 * s + 4 * c1), r("rx", lo + 65 + s, hi, 67), OP.min)
            ts(r("off", 8 * c0, 8 * c1), r3("xa", slice(c0, c1), al, 8 * c0, 8 * c1, 2 * n), 16384.0, OP.mult)
            for c in range(c1 - 1, c0 - 1, -1):
                v("copy", ind(r("xt"), r("off", 8 * c, 8 * c + 8)), r3("nv", c, al, 0, 512, 128))
        if last:
            for i in range(2):
                dma("y", T.yx[:, 2048 * i:2048 * i + 2048], r("xt", XW0 + 2048 * i, XW0 + 2048 * i + 2048))

        ts(r("jm"), r("p3", 0, 128), 0.0, OP.is_gt)
        v("tt", r("je"), r("p3", 256, 384), r("jm"), OP.mult)
        v("scan", r("jb"), r("vn", 0, 256, 2), r("vn", 1, 256, 2), 0.0, OP.min, OP.mult)
        jt = r("jt", 128 * t, 128 * t + 128)
        v("scan", jt, r("jb"), r("neg"), -128.0, OP.add, OP.add)
        send(r("cn", 8 * t, 8 * t + 8), r("jt", 128 * t + 120, 128 * t + 128), "c%d" % t, t, RW1)
        for j in made if t == 0 else ():
            behind(j)
        v("scan", r("ju"), r("jb"), jt, 0.0, OP.max, OP.mult)
        pe(r("p6", 0, 8), r("id"), r("jc8"), True, False)
        for q in range(16):
            pe(r("p6", 0, 8), sel(q), r("ju", q, 128, 16), False, q == 15)
        ts(r("jo"), r("p6", 0, 8), 1.0 / 16, OP.mult)
        v("tt", ind(r("jw", 256 * t, 256 * t + 256), r("jo")), r("je"), r("lf", 0, 256, 2), OP.add)
        sent = len(ops) - 1
        send(r("jl", 128 * t, 128 * t + 128), r("jw", 256 * t, 256 * t + 128), "a%d" % t, t, RW2)

        for e, lo, hi in FROZEN:
            if lo < FT:
                for k in range(16):
                    pe(r("p7", lo, hi), r("id"), r("sz", 16 * lo + k, 16 * hi, 16), k == 0, k == 15)
            else:
                v("scan", r("mx", 16 * lo, 16 * hi), r("mk", 0, 16 * (hi - lo)), r("sz", 16 * lo, 16 * hi), 0.0, OP.min, OP.max)
        if FT:
            act(r("fz", 0, FT), r("p7", 0, FT), AF.Relu, bias=1.0, scale=-1.0)
        if FT < 256:
            ts(r("fz", FT, 256), r("mx", 16 * FT + 15, 4096, 16), 0.5, OP.is_lt)
        pe(r("p1", 256, 512), r("id"), r("rr"), True, False)
        pe(r("p1", 256, 512), r("nbq"), r("fz"), False, True)
        v("scan", r("st", 256, 512), r("fs", 256, 512), r("p1", 256, 512), 0.0, OP.mult, OP.max)
        v("tt", r("kl"), ind(r("st"), r("eo", 0, 9)), r("th2", 0, 144), OP.is_lt)
        if not last:
            act(r("junk"), r("vn"), AF.Copy, accum_out=r("vs"))

        jl = r("jl", 128 * t, 128 * t + 128)
        cn = r("cn", 8 * t + 7, 8 * t + 8)
        act(r("c4"), cn, AF.Copy, scale=-4096.0)
        behind(sent)
        act(r("tk"), r("th2", 133, 197), AF.Relu, bias=cn)
        behind(sent)
        act(r("du"), r("jn"), AF.Relu, scale=4096.0, bias=r("c4"))
        pe(r("p5", 16, 24), r("idf"), r("dp"), True, False)
        pe(r("p5", 16, 24), r("idf"), r("du"), False, True)
        v("tt", r("dy"), r("p5", 16, 24), r("trd"), OP.min)
        v("copy", r("do"), r("dy"))
        v("copy", ind(r("ct"), r("do")), jl)
        if last:
            dma("s", T.yc[:, 0:512], r("ct", 0, 512))
            dma("y", T.yc[:, 512:1024], r("ct", 512, 1024))
        else:
            n = 341 * (t + 1) // 16 * 16 + 16
            act(r("ct", 1024, 1024 + n), r("ct", 0, n))

        parts = [("id", "fn", 0, 64, 0), ("idk", "tk", 0, 64, 0)]
        for m, x in (("id16", "il"), ("idk", "kl")):
            for seg, step in ((1, 170), (67, 341)):
                c0 = step * t % 1024 // 16
                parts += [(m, x, c0, 64, seg), (m, x, 0, c0 + 1, seg + 64 - c0)] if t else [(m, x, 0, 64, seg)]
        for i, (m, x, lo, hi, at) in enumerate(parts):
            pe(r("p6", lo, hi), r(m), r(x, at, at + hi - lo), i == 0, i == len(parts) - 1)
        if not last:
            pe(r("p3", 400, 401), r("onf"), r("vs"), True, True)
            aw = [r("aw", i, i + 1) for i in range(4)]
            act(aw[0], r("p3", 400, 401), AF.Identity, scale=0.25, bias=-0.375)
            act(aw[1], r("p3", 400, 401), AF.Identity, bias=r("thf"))
            act(aw[2], aw[0], AF.Identity, bias=12582912.0)
            act(aw[3], aw[2], AF.Identity, scale=-4.0, bias=4 * 12582912.0)
            act(r("thr"), aw[3], AF.Identity, bias=aw[1])
            act(r("nthr"), r("thr"), AF.Identity, scale=-1.0, bias=1.0)
            lists(t + 1)
    ts(r("fn"), r("p6", 0, 64), 0.0, OP.max)
    pe(r("p5", 0, 128, P=64), r("fn"), r("id"), True, True)
    ts(r("fo", P=64), r("p5", 0, 128, P=64), 1.0 / 16, OP.mult)
    for gr in range(8):
        dma("y" if gr % 2 == 0 else "s", T.yf[gr:gr + 1, :], r("fo", 16 * gr, 16 * gr + 16, P=64))
    order()
    for q in "vstg":
        need("g", "e" + q, cnt[q])
    for i in range(nd[0]):
        need("g", "d%d" % i, 16)
    for t in range(4):
        d = T.cores[(rank + 1 + t % 3) % len(T.cores)]
        need("g", "l%d" % t, 2 * len(topo.engines(core, d)))
